import numpy as np, ml_dtypes
CORES = [35,38,43,46]
N = 4
import mx_ref
BF = ml_dtypes.bfloat16
def gcols(t, e):
    v = np.concatenate([t.reshape(8, 16, -1, 4), np.zeros((8, 16, 1, 4), BF)], axis=2)
    return np.ascontiguousarray(np.stack([v[g][:, e[g]] for g in range(8)])).reshape(128, -1)
def tile(rs):
    return np.stack(rs, axis=2).reshape(128, -1).astype(BF)
def pick(q, e):
    c = np.concatenate([q[0].reshape(128, -1, 4), np.zeros((128, 1, 4), np.uint8)], axis=1); s = np.concatenate([q[1], np.ones((16, 1), np.uint8)], axis=1)
    return (np.ascontiguousarray(c[:, e].reshape(128, -1)), np.ascontiguousarray(s[:, e]))
def join(*qs):
    return (np.concatenate([q[0] for q in qs], axis=1), np.concatenate([q[1] for q in qs], axis=1))
def put(q, e, v):
    c, s = q[0].reshape(128, -1, 4).copy(), q[1].copy(); c[:, e] = v[0].reshape(128, -1, 4); s[:, e] = v[1]
    return (c.reshape(128, -1), s)
def pk(c, s):
    return (np.ascontiguousarray(c), mx_ref.live(s))
def emit(q):
    return q[0], q[1]
def packed(v, rng):
    q = [mx_ref.quantize(np.ascontiguousarray(v[r])) for r in range(N)]
    return np.stack([a for a, b in q]), np.stack([mx_ref.plane(b, rng) for a, b in q])
def values_of_codes():
    e, c = np.zeros((128, 128, 4), np.float32), np.zeros((128, 2, 4), np.uint8)
    e[np.arange(128), np.arange(128), 0] = 1
    c[:127, :, 0] = np.arange(256).reshape(2, 128).T[:127]
    return mx_ref.matmul(mx_ref.quantize(e.reshape(128, 512).astype(BF)), (c.reshape(128, 8), np.full((16, 2), 127, np.uint8))).T.reshape(-1).astype(np.float64)
CODE_VALUE, SCALE_VALUE = values_of_codes(), 2.0 ** (np.arange(256) - 127.0)
def decode(q):
    return (CODE_VALUE[q[0]].reshape(16, 8, -1, 4) * SCALE_VALUE[q[1]][:, None, :, None] + 0.0).reshape(128, -1).astype(np.float32)
def f(rng, *shape):
    return mx_ref.flush((rng.standard_normal(shape, dtype=np.float32) * np.exp2(rng.integers(-2, 3, shape[:-1] + (1,)))).astype(BF))
def wide(rng, *shape, cols=0):
    v = rng.standard_normal(shape, dtype=np.float32) * np.exp2(rng.integers(-12, 13, shape)).astype(np.float32)
    if cols: v *= np.repeat(np.exp2(rng.integers(-cols, cols + 1, shape[:-2] + (1, shape[-1] // 4))) * (rng.random(shape[:-2] + (1, shape[-1] // 4)) > 0.0625), 4, axis=-1).astype(np.float32)
    return mx_ref.flush(v.astype(BF))
C, R = 336, 2
def alike(w):
    return np.stack([w] * N)
def layers(rng):
    return f(rng, N, 128, 4096)
def weights(rng, w, still=()):
    w = np.array(w).reshape(N, 8, 16, 8, 8, 16, 4)
    for i in still:
        w[:, :, i] = 0
        w[:, :, :, :, :, i] = 0
    c, p = packed(w.reshape(N, 128, 4096), rng)
    return {"wc": c, "ws": p}
def numbers_of(rng):
    return {"x": np.array(f(rng, N, 128, 4 * C)), "u": alike(f(rng, 128, 512)), "v": np.array(f(rng, N, 128, 512))}
def unscored(rng):
    a = np.array(f(rng, 128, 512)).reshape(128, 128, 4)
    a[:, ::16] = 0
    a[:, 1::16] = 0
    return a
def setup_inputs(rng):
    return {**numbers_of(rng), **weights(rng, layers(rng))}
def setup_inputs_ties(rng):
    d = numbers_of(rng)
    o = rng.permutation(N)
    k = rng.integers(0, 3, (N, 8, C))
    m = np.where((o % 2 == 0)[:, None, None], k, rng.integers(-2, 3, (N, 8, C)))
    k[o == 0] = 0
    m[o == 0] = 0
    k[o == 1] *= -1
    x = d["x"].reshape(N, 8, 16, C, 4)
    x[:, :, 0] = 0
    x[:, :, 0, :, 0] = k.astype(np.float32).astype(BF)
    x[:, :, 0, :, 1] = m.astype(np.float32).astype(BF)
    a = unscored(rng)
    for h in range(0, 128, 16):
        a[h, h, 0] = 1
        a[h, h + 1, 1] = 1
    return {"x": x.reshape(N, 128, 4 * C), "u": alike(a.reshape(128, 512)), "v": d["v"], **weights(rng, layers(rng), [0])}
def setup_inputs_near(rng):
    d = numbers_of(rng)
    x = d["x"].astype(np.float32).reshape(N, 8, 16, C, 4)
    x[:, :, 0] = 0
    x[:, :, 8:] = 0
    a = unscored(rng)
    o = rng.permutation(8) % 4
    for g in range(8):
        h = 16 * g
        for m in range(2):
            s = rng.integers(0, 16, (N, C))
            c = rng.integers(0, 2, (N, C)) * 2.0 - 1.0
            if o[g] < 3: x[:, g, 8 + m] = ((s[:, :, None] >> np.arange(4)) & 1) * np.exp2(np.arange(4) - 23.0)
            if o[g] < 2:
                k = 1.0 if o[g] == 0 else 2.0 ** -30
                x[:, g, 0, :, m] = c
                x[:, g, 11, :, 0] = 2.0 ** -10
                a[h, h + m, m] = k
                a[h + 8 + m, h + m] = k
                a[h + 11, h + m, 0] = k
            elif o[g] == 2:
                for r in range(N): x[r, g, 0, rng.permutation(C)[:2], m] = [1.0, -1.0]
                a[h, h + m, m] = 2.0 ** 30
                a[h + 8 + m, h + m] = 2.0 ** -30
            else:
                x[:, g, 10, :, m] = np.where(s % 2 == 0, 1.125 * 2.0 ** -30 * c, 0.0)
                x[:, g, 12, :, m] = np.where(s % 2 == 0, 0.0, 1.25 * 2.0 ** -30 * c)
                a[h + 10, h + m, m] = 1.125 * 2.0 ** -30
                a[h + 12, h + m, m] = 2.0 ** -30
    return {"x": x.reshape(N, 128, 4 * C).astype(BF), "u": alike(a.reshape(128, 512)), "v": d["v"], **weights(rng, layers(rng), [0, 8, 9, 10, 11, 12, 13, 14, 15])}
def setup_inputs_odd(rng):
    d = numbers_of(rng)
    a = (1.0 + (2 * rng.integers(0, 64, (N, 16, 8, C, 4)) + 1) * 2.0 ** -7) * np.exp2(-rng.integers(8, 15, (N, 16, 8, C, 4)).astype(np.float64))
    a = np.where(np.arange(8)[:, None, None] * 4 + np.arange(4) == rng.integers(0, 32, (N, 16, 1, C, 1)), 1.96875, a)
    a = a * (rng.integers(0, 2, a.shape) * 2.0 - 1.0) * np.exp2(rng.integers(-2, 3, (N, 16, 1, C, 1)).astype(np.float64))
    return {"x": a.astype(np.float32).reshape(N, 128, 4 * C).astype(BF), "u": d["u"], "v": d["v"], **weights(rng, layers(rng), [8, 9, 10, 11, 12, 13, 14, 15])}
def setup_inputs_ends(rng):
    d = numbers_of(rng)
    o = rng.permutation(N) % 4
    x = np.zeros((N, 8, 16, C, 4), np.float32)
    x[:, :, 8:12] = f(rng, N, 8, 4, C, 4).astype(np.float32) * np.float32(1024)
    for r in range(N):
        c = rng.integers(0, 2, C) * 2.0 - 1.0
        w = rng.choice([1.375, 1.5], (8, C))
        a, b = rng.permutation(C)[:2]
        w[:, b] = 1.625
        if o[r] == 0:
            w[:, a] = 1.625
            c[a], c[b] = 1.0, -1.0
        else: w[:, a] = 1.25
        if o[r] == 1: c[:] = -1.0
        if o[r] == 2: c[:] = 1.0
        e = w * c * 2.0 ** 29 if o[r] < 2 else np.ones((8, 1)) * c * 2.0 ** -30
        x[r, :, :8] = e[:, None, :, None]
        k = (rng.integers(0, 2, (128, 512)) * 2.0 - 1.0).astype(np.float32)
        if o[r] == 1: d["v"][r] = (k * np.float32(2.0 ** 30)).astype(BF)
        if o[r] == 2: d["v"][r] = (k * np.float32(2.0 ** -30)).astype(BF)
    u = unscored(rng).reshape(8, 16, 128, 4)
    p = rng.permutation(8)
    for g in range(8):
        k = (2.0 ** 30 if p[g] < 4 else 2.0 ** -29) * (1.0 if p[g] % 2 == 0 else -1.0)
        for m in range(2):
            u[:, :8, 16 * g + m] = 0.75 * k * (1 - 2 * m)
            u[g, :8, 16 * g + m] = k * (1 - 2 * m)
    w = ((rng.integers(0, 2, (N, 128, 4096)) * 2.0 - 1.0) * 2.0 ** -11).astype(np.float32).astype(BF)
    return {"x": x.reshape(N, 128, 4 * C).astype(BF), "u": alike(u.reshape(128, 512)), "v": d["v"], **weights(rng, w, [0, 1, 2, 3, 4, 5, 6, 7])}
def setup_inputs_spread(rng):
    d = numbers_of(rng)
    w = np.array(mx_ref.flush((layers(rng).astype(np.float32) * np.float32(2.0 ** -7)).astype(BF)))
    x = np.array(wide(rng, N, 128, 4 * C, cols=3))
    e = int(rng.integers(N))
    x[e] = ((1.0 + 0.25 * rng.random((128, 4 * C))) * 2.0 ** 24).astype(np.float32).astype(BF)
    w[e ^ 1] = (-0.1875 - 0.0625 * rng.random((128, 4096))).astype(np.float32).astype(BF)
    return {"x": x, "u": d["u"], "v": d["v"], **weights(rng, w)}
def check_inputs(d):
    b = []
    for k in ("x", "u", "v"):
        a = np.abs(d[k].astype(np.float32))
        if not (np.isfinite(a).all() and ((a == 0) | (a >= 2.0 ** -30) & (a <= 2.0 ** 30)).all()): b.append("a value of " + k)
    if (d["u"] != d["u"][:1]).any(): b.append("u isn't the same on all ranks")
    none, least, most = [emit(mx_ref.quantize(np.full((128, 16), k, np.float32).astype(BF)))[1][0, 0] for k in (0.0, 2.0 ** -30, 2.0 ** 30)]
    size = 0.0
    for r in range(N):
        if ((d["wc"][r] == 0x7F) | (d["wc"][r] == 0xFF)).any(): b.append("wc: a code that is no number")
        s = mx_ref.live(d["ws"][r])
        if ((s != none) & ((s < least) | (s > most))).any(): b.append("ws: a scale out of range")
        if (((d["wc"][r].reshape(16, 8, -1, 4) & 0x7F) != 0) & (s == none)[:, None, :, None]).any(): b.append("wc: a code other than zero where the scale is that of zeros")
        size = max(size, float(np.abs(decode(pk(d["wc"][r], d["ws"][r]))).max()))
    if not float(np.abs(d["x"].astype(np.float32)).max()) * (1.0 + 20.0 * size) * (1.0 + 20.0 * size) <= 900000000.0: b.append("the sizes of x and W together")
    return b
def places(s):
    o = np.argsort(-s, axis=1, kind="stable")
    i = np.zeros(s.shape, np.int64)
    np.put_along_axis(i, o, np.broadcast_to(np.arange(C), s.shape), axis=1)
    return o, i
def reference(x, u, v, wc, ws):
    qu = [mx_ref.quantize(u[r]) for r in range(N)]
    lay = [pk(wc[r], ws[r]) for r in range(N)]
    now = [x[r] for r in range(N)]
    total = np.zeros((N, C), np.int64)
    for t in range(R):
        q = [mx_ref.quantize(now[r]) for r in range(N)]
        full = [decode(q[r]).astype(BF) for r in range(N)]
        s = [mx_ref.matmul(qu[r], q[r]) + np.float32(0.0) for r in range(N)]
        first = [places(s[r][::16]) for r in range(N)]
        second = [places(s[r][1::16])[1] for r in range(N)]
        made = [None] * N
        for r in range(N):
            e = r ^ (1 << t)
            total[r] = first[r][1][0]
            took = np.zeros((8, C), np.int64)
            for g in range(8):
                turn = places(total[r][None])[1][0]
                took[g] = first[e][0][g][turn]
                total[r] = total[r] + second[e][g][took[g]]
            z = mx_ref.quantize(gcols(full[e], took))
            p = [mx_ref.matmul(pick(lay[r], np.arange(128 * b, 128 * b + 128)), z) for b in range(8)]
            y = tile([np.maximum(p[b], p[b + 4]) * np.float32(0.03125) for b in range(4)])
            back = gcols(decode(mx_ref.quantize(y)).astype(BF), np.argsort(took, axis=1))
            made[e] = (full[e].astype(np.float32) + back.astype(np.float32)).astype(BF)
        now = made
    y, tot = np.zeros((N, 128, C), np.float32), np.zeros((N, 1, C), np.float32)
    oc, osc = np.zeros((N, 128, 4 * C), np.uint8), np.zeros((N, 16, C), np.uint8)
    for r in range(N):
        q = mx_ref.quantize(now[r])
        y[r] = mx_ref.matmul(mx_ref.quantize(v[r]), q)
        tot[r, 0] = total[r]
        oc[r], osc[r] = emit(q)
    return {"y": y, "tot": tot, "oc": oc, "osc": osc}

@@ -1,0 +1,516 @@
+from concourse.mybir import dt, AluOpType, ActivationFunctionType
+
+AL, AF = AluOpType, ActivationFunctionType
+C, R = 336, 2
+HV = [(0, 160), (160, 336)]
+LV = [(0, 10), (10, 21)]
+INF = float(2 ** 90)
+TINY = float(2.0 ** -120)
+BIG = float(2 ** 21)
+MAGIC = 1.5 * 2.0 ** 28
+OFF = 47
+
+SCRATCH = {}
+
+
+def _s(name, n, d="float32", where="sbuf"):
+    SCRATCH[name] = (where, [128, n], d)
+
+
+def _q(name, n):
+    _s(name + "q", n, "float8_e4m3fn_x4")
+    _s(name + "s", n, "uint8")
+
+
+CONST = ["EU0", "EU1", "EU2", "EU3", "EG", "EA", "ED"] + ["EP%d" % _k for _k in range(8)]
+for _n in ("xin", "xt0", "xt1", "Z", "Yp", "Ca", "Cb", "C5", "PT", "F", "G", "Y"):
+    _s(_n, 4 * C, "bfloat16")
+for _n in ("uin", "vin", "ones", "W2", "W3", "W4"):
+    _s(_n, 512, "bfloat16")
+_s("Eb", 512 * len(CONST), "bfloat16")
+_q("E", 128 * len(CONST))
+for _n in ("yt", "ym"):
+    _s(_n, 4 * 176)
+_s("P", 8 * C)
+_s("Lg", 8 * 22, "uint16")
+for _k in range(8):
+    _s("pb%d" % _k, 512, "float32", "psum")
+for _n, _k in (("u", 128), ("v", 128), ("uu", 256), ("wl", 1024), ("ca", C), ("cb", C), ("z", C), ("pp", C)):
+    _q(_n, _k)
+for _h in range(2):
+    _s("CD%d" % _h, 4 * (HV[_h][1] - HV[_h][0]), "bfloat16")
+    _q("cd%d" % _h, HV[_h][1] - HV[_h][0])
+    _s("V%d" % _h, C)
+    _s("df%d" % _h, C)
+for _t in range(R):
+    _q("rx%d" % _t, C)
+    _q("ry%d" % _t, C)
+    _q("y%d" % _t, C)
+    _s("ls%d" % _t, 44, "uint16")
+    _s("ll%d" % _t, 44, "uint16")
+    _s("NL%d" % _t, 22, "uint16")
+for _t in range(R + 1):
+    _q("x%d" % _t, C)
+for _n in ("jp", "ji", "d", "dn", "de", "k1", "k2", "k3", "JR", "MN", "MNd", "MH", "RH", "t1", "Hd", "sa", "oW", "iW",
+           "tm", "tb", "va", "SD", "ysb", "sc"):
+    _s(_n, C)
+_s("hi", C, "bfloat16")
+_s("lo", C, "bfloat16")
+_s("MD", 112)
+_s("x6", 22)
+_s("x7", 22)
+_s("pI", 4, "int32")
+_s("oI", 16, "int32")
+_s("oU", 16, "uint16")
+_s("ML", 22, "uint16")
+_s("bc", 32)
+
+SEMAPHORES = ["ve", "ac", "pe", "gp", "lx", "lu", "lv", "lw", "lz", "out", "loc"]
+SEMAPHORES += ["%s%d" % (a, t) for a in ("xa", "la", "nl", "ya", "yb") for t in range(R)]
+
+
+def rank_program(g, core, T, topo):
+    r = T.rank_of(core)
+    if r is None:
+        return
+    queue = {"ve": g.vector, "ac": g.scalar, "pe": g.tensor, "gp": g, "sy": g.sync}
+    tick = {"ve": 0, "ac": 0, "pe": 0, "gp": 0}
+    known = {e: {} for e in queue}
+    wr, rd, dcount, arr, sent = {}, {}, {}, {}, [0]
+
+    def deps(e, reads, writes):
+        want = {}
+        for k in reads:
+            for s, v in wr.get(k, {}).items():
+                want[s] = max(v, want.get(s, 0))
+        for k in list(writes) + [k for k in reads if k[:2] == "pb"]:
+            for tab in (wr, rd):
+                for s, v in tab.get(k, {}).items():
+                    if s != e or tab is rd and e != "pe" and k in writes:
+                        want[s] = max(v, want.get(s, 0))
+        for s, v in want.items():
+            if known[e].get(s, 0) < v:
+                queue[e].wait_ge(T.sem[s], v)
+                known[e][s] = v
+
+    def op(e, fn, reads, writes):
+        deps(e, reads, writes)
+        fn(queue[e]).then_inc(T.sem[e], 1)
+        tick[e] += 1
+        for k in reads:
+            rd.setdefault(k, {})[e] = tick[e]
+        for k in writes:
+            wr.setdefault(k, {})[e] = tick[e]
+
+    def dma(e, out, in_, sem, total, reads=(), writes=()):
+        deps(e, reads, writes)
+        queue[e].dma_start(out, in_).then_inc(T.sem[sem], 16)
+        dcount[sem] = dcount.get(sem, 0) + 16
+        for k in writes:
+            wr.setdefault(k, {})[sem] = total
+        for k in reads:
+            rd.setdefault(k, {})[sem] = total
+
+    def tt(out, a, b, o, reads, writes):
+        op("ve", lambda q: q.tensor_tensor(out, a, b, o), reads, writes)
+
+    def ts(out, a, s1, s2, o0, o1, reads, writes):
+        if o1 is None:
+            op("ve", lambda q: q.tensor_scalar(out, a, s1, None, o0), reads, writes)
+        else:
+            op("ve", lambda q: q.tensor_scalar(out, a, s1, s2, o0, o1), reads, writes)
+
+    def cp(out, a, reads, writes):
+        op("ve", lambda q: q.tensor_copy(out, a), reads, writes)
+
+    def fill(ap, c, key):
+        op("ve", lambda q: q.memset(ap, c), [], [key])
+
+    def scan(out, a, b, ini, o0, o1, reads, writes):
+        op("ve", lambda q: q.tensor_tensor_scan(out, a, b, ini, o0, o1), reads, writes)
+
+    def act(out, a, f, reads, writes, **k):
+        op("ac", lambda q: q.activation(out, a, f, **k), reads, writes)
+
+    def at(n):
+        return ("E", 128 * CONST.index(n)) if n in CONST else (n, 0)
+
+    def eb(n, m=1):
+        k = 512 * CONST.index(n)
+        return T.Eb[:, k:k + 512 * m]
+
+    def pl(n, b, a=0, e=C):
+        return T[n][:, C * b + a:C * b + e]
+
+    def quant(name, a, b, src, reads):
+        n, o = at(name)
+        op("ve", lambda q: q.quantize_mx(T[n + "q"][:, o + a:o + b], T[n + "s"][:, o + a:o + b], src),
+           reads, [name + str(a)])
+
+    def mm(bank, n, st, sa, mv, ma, start, stop, reads):
+        w, o = at(st)
+        o += sa
+        op("pe", lambda q: q.matmul_mx(T[bank][:, 0:n], T[w + "q"][:, o:o + 128], T[w + "s"][:, o:o + 128],
+                                       T[mv + "q"][:, ma:ma + n], T[mv + "s"][:, ma:ma + n], start, stop),
+           reads, [bank])
+
+    def send(pc, out, in_, rsem, reads):
+        deps("gp", reads, ())
+        rid, pid, _e = topo.addr(pc)
+        g.remote_dma(out, in_, T.sem[rsem], T.sem.loc, pid, rid, topo.mask(core, pc))
+        sent[0] += len(topo.engines(core, pc))
+
+    def arrives(keys, sem, val):
+        for k in keys:
+            wr.setdefault(k, {})[sem] = val
+        arr[sem] = val
+
+    def part(t):
+        return T.cores[r ^ (1 << t)]
+
+    def ne(t):
+        return len(topo.engines(part(t), core))
+
+    def send_x(t):
+        send(part(t), T["rx%dq" % t][:].bitcast(dt.uint8), T["x%dq" % t][:].bitcast(dt.uint8), "xa%d" % t,
+             ["x%d0" % t, "x%d160" % t])
+        send(part(t), T["rx%ds" % t][:], T["x%ds" % t][:], "xa%d" % t, ["x%d0" % t])
+        arrives(["rx%d" % t], "xa%d" % t, 2 * ne(t))
+
+    dma("sy", T.xin[:], T.x[:], "lx", 16, (), ["xin"])
+    dma("ac", T.uin[:], T.u[:], "lu", 16, (), ["uin"])
+    dma("sy", T.wlq[:].bitcast(dt.uint8), T.wc[:], "lw", 16, (), ["w0"])
+    dma("sy", T.vin[:], T.v[:], "lv", 16, (), ["vin"])
+    dma("sy", T.wls[:], T.ws[:], "lz", 16, (), ["wsc"])
+    f32 = dict(allow_small_or_imprecise_dtypes=True)
+    bc = T.bc
+
+    def iota(ap, pat, base, cm, key, **k):
+        op("gp", lambda q: q.iota(ap, pat, base, cm, **k), [], [key])
+
+    def sel(ap, src, pat, o, fl, base, cm, reads, key):
+        op("gp", lambda q: q.affine_select(ap, src, pat, o, fl, base, cm), reads, [key])
+
+    iota(T.pI[:, 0:1], [[1, 1]], 0, 1, "pI")
+    iota(T.oI[:], [[1, 2], [16, 8]], 0, 0, "oI")
+    iota(T.jp[:], [[0, 21], [1, 16]], 0, 0, "jp", **f32)
+    fill(T.ones[:], 1.0, "ones")
+    fill(T.k3[:], INF, "k3")
+    fill(T.W4[:], 1.0, "W4")
+    ts(T.W4[:, 3::4], T.W4[:, 3::4], 0.5, None, AL.mult, None, ["W4"], ["W4"])
+    ts(T.pI[:, 1:2], T.pI[:, 0:1], 15, None, AL.bitwise_and, None, ["pI"], ["pI1"])
+    ts(T.pI[:, 2:3], T.pI[:, 0:1], 4, None, AL.arith_shift_right, None, ["pI"], ["pI2"])
+    cp(bc[:, 0:1], T.pI[:, 1:2], ["pI1"], ["i"])
+    cp(T.oU[:], T.oI[:], ["oI"], ["oU"])
+    ts(T.d[:], T.jp[:], bc[:, 0:1], None, AL.subtract, None, ["jp", "i"], ["d"])
+    act(T.de[:], T.d[:], AF.Abs, ["d"], ["de"])
+    act(T.de[:], T.de[:], AF.Relu, ["de"], ["de"], bias=1.0, scale=-1.0)
+    act(T.MH[:], T.de[:], AF.Identity, ["de"], ["MH"], bias=-INF, scale=2 * INF)
+    sel(T.RH[:], T.k3[:], [[0, 21], [1, 16]], AL.is_gt, -INF, 0, 0, ["k3"], "RH")
+    act(T.dn[:], T.d[:], AF.Sign, ["d"], ["dn"], scale=-1.0)
+    act(T.k1[:], T.dn[:], AF.Relu, ["dn"], ["k1"], scale=4096.0)
+    act(T.k2[:], T.de[:], AF.Copy, ["de"], ["k2"], scale=-1024.0)
+    cp(bc[:, 1:2], T.pI[:, 2:3], ["pI2"], ["g"])
+    ts(bc[:, 3:4], bc[:, 0:1], 0.0, -3072.0, AL.is_equal, AL.mult, ["i"], ["bn"])
+    for k, sg, b in ((4, 1.0, float(OFF)), (5, -1.0, 335.0 - OFF), (6, -1.0, 1024.0)):
+        act(bc[:, k:k + 1], bc[:, 3:4], AF.Identity, ["bn"], ["b%d" % k], bias=b, scale=sg)
+    fill(bc[:, 24:25], -TINY, "tiny")
+    fill(bc[:, 25:26], TINY, "tiny")
+    quant("u", 0, 128, T.uin[:], ["uin"])
+    cp(T.uuq[:].bitcast(dt.uint32), T.uq[:].bitcast(dt.uint32).indirect(T.oU[:]), ["u0", "oU"], ["uuc"])
+    act(T.uus[:], T.us[:].indirect(T.oU[:]), AF.Copy, ["u0", "oU"], ["uup"])
+    quant("x0", 0, C, T.xin[:], ["xin"])
+    for pb in ("pb0", "pb7"):
+        mm(pb, C, "uu", 0, "x0", 0, True, True, ["uuc", "uup", "x00"])
+    sel(eb("EG"), T.W4[:], [[-16, 8], [0, 64]], AL.is_ge, 0.0, 0, 1, ["W4"], "EGb")
+    sel(eb("EG"), eb("EG"), [[16, 8], [0, 64]], AL.is_ge, 0.0, 15, -1, ["EGb"], "EGb")
+    sel(eb("EA"), T.W4[:], [[0, 512]], AL.is_ge, 0.0, 15, -1, ["W4"], "EAb")
+    send_x(0)
+    iota(T.ji[:], [[1, C]], 0, 0, "ji", **f32)
+    iota(T.JR[:], [[-1, C]], 512 * OFF + 511, 0, "JR", **f32)
+    for b in range(4):
+        sel(eb("EU%d" % b), T.ones[:], [[1, 512]], AL.is_equal, 0.0, -b, -4, ["ones"], "EU%db" % b)
+    fill(T.MD[:], BIG, "MD0")
+    sel(T.MD[:], T.MD[:], [[-1, 112]], AL.is_gt, 0.0, 0, 1, ["MD0"], "MD1")
+    sel(T.MD[:], T.MD[:], [[1, 112]], AL.not_equal, -BIG, 0, -1, ["MD1"], "MD")
+
+    def consts1(q):
+        if q == 0:
+            quant("EG", 0, 256, eb("EG", 2), ["EGb", "EAb"])
+        zeros = [("C5", 1, C), ("C5", 2, C)] if q == 1 else []
+        if q == 4:
+            zeros = [("CD0", 3, 160), ("CD1", 3, 176), ("PT", 2, C), ("PT", 3, C)]
+        for n, k, m in zeros:
+            act(T[n][:, k::4], T.ones[:, 0:m], AF.Copy, ["ones"], [n + "z"], scale=0.0)
+        if q in (2, 3):
+            n, w = (("W3", (0.5, 0.5, 1.0, 0.0)), ("W2", (512.0, 512.0, 0.0, 0.0)))[q - 2]
+            for k in range(4):
+                act(T[n][:, k::4], T.ones[:, 0:128], AF.Copy, ["ones"], [n], scale=w[k])
+
+    def consts2():
+        tt(T.MN[:], T.k1[:], T.k2[:], AL.add, ["k1", "k2"], ["MN"])
+        ts(T.MN[:, 15::16], T.MN[:, 15::16], bc[:, 6:7], None, AL.add, None, ["MN", "b6"], ["MN"])
+        for t in range(R):
+            fill(T["ls%d" % t][:], 0, "ls%d" % t)
+
+    def consts3():
+        quant("EU0", 0, 512, eb("EU0", 4), ["EU%db" % b for b in range(4)])
+        act(T.k3[:, 0:160], T.de[:, 0:160], AF.Copy, ["de", "RH"], ["k3"], scale=-1024.0 + 111.5)
+        act(T.k3[:, 160:C], T.de[:, 160:C], AF.Copy, ["de", "RH"], ["k3"], scale=-1024.0 + 56.0)
+        tt(T.MNd[:], T.k1[:], T.k3[:], AL.add, ["k1", "k3"], ["MNd"])
+        ts(T.MNd[:, 15::16], T.MNd[:, 15::16], bc[:, 6:7], None, AL.add, None, ["MNd", "b6"], ["MNd"])
+        ts(T.MD[:, 111:112], T.MD[:, 111:112], BIG, None, AL.add, None, ["MD"], ["MD"])
+        act(bc[:, 8:9], bc[:, 1:2], AF.Identity, ["g"], ["g6"], bias=-6.0)
+        act(bc[:, 8:9], bc[:, 8:9], AF.Abs, ["g6"], ["g6"])
+        act(bc[:, 9:10], bc[:, 8:9], AF.Relu, ["g6"], ["m6"], bias=1.0, scale=-1.0)
+        act(bc[:, 10:11], bc[:, 9:10], AF.Copy, ["m6", "bn"], ["mb"], scale=bc[:, 3:4])
+        act(bc[:, 11:12], bc[:, 9:10], AF.Identity, ["m6", "mb"], ["c6"], bias=bc[:, 10:11], scale=14096.0)
+        act(bc[:, 11:12], bc[:, 11:12], AF.Identity, ["c6"], ["c6"], bias=-10000.0)
+        act(bc[:, 12:13], bc[:, 9:10], AF.Identity, ["m6", "bn"], ["b7"], bias=bc[:, 3:4], scale=-4096.0)
+        act(bc[:, 13:14], bc[:, 10:11], AF.Copy, ["mb"], ["nb"], scale=-1.0)
+        act(bc[:, 12:13], bc[:, 12:13], AF.Identity, ["b7", "nb"], ["b7"], bias=bc[:, 13:14])
+        quant("ED", 0, 128, eb("ED"), ["EDb"])
+
+    def places(bank, counts, hook):
+        S = T[bank]
+        tt(T.t1[:], S[:, 0:C], T.MH[:], AL.min, [bank, "MH"], ["t1"])
+        scan(T.Hd[:], T.RH[:], T.t1[:], -INF, AL.min, AL.max, ["RH", "t1"], ["Hd"])
+
+        def count(q):
+            n, k = ("C5" if q == 5 else ("Ca", "Cb")[q % 2]), ("ca", "cb")[q % 2]
+            hook(q)
+            quant(k, 0, C, T[n][:], [n + ".0", n + ".1", n + ".2", n + ".3"] + (["C5z"] if q == 5 else []))
+            for st, pb in counts:
+                mm(pb, C, st, 0, k, 0, q == 0, q == 5, [k + "0", "EG0"])
+
+        for q in range(6):
+            n = "C5" if q == 5 else ("Ca", "Cb")[q % 2]
+            for k in ((3, 0, 1, 2) if q < 5 else (3,)):
+                c = 4 * q + k if q < 5 else 20
+                m = 16 * (c + 1)
+                D = T.Hd[:, m - 1:m]
+                parts = [(0, m, AL.is_lt, 24), (m, C, AL.is_le, 25)][:1 if c == 20 else 2]
+                if k == 3:
+                    df = "df%d" % (q % 2)
+                    act(T[df][:], T.pb7[:, 0:C], AF.Identity, ["pb7", "Hd"], [df], bias=D, scale=-1.0)
+                    for a, e, o, z in parts:
+                        act(T[n][:, 4 * a + 3:4 * e:4], T[df][:, a:e], AF.Sign, [df, "tiny"], [n + ".3"],
+                            bias=bc[:, z:z + 1])
+                else:
+                    for a, e, o, z in parts:
+                        ts(T[n][:, 4 * a + k:4 * e:4], S[:, a:e], D, None, o, None, [bank, "Hd"], [n + ".%d" % k])
+                    if k == 0 and q:
+                        count(q - 1)
+            if q == 5:
+                tt(T[n][:, 0::4], S[:, 0:C], T.Hd[:], AL.is_equal, [bank, "Hd"], [n + ".0"])
+                count(4)
+                count(5)
+
+    def to_list(src, key, bias, sign, o, okey):
+        scan(T.sa[:], src, T.MN[:], 4096.0, AL.min, AL.add, [key, "MN"], ["sa"])
+        ts(o, T.sa[:, 15::16], sign, bias, AL.mult, AL.add, ["sa", "bn", "b4", "b5"], [okey])
+
+    for t in range(R):
+        pc, ls, ll, NL = part(t), T["ls%d" % t], T["ll%d" % t], T["NL%d" % t]
+        lk, X = "ls%d" % t, "x%d" % t
+        places("pb0", [("EG", "pb2"), ("EA", "pb3")], lambda q: consts1(q) if t == 0 else None)
+        if t == 0:
+            consts2()
+        for pb in ("pb1", "pb7"):
+            mm(pb, C, "uu", 128, "rx%d" % t, 0, True, True, ["uuc", "uup", "rx%d" % t])
+        to_list(T.pb2[:, 0:C], "pb2", bc[:, 4:5], 1.0, ls[:, 0:21], lk)
+        cp(T.oW[:].indirect(ls[:, 0:21]), T.ji[:], [lk, "ji"], ["oW"])
+        to_list(T.oW[:], "oW", bc[:, 3:4], 1.0, ls[:, 22:43], lk)
+        send(pc, ll[:], ls[:], "la%d" % t, [lk])
+        arrives(["ll%d" % t], "la%d" % t, ne(t))
+        if t == 0:
+            sel(eb("ED"), T.W3[:], [[0, 512]], AL.is_ge, 0.0, 111, -1, ["W3"], "EDb")
+            for k in range(8):
+                sel(eb("EP%d" % k), T.W2[:], [[0, 512]], AL.is_equal, 0.0, -16 * k, 1, ["W2"], "EP%db" % k)
+        act(T.va[:], T.pb3[:, 0:C], AF.Copy, ["pb3"], ["va"], scale=512.0)
+        to_list(T.pb3[:, 0:C], "pb3", bc[:, 5:6], -1.0, T.Lg[:, 0:21], "Lg0")
+        tt(T.V0[:], T.va[:], T.JR[:], AL.add, ["va", "JR"], ["V0.0", "V0.1"])
+        if t == 0:
+            consts3()
+
+        def unpack(q):
+            if q < 4:
+                pb = ("pb4", "pb5", "pb6", "pb0")[q]
+                mm(pb, C, "EU%d" % q, 0, "rx%d" % t, 0, True, True, ["EU00", "rx%d" % t])
+                act(pl("F", q), T[pb][:, 0:C], AF.Copy, [pb], ["F%d" % q])
+
+        places("pb1", [("EG", "pb2")], unpack)
+        if t == 0:
+            for k in (0, 4):
+                quant("EP%d" % k, 0, 512, eb("EP%d" % k, 4), ["EP%db" % (k + i) for i in range(4)])
+        ts(T.hi[:], T.pb2[:, 0:C], MAGIC, -MAGIC, AL.add, AL.add, ["pb2"], ["hi"])
+        tt(T.lo[:], T.pb2[:, 0:C], T.hi[:], AL.subtract, ["pb2", "hi"], ["lo"])
+        act(T.PT[:, 0::4], T.hi[:].indirect(ll[:, 22:43]), AF.Copy, ["hi", "ll%d" % t], ["PT0"])
+        cp(T.PT[:, 1::4], T.lo[:].indirect(ll[:, 22:43]), ["lo", "ll%d" % t], ["PT1"])
+        quant("pp", 0, C, T.PT[:], ["PTz", "PT0", "PT1"])
+
+        def table(k):
+            pb = "pb%d" % (4 + k % 4)
+            mm(pb, C, "EP%d" % k, 0, "pp", 0, True, True, ["EP%d0" % (k // 4 * 4), "pp0"])
+            act(pl("P", k), T[pb][:, 0:C], AF.Copy, [pb], ["P%d" % k])
+
+        def sort(b):
+            act(pl("G", b), pl("F", b).indirect(ll[:, 22:43]), AF.Copy, ["F%d" % b, "ll%d" % t], ["G%d" % b])
+
+        def grow(k):
+            old, new = "V%d" % (k % 2), "V%d" % ((k + 1) % 2)
+            for h in range(2):
+                a, e = HV[h]
+                tt(T[new][:, a:e], pl("P", k).indirect(T.Lg[:, 22 * k + LV[h][0]:22 * k + LV[h][1]]), T[old][:, a:e],
+                   AL.add, ["P%d" % k, "Lg%d.%d" % (k, h) if k else "Lg0", old + ".%d" % h], [new + ".%d" % h])
+
+        def hold(k):
+            V = "V%d" % ((k + 1) % 2)
+            for s in range(3):
+                scan(T.SD[:, 112 * s:112 * s + 112], T[V][:, 112 * s:112 * s + 112], T.MD[:], BIG, AL.min, AL.add,
+                     ["MD", V + ".0", V + ".1"][:3 if s else 2], ["SD%d" % s])
+
+        def rows(k):
+            dma("sy", NL[16 * k:16 * k + 16, 0:21], T.Lg[16 * k:16 * k + 16, 22 * k:22 * k + 21], "nl%d" % t, 96,
+                ["Lg%d.0" % k, "Lg%d.1" % k] if k else ["Lg0"], [] if k else ["NLd%d" % t])
+
+        table(0)
+        table(1)
+        grow(0)
+        hold(0)
+        rows(0)
+        for k in range(1, 8):
+            V = "V%d" % (k % 2)
+            for h, s in ((0, 0), (0, 1), (1, 0)):
+                a, e = HV[h]
+                act(T["CD%d" % h][:, s::4], T[V][:, a:e], AF.Sign, [V + ".%d" % h, "SD%d" % s],
+                    ["CD%d.%d" % (h, s)], bias=T.SD[:, 112 * s + 111:112 * s + 112], scale=-1.0)
+            if k < 7:
+                table(k + 1)
+            if 2 <= k < 6:
+                sort(k - 2)
+
+            def beats(h, s, two):
+                a, e = HV[h]
+                ts(T["CD%d" % h][:, s::4], T[V][:, a:e], T.SD[:, 112 * s + 111:112 * s + 112], two, AL.is_lt,
+                   AL.mult if two else None, [V + ".%d" % h, "SD%d" % s], ["CD%d.%d" % (h, s)])
+
+            beats(1, 1, 2.0)
+            beats(0, 2, None)
+            beats(1, 2, None)
+            for h in range(2):
+                n = HV[h][1] - HV[h][0]
+                quant("cd%d" % h, 0, n, T["CD%d" % h][:], ["CD%d.%d" % (h, s) for s in range(3)] + ["CD%dz" % h])
+                mm("pb%d" % h, n, "ED", 0, "cd%d" % h, 0, True, True, ["ED0", "cd%d0" % h])
+            for h in range(2):
+                a, e = HV[h]
+                scan(T.sc[:, a:e], T["pb%d" % h][:, 0:e - a], T.MNd[:, a:e], 4096.0, AL.min, AL.add,
+                     ["pb%d" % h, "MNd"], ["sc%d" % h])
+            if k == 7:
+                tt(T.x7[96:128, 0:21], T.sc[96:128, 15::16], T.x6[96:128, 0:21], AL.max, ["sc0", "sc1", "x6"], ["x7"])
+                ts(NL[96:128, 0:21], T.x7[96:128, 0:21], bc[96:128, 12:13], None, AL.add, None, ["x7", "b7"],
+                   ["NL%d" % t])
+            if k < 7 or t == R - 1:
+                for h in range(2):
+                    a, e = HV[h]
+                    ts(T.Lg[:, 22 * k + LV[h][0]:22 * k + LV[h][1]], T.sc[:, a + 15:e:16], bc[:, 3:4], None, AL.add,
+                       None, ["sc%d" % h, "bn"], ["Lg%d.%d" % (k, h)])
+            if k == 6:
+                ts(T.x6[96:128, 0:21], T.sc[96:128, 15::16], bc[96:128, 9:10], bc[96:128, 11:12], AL.mult, AL.add,
+                   ["sc0", "sc1", "m6", "c6"], ["x6"])
+            if k < 7:
+                grow(k)
+                hold(k)
+            if k < 6:
+                rows(k)
+        zk = ["NL%d" % t, "NLd%d" % t]
+        for h in range(2):
+            a, e = HV[h]
+            x, y = LV[h]
+            for b in range(4):
+                o, i = T.Z[:, 4 * a + b:4 * e:4], pl("G", b).indirect(NL[:, x:y])
+                if b < 2:
+                    cp(o, i, ["G%d" % b] + zk, ["Z%d.%d" % (h, b)])
+                else:
+                    act(o, i, AF.Copy, ["G%d" % b] + zk, ["Z%d.%d" % (h, b)])
+            quant("z", a, e, T.Z[:, 4 * a:4 * e], ["Z%d.%d" % (h, b) for b in range(4)])
+
+        def layer(h):
+            a, e = HV[h]
+            for b in range(4):
+                for j in (1, 0):
+                    mm("pb%d" % (2 * b + j), e - a, "wl", 128 * (b + 4 * j), "z", a, True, True,
+                       ["w0", "wsc", "z%d" % a])
+                act(T.yt[:, 176 * b:176 * b + e - a], T["pb%d" % (2 * b + 1)][:, 0:e - a], AF.Copy,
+                    ["pb%d" % (2 * b + 1)], ["yt%d" % b])
+
+        def best(h):
+            a, e = HV[h]
+            for b in range(4):
+                m = T.ym[:, 176 * b:176 * b + e - a]
+                tt(m, T["pb%d" % (2 * b)][:, 0:e - a], T.yt[:, 176 * b:176 * b + e - a], AL.max,
+                   ["pb%d" % (2 * b), "yt%d" % b], ["ym%d" % b])
+                act(pl("Y", b, a, e), m, AF.Copy, ["ym%d" % b], ["Y%d.%d" % (b, h)], scale=0.03125)
+
+        layer(0)
+        cp(T.iW[:].indirect(NL[:, 0:21]), T.ji[:], ["ji"] + zk, ["iW"])
+        best(0)
+        layer(1)
+        cp(T.tm[:], T.iW[:].indirect(ll[:, 0:21]), ["iW", "ll%d" % t], ["tm"])
+        to_list(T.tm[:], "tm", bc[:, 3:4], 1.0, T.ML[:, 0:21], "ML")
+        best(1)
+        for h in range(2):
+            a, e = HV[h]
+            x, y = LV[h]
+            for b in range(4):
+                o, i = T.Yp[:, 4 * a + b:4 * e:4], pl("Y", b).indirect(T.ML[:, x:y])
+                rk = ["ML", "Y%d.0" % b, "Y%d.1" % b]
+                if b < 3 - h:
+                    cp(o, i, rk, ["Yp%d.%d" % (h, b)])
+                else:
+                    act(o, i, AF.Copy, rk, ["Yp%d.%d" % (h, b)])
+            quant("y%d" % t, a, e, T.Yp[:, 4 * a:4 * e], ["Yp%d.%d" % (h, b) for b in range(4)])
+            k, sm = ["y%d%d" % (t, a)], ("ya%d", "yb%d")[h] % t
+            send(pc, T["ry%dq" % t][:, a:e].bitcast(dt.uint8), T["y%dq" % t][:, a:e].bitcast(dt.uint8), sm, k)
+            send(pc, T["ry%ds" % t][:, a:e], T["y%ds" % t][:, a:e], sm, k)
+            arrives(["ry%d.%d" % (t, h)], sm, 2 * ne(t))
+        for h in range(2):
+            a, e = HV[h]
+            for b in range(4):
+                mm("pb%d" % (4 * h + b), e - a, "EU%d" % b, 0, X, a, True, False, ["EU00", X + "0", X + "160"])
+        if t == R - 1:
+            grow(7)
+            tt(T.tb[0:1, :], T.V0[0:1, :], T.JR[0:1, :], AL.subtract, ["V0.0", "V0.1", "JR"], ["tb"])
+            ts(T.tb[0:1, :], T.tb[0:1, :], 2.0 ** -9, 9.0 * OFF, AL.mult, AL.add, ["tb"], ["tb"])
+            dma("sy", T.tot[:], T.tb[0:1, :], "out", 0, ["tb"], [])
+            quant("v", 0, 128, T.vin[:], ["vin"])
+        N, xt = "x%d" % (t + 1), T["xt%d" % t]
+        for h in range(2):
+            a, e = HV[h]
+            for b in range(4):
+                pb = "pb%d" % (4 * h + b)
+                mm(pb, e - a, "EU%d" % b, 0, "ry%d" % t, a, False, True, ["ry%d.%d" % (t, h)])
+                o = xt[:, 4 * a + b:4 * e:4]
+                if b > 0:
+                    cp(o, T[pb][:, 0:e - a], [pb], ["xt%d.%d" % (h, b)])
+                else:
+                    act(o, T[pb][:, 0:e - a], AF.Copy, [pb], ["xt%d.%d" % (h, b)])
+            quant(N, a, e, xt[:, 4 * a:4 * e], ["xt%d.%d" % (h, b) for b in range(4)])
+        if t < R - 1:
+            send_x(t + 1)
+            for pb in ("pb0", "pb7"):
+                mm(pb, C, "uu", 0, N, 0, True, True, [N + "0", N + "160"])
+    nk = ["x20", "x2160"]
+    mm("pb0", C, "v", 0, "x2", 0, True, True, ["v0"] + nk)
+    dma("sy", T.oc[:], T.x2q[:].bitcast(dt.uint8), "out", 0, nk, [])
+    act(T.ysb[:], T.pb0[:, 0:C], AF.Copy, ["pb0"], ["ysb"])
+    for k in range(4):
+        dma("sy", T.osc[4 * k:4 * k + 4, :], T.x2s[32 * k:32 * k + 4, :], "out", 0, nk, [])
+    dma("ac", T.y[:], T.ysb[:], "out", 0, ["ysb"], [])
+    for s in tick:
+        g.wait_ge(T.sem[s], tick[s])
+    for s in dcount:
+        g.wait_ge(T.sem[s], dcount[s])
+    for s in arr:
+        g.wait_ge(T.sem[s], arr[s])
+    g.wait_ge(T.sem.loc, sent[0])

@@ -6,9 +6,18 @@ HV = [(0, 160), (160, 336)]
 LV = [(0, 10), (10, 21)]
 INF = float(2 ** 90)
 TINY = float(2.0 ** -120)
-BIG = float(2 ** 21)
-MAGIC = 1.5 * 2.0 ** 28
-OFF = 47
+M32 = 1.5 * 2.0 ** 28
+M1 = 1.5 * 2.0 ** 23
+KEY = 385.0
+BASE = float(2 ** 18)
+UP = 128
+MID = 168.0 + UP
+SW, TW = 184, 704
+S0 = 175
+TILES = [(("d", 13, 12, 11), 336, "ERc"), ((10, 9, 8, 7), 160, "ERc"), ((6, 5), 128, "ERc"),
+         ((20, 19, 18, 17), 320, "ERb"), ((16, 15, 14, 1), 256, "ERb"), ((4, 3, 2), 128, "ERb")]
+ON_ACT = [20, 19, 18, 17, 16, 15, 14, 1, 4, 3, 2]
+ON_VE = range(13, 4, -1)
 
 SCRATCH = {}
 
@@ -22,51 +31,59 @@ def _q(name, n):
     _s(name + "s", n, "uint8")
 
 
-CONST = ["EU0", "EU1", "EU2", "EU3", "EG", "EA", "ED"] + ["EP%d" % _k for _k in range(8)]
-for _n in ("xin", "xt0", "xt1", "Z", "Yp", "Ca", "Cb", "C5", "PT", "F", "G", "Y"):
+CONST = ["ERc", "ERb", "EL", "EU0", "EU1", "EU2", "EU3", "ETp", "EP0a", "EP0b", "EX", "EK"]
+BATCH = {"ERc": 2, "EL": 1, "EU0": 4, "ETp": 3, "EX": 2}
+VB = [("pb0", "pb1"), ("pb6", "pb7")]
+_s("XT", 8 * C, "bfloat16")
+for _n in ("xin", "xt0", "xt1", "Z", "Yp", "PT", "F", "G"):
     _s(_n, 4 * C, "bfloat16")
-for _n in ("uin", "vin", "ones", "W2", "W3", "W4"):
+for _n in ("uin", "vin", "ones", "W1"):
     _s(_n, 512, "bfloat16")
 _s("Eb", 512 * len(CONST), "bfloat16")
 _q("E", 128 * len(CONST))
-for _n in ("yt", "ym"):
-    _s(_n, 4 * 176)
-_s("P", 8 * C)
-_s("Lg", 8 * 22, "uint16")
+_s("yt", 4 * 176)
+_s("Ym", 4 * C)
+_s("TT", TW, "bfloat16")
+_s("TB", 7 * TW, "bfloat16")
+_s("SM", 7 * SW)
+_s("J", 21 * 112)
+_s("LS", 256)
+_s("K1", 384)
 for _k in range(8):
     _s("pb%d" % _k, 512, "float32", "psum")
-for _n, _k in (("u", 128), ("v", 128), ("uu", 256), ("wl", 1024), ("ca", C), ("cb", C), ("z", C), ("pp", C)):
+for _n, _k in (("u", 128), ("v", 128), ("uu", 256), ("wl", 1024), ("z", C), ("pp", C), ("xx", 2 * C), ("xk", C),
+               ("lt", 160), ("lf", 128), ("rq", sum(_t[1] for _t in TILES))):
     _q(_n, _k)
-for _h in range(2):
-    _s("CD%d" % _h, 4 * (HV[_h][1] - HV[_h][0]), "bfloat16")
-    _q("cd%d" % _h, HV[_h][1] - HV[_h][0])
-    _s("V%d" % _h, C)
-    _s("df%d" % _h, C)
+_s("RT", 4 * sum(_t[1] for _t in TILES), "bfloat16")
 for _t in range(R):
     _q("rx%d" % _t, C)
     _q("ry%d" % _t, C)
     _q("y%d" % _t, C)
-    _s("ls%d" % _t, 44, "uint16")
-    _s("ll%d" % _t, 44, "uint16")
-    _s("NL%d" % _t, 22, "uint16")
+    _s("ls%d" % _t, 21, "uint16")
+    _s("ll%d" % _t, 21, "uint16")
 for _t in range(R + 1):
     _q("x%d" % _t, C)
-for _n in ("jp", "ji", "d", "dn", "de", "k1", "k2", "k3", "JR", "MN", "MNd", "MH", "RH", "t1", "Hd", "sa", "oW", "iW",
-           "tm", "tb", "va", "SD", "ysb", "sc"):
+for _n in ("jp", "ji", "d", "de", "k1", "JR", "nt", "MN", "MNx", "MH", "RH", "t1", "Hd", "sa", "sx", "oW", "iW",
+           "tm", "tb", "Bx", "P0", "y1", "y2", "Vs", "df0", "df1", "ysb"):
     _s(_n, C)
-_s("hi", C, "bfloat16")
-_s("lo", C, "bfloat16")
-_s("MD", 112)
-_s("x6", 22)
-_s("x7", 22)
-_s("pI", 4, "int32")
-_s("oI", 16, "int32")
+for _n in ("rm", "DS", "CB"):
+    _s(_n, C, "bfloat16")
+_s("jk", 3 * C, "bfloat16")
+for _n in ("M48", "G48", "s48"):
+    _s(_n, 48)
+_s("sm", 128)
+_s("pI", 128, "int32")
+_s("CL", 64, "uint16")
 _s("oU", 16, "uint16")
-_s("ML", 22, "uint16")
+_s("OF", 48, "uint16")
+_s("NL", 32, "uint16")
+for _n in ("ML", "IL", "L0s", "L0"):
+    _s(_n, 22, "uint16")
 _s("bc", 32)
 
-SEMAPHORES = ["ve", "ac", "pe", "gp", "lx", "lu", "lv", "lw", "lz", "out", "loc"]
-SEMAPHORES += ["%s%d" % (a, t) for a in ("xa", "la", "nl", "ya", "yb") for t in range(R)]
+SEMAPHORES = ["ve", "ac", "pe", "gp", "lx", "lu", "lv", "lw", "lz", "out", "loc", "l0"]
+SEMAPHORES += ["tb%d" % _g for _g in range(1, 8)]
+SEMAPHORES += ["%s%d" % (a, t) for a in ("xa", "la", "ya", "yb") for t in range(R)]
 
 
 def rank_program(g, core, T, topo):
@@ -102,14 +119,16 @@ def rank_program(g, core, T, topo):
         for k in writes:
             wr.setdefault(k, {})[e] = tick[e]
 
-    def dma(e, out, in_, sem, total, reads=(), writes=()):
+    def dmas(e, pairs, sem, reads=(), writes=()):
         deps(e, reads, writes)
-        queue[e].dma_start(out, in_).then_inc(T.sem[sem], 16)
-        dcount[sem] = dcount.get(sem, 0) + 16
+        for out, in_ in pairs:
+            queue[e].dma_start(out, in_).then_inc(T.sem[sem], 16)
+        dcount[sem] = dcount.get(sem, 0) + 16 * len(pairs)
         for k in writes:
-            wr.setdefault(k, {})[sem] = total
-        for k in reads:
-            rd.setdefault(k, {})[sem] = total
+            wr.setdefault(k, {})[sem] = dcount[sem]
+        if sem != "out":
+            for k in reads:
+                rd.setdefault(k, {})[sem] = dcount[sem]
 
     def tt(out, a, b, o, reads, writes):
         op("ve", lambda q: q.tensor_tensor(out, a, b, o), reads, writes)
@@ -135,9 +154,9 @@ def rank_program(g, core, T, topo):
     def at(n):
         return ("E", 128 * CONST.index(n)) if n in CONST else (n, 0)
 
-    def eb(n, m=1):
+    def eb(n, m=1, a=0, step=1):
         k = 512 * CONST.index(n)
-        return T.Eb[:, k:k + 512 * m]
+        return T.Eb[:, k + a:k + 512 * m:step]
 
     def pl(n, b, a=0, e=C):
         return T[n][:, C * b + a:C * b + e]
@@ -147,9 +166,15 @@ def rank_program(g, core, T, topo):
         op("ve", lambda q: q.quantize_mx(T[n + "q"][:, o + a:o + b], T[n + "s"][:, o + a:o + b], src),
            reads, [name + str(a)])
 
+    def quantc(name):
+        k, m = CONST.index(name), BATCH[name]
+        quant(name, 0, 128 * m, eb(name, m), [n + "b" for n in CONST[k:k + m]])
+
     def mm(bank, n, st, sa, mv, ma, start, stop, reads):
         w, o = at(st)
         o += sa
+        if st in CONST:
+            reads = reads + [[b for b in CONST[:CONST.index(st) + 1] if b in BATCH][-1] + "0"]
         op("pe", lambda q: q.matmul_mx(T[bank][:, 0:n], T[w + "q"][:, o:o + 128], T[w + "s"][:, o:o + 128],
                                        T[mv + "q"][:, ma:ma + n], T[mv + "s"][:, ma:ma + n], start, stop),
            reads, [bank])
@@ -177,253 +202,330 @@ def rank_program(g, core, T, topo):
         send(part(t), T["rx%ds" % t][:], T["x%ds" % t][:], "xa%d" % t, ["x%d0" % t])
         arrives(["rx%d" % t], "xa%d" % t, 2 * ne(t))
 
-    dma("sy", T.xin[:], T.x[:], "lx", 16, (), ["xin"])
-    dma("ac", T.uin[:], T.u[:], "lu", 16, (), ["uin"])
-    dma("sy", T.wlq[:].bitcast(dt.uint8), T.wc[:], "lw", 16, (), ["w0"])
-    dma("sy", T.vin[:], T.v[:], "lv", 16, (), ["vin"])
-    dma("sy", T.wls[:], T.ws[:], "lz", 16, (), ["wsc"])
+    dmas("sy", [(T.xin[:], T.x[:])], "lx", (), ["xin"])
+    dmas("ac", [(T.uin[:], T.u[:])], "lu", (), ["uin"])
+    dmas("sy", [(T.wlq[:].bitcast(dt.uint8), T.wc[:])], "lw", (), ["w0"])
+    dmas("sy", [(T.vin[:], T.v[:])], "lv", (), ["vin"])
+    dmas("sy", [(T.wls[:], T.ws[:])], "lz", (), ["wsc"])
     f32 = dict(allow_small_or_imprecise_dtypes=True)
-    bc = T.bc
+    bc, sm, pI, CL = T.bc, T.sm, T.pI, T.CL
+    CX, CW, CK, CP, CB, CF = CL[:, 0:21], CL[:, 22:25], CL[:, 26:29], CL[:, 30:32], CL[:, 32:42], CL[:, 42:46]
+    MC, X2 = sm[:, 8:29], sm[:, 32:53]
+    start, slot, o = {}, {}, 0
+    for q, (blocks, w, _e) in enumerate(TILES):
+        start[q] = o
+        for k, c in enumerate(blocks):
+            slot[c] = 4 * o + k
+        o += w
+    zs = ["RTz%d" % q for q in start]
 
     def iota(ap, pat, base, cm, key, **k):
         op("gp", lambda q: q.iota(ap, pat, base, cm, **k), [], [key])
 
+    def flat(ap, val, key):
+        iota(ap, [[0, ap.shape[1]]], val, 0, key, **f32)
+
     def sel(ap, src, pat, o, fl, base, cm, reads, key):
         op("gp", lambda q: q.affine_select(ap, src, pat, o, fl, base, cm), reads, [key])
 
-    iota(T.pI[:, 0:1], [[1, 1]], 0, 1, "pI")
-    iota(T.oI[:], [[1, 2], [16, 8]], 0, 0, "oI")
+    fill(T.W1[:], -1.0, "W1")
+    iota(pI[:, 0:1], [[1, 1]], 0, 1, "pI")
     iota(T.jp[:], [[0, 21], [1, 16]], 0, 0, "jp", **f32)
+    iota(pI[:, 16:32], [[1, 2], [16, 8]], 0, 0, "oI")
+    sel(eb("ERc"), T.W1[:], [[-16, 8], [0, 64]], AL.is_ge, 0.0, 0, 1, ["W1"], "ERcb")
+    sel(eb("ERc"), eb("ERc"), [[16, 8], [0, 64]], AL.is_ge, 0.0, 15, -1, ["ERcb"], "ERcb")
     fill(T.ones[:], 1.0, "ones")
-    fill(T.k3[:], INF, "k3")
-    fill(T.W4[:], 1.0, "W4")
-    ts(T.W4[:, 3::4], T.W4[:, 3::4], 0.5, None, AL.mult, None, ["W4"], ["W4"])
-    ts(T.pI[:, 1:2], T.pI[:, 0:1], 15, None, AL.bitwise_and, None, ["pI"], ["pI1"])
-    ts(T.pI[:, 2:3], T.pI[:, 0:1], 4, None, AL.arith_shift_right, None, ["pI"], ["pI2"])
-    cp(bc[:, 0:1], T.pI[:, 1:2], ["pI1"], ["i"])
-    cp(T.oU[:], T.oI[:], ["oI"], ["oU"])
-    ts(T.d[:], T.jp[:], bc[:, 0:1], None, AL.subtract, None, ["jp", "i"], ["d"])
-    act(T.de[:], T.d[:], AF.Abs, ["d"], ["de"])
-    act(T.de[:], T.de[:], AF.Relu, ["de"], ["de"], bias=1.0, scale=-1.0)
-    act(T.MH[:], T.de[:], AF.Identity, ["de"], ["MH"], bias=-INF, scale=2 * INF)
-    sel(T.RH[:], T.k3[:], [[0, 21], [1, 16]], AL.is_gt, -INF, 0, 0, ["k3"], "RH")
-    act(T.dn[:], T.d[:], AF.Sign, ["d"], ["dn"], scale=-1.0)
-    act(T.k1[:], T.dn[:], AF.Relu, ["dn"], ["k1"], scale=4096.0)
-    act(T.k2[:], T.de[:], AF.Copy, ["de"], ["k2"], scale=-1024.0)
-    cp(bc[:, 1:2], T.pI[:, 2:3], ["pI2"], ["g"])
-    ts(bc[:, 3:4], bc[:, 0:1], 0.0, -3072.0, AL.is_equal, AL.mult, ["i"], ["bn"])
-    for k, sg, b in ((4, 1.0, float(OFF)), (5, -1.0, 335.0 - OFF), (6, -1.0, 1024.0)):
-        act(bc[:, k:k + 1], bc[:, 3:4], AF.Identity, ["bn"], ["b%d" % k], bias=b, scale=sg)
-    fill(bc[:, 24:25], -TINY, "tiny")
+    ts(pI[:, 1:2], pI[:, 0:1], 15, None, AL.bitwise_and, None, ["pI"], ["pI1"])
+    ts(pI[:, 2:3], pI[:, 0:1], 4, None, AL.arith_shift_right, None, ["pI"], ["pI2"])
     fill(bc[:, 25:26], TINY, "tiny")
+    cp(bc[:, 0:2], pI[:, 1:3], ["pI1", "pI2"], ["i"])
+    act(T.rm[:], T.jp[:], AF.Sign, ["jp"], ["rm"])
+    act(T.RH[:], T.rm[:], AF.Identity, ["rm"], ["RH"], bias=INF, scale=-2 * INF)
+    for q, (blocks, w, _e) in enumerate(TILES):
+        z = min([16 * c for c in blocks if c != "d"]) if len(blocks) == 4 else 0
+        fill(T.RT[:, 4 * (start[q] + z):4 * (start[q] + w)], 0.0, "RTz%d" % q)
+        if q == 0:
+            ts(T.d[:], T.jp[:], bc[:, 0:1], None, AL.subtract, None, ["jp", "i"], ["d"])
+            cp(T.oU[:], pI[:, 16:32], ["oI"], ["oU"])
+        if q == 1:
+            ts(T.de[:], T.d[:], 0.0, None, AL.is_equal, None, ["d"], ["de"])
+    act(T.k1[:], T.d[:], AF.Sign, ["d"], ["k1"], scale=-1.0)
+    act(T.MH[:], T.de[:], AF.Identity, ["de"], ["MH"], bias=INF, scale=-2 * INF)
+    act(T.k1[:], T.k1[:], AF.Abs, ["k1"], ["k1"], bias=2048.0, scale=5120.0)
     quant("u", 0, 128, T.uin[:], ["uin"])
     cp(T.uuq[:].bitcast(dt.uint32), T.uq[:].bitcast(dt.uint32).indirect(T.oU[:]), ["u0", "oU"], ["uuc"])
     act(T.uus[:], T.us[:].indirect(T.oU[:]), AF.Copy, ["u0", "oU"], ["uup"])
     quant("x0", 0, C, T.xin[:], ["xin"])
     for pb in ("pb0", "pb7"):
         mm(pb, C, "uu", 0, "x0", 0, True, True, ["uuc", "uup", "x00"])
-    sel(eb("EG"), T.W4[:], [[-16, 8], [0, 64]], AL.is_ge, 0.0, 0, 1, ["W4"], "EGb")
-    sel(eb("EG"), eb("EG"), [[16, 8], [0, 64]], AL.is_ge, 0.0, 15, -1, ["EGb"], "EGb")
-    sel(eb("EA"), T.W4[:], [[0, 512]], AL.is_ge, 0.0, 15, -1, ["W4"], "EAb")
+    act(eb("ERb"), eb("ERc"), AF.Copy, ["ERcb"], ["ERbb"], scale=0.5)
+    act(T.MNx[:], T.k1[:], AF.Identity, ["k1"], ["MNx"], bias=-3072.0)
+    act(bc[:, 2:3], T.de[:, 15:16], AF.Identity, ["de", "i"], ["b2"], bias=bc[:, 0:1], scale=-1024.0)
+    for a, e, step, base in ((0, 5, 0, 232), (5, 14, -16, 264 - 80), (14, 21, 0, 160)):
+        iota(sm[:, 64 + a:64 + e], [[step, e - a]], base + UP + 1024, 0, "c15", **f32)
+    flat(T.J[:, 111:112], 0, "J0")
+    act(MC, sm[:, 64:85], AF.Identity, ["c15", "b2"], ["MC"], bias=bc[:, 2:3])
+    quantc("ERc")
     send_x(0)
     iota(T.ji[:], [[1, C]], 0, 0, "ji", **f32)
-    iota(T.JR[:], [[-1, C]], 512 * OFF + 511, 0, "JR", **f32)
+    iota(pI[:, 32:53], [[16, 21]], 15, 0, "CXi")
+    iota(pI[:, 64:80], [[0, 8], [16, 2]], 0, 0, "e16")
+    iota(pI[:, 80:94], [[SW, 7], [0, 2]], S0, 0, "w14")
+    iota(sm[:, 88:91], [[16, 3]], 0, 3, "k3", **f32)
+    iota(sm[:, 92:94], [[16, 2]], 0, 2, "p2", **f32)
     for b in range(4):
         sel(eb("EU%d" % b), T.ones[:], [[1, 512]], AL.is_equal, 0.0, -b, -4, ["ones"], "EU%db" % b)
-    fill(T.MD[:], BIG, "MD0")
-    sel(T.MD[:], T.MD[:], [[-1, 112]], AL.is_gt, 0.0, 0, 1, ["MD0"], "MD1")
-    sel(T.MD[:], T.MD[:], [[1, 112]], AL.not_equal, -BIG, 0, -1, ["MD1"], "MD")
 
-    def consts1(q):
+    def consts_gp():
+        sel(eb("EP0b"), T.W1[:], [[0, 512]], AL.is_ge, 0.0, 15, -1, ["W1"], "EP0bb")
+        flat(T.PT[:], 0, "PTz")
+        iota(T.nt[:], [[-int(KEY), C]], 0, 0, "nt", **f32)
+        iota(T.JR[:], [[-1, C]], int(BASE) + 335, 0, "JR", **f32)
+        for ap, val, key in ((T.K1[:, C:384], 0, "K1z"), (T.TT[:, C:352], 0, "TTz"), (T.TT[:, 688:TW], 0, "TTz"),
+                             (T.SM[:, S0 + 3::SW], -337, "SMc"), (T.SM[:, S0 + 4::SW], 0, "SMc"),
+                             (T.LS[:, 21:32], 0, "LS0"), (bc[:, 13:15], 0, "pc")):
+            flat(ap, val, key)
+        for j, big in enumerate((1.5 * 2.0 ** 43, 1.5 * 2.0 ** 38, 1.5 * 2.0 ** 33, M32)):
+            sel(bc[:, 13:15], bc[:, 13:15], [[8, 2]], AL.not_equal, big, -8 * j, 1, ["pc"], "pc")
+
+    def consts_ac(q):
         if q == 0:
-            quant("EG", 0, 256, eb("EG", 2), ["EGb", "EAb"])
-        zeros = [("C5", 1, C), ("C5", 2, C)] if q == 1 else []
-        if q == 4:
-            zeros = [("CD0", 3, 160), ("CD1", 3, 176), ("PT", 2, C), ("PT", 3, C)]
-        for n, k, m in zeros:
-            act(T[n][:, k::4], T.ones[:, 0:m], AF.Copy, ["ones"], [n + "z"], scale=0.0)
-        if q in (2, 3):
-            n, w = (("W3", (0.5, 0.5, 1.0, 0.0)), ("W2", (512.0, 512.0, 0.0, 0.0)))[q - 2]
+            act(T.MN[:], T.k1[:], AF.Identity, ["k1"], ["MN"], bias=-3072.0)
+            act(T.M48[:], T.MN[:, 0:48], AF.Copy, ["MN"], ["M48"], scale=2048.0)
+            act(T.MN[:, 15::16], T.MN[:, 15::16], AF.Identity, ["MN"], ["MN"], bias=1536.0)
+            act(eb("ETp"), eb("ERc"), AF.Copy, ["ERcb"], ["ETpb"], scale=-1.0)
+            sel(eb("ETp", 1, 0, 4), eb("ETp", 1, 0, 4), [[0, 8], [-1, 16]], AL.is_ge, 0.0, 1, 0, ["ETpb"], "ETpb")
+            sel(eb("ETp", 1, 1, 4), eb("ETp", 1, 1, 4), [[0, 8], [1, 16]], AL.is_ge, 0.0, -14, 0, ["ETpb"], "ETpb")
+        if q == 1:
+            act(eb("EP0a"), eb("EP0b"), AF.Copy, ["EP0bb"], ["EP0ab"], scale=KEY - 1)
+            act(bc[:, 7:8], T.de[:, 15:16], AF.Identity, ["de"], ["b7"], bias=2.0 ** 21, scale=-2.0 ** 21)
+            act(bc[:, 21:22], bc[:, 7:8], AF.Identity, ["b7"], ["b21"], bias=2.0 ** 19)
+            act(bc[:, 16:18], T.de[:, 0:15:14], AF.Copy, ["de"], ["b8"], scale=KEY - 1, accum_out=bc[:, 8:9])
+            act(bc[:, 18:20], T.de[:, 1:16:14], AF.Copy, ["de"], ["b9"], accum_out=bc[:, 9:10])
+            act(bc[:, 26:27], bc[:, 13:14], AF.Sign, ["pc"], ["b26"])
+            act(bc[:, 8:9], bc[:, 8:9], AF.Identity, ["b8", "b9"], ["b8"], bias=bc[:, 9:10])
+            act(eb("EK"), T.ones[:], AF.Copy, ["ones", "b26"], ["EKb"], scale=bc[:, 26:27])
+            act(eb("EX"), T.ones[:], AF.Copy, ["ones", "b8"], ["EXb"], scale=bc[:, 8:9])
+            act(eb("EK", 1, 1, 4), T.ones[:, 0:128], AF.Copy, ["ones", "EKb"], ["EKb"], scale=0.0)
+        if q == 2:
             for k in range(4):
-                act(T[n][:, k::4], T.ones[:, 0:128], AF.Copy, ["ones"], [n], scale=w[k])
+                act(eb("EL", 1, k, 4), T.de[:, 0:128], AF.Copy, ["de"], ["ELb"])
 
-    def consts2():
-        tt(T.MN[:], T.k1[:], T.k2[:], AL.add, ["k1", "k2"], ["MN"])
-        ts(T.MN[:, 15::16], T.MN[:, 15::16], bc[:, 6:7], None, AL.add, None, ["MN", "b6"], ["MN"])
-        for t in range(R):
-            fill(T["ls%d" % t][:], 0, "ls%d" % t)
+    def consts_ve():
+        v, z = pI[:, 64:80], pI[:, 96:110]
+        ts(bc[:, 3:4], bc[:, 1:2], -3.0, bc[:, 0:1], AL.mult, AL.add, ["i"], ["b3"])
+        cp(CX, pI[:, 32:53], ["CXi"], ["CX"])
+        ts(v, v, bc[:, 3:4], None, AL.add, None, ["e16", "b3"], ["e16"])
+        ts(CK, sm[:, 88:91], bc[:, 0:1], bc[:, 0:1], AL.subtract, AL.subtract, ["k3", "i"], ["CK"])
+        ts(v, v, 63, None, AL.bitwise_and, None, ["e16"], ["e16"])
+        ts(CP, sm[:, 92:94], bc[:, 0:1], None, AL.subtract, None, ["p2", "i"], ["CP"])
+        ts(z, pI[:, 64:78], 3.0, 1.2, AL.min, AL.mult, ["e16"], ["z14"])
+        ts(CL[:, 22:24], pI[:, 64:66], 3.0, float(S0), AL.min, AL.add, ["e16"], ["CW"])
+        ts(CL[:, 24:25], bc[:, 0:1], 3.0, float(S0), AL.min, AL.add, ["i"], ["CW"])
+        tt(z, z, pI[:, 80:94], AL.add, ["z14", "w14"], ["z14"])
+        cp(CL[:, 32:46], z, ["z14"], ["CB"])
 
-    def consts3():
-        quant("EU0", 0, 512, eb("EU0", 4), ["EU%db" % b for b in range(4)])
-        act(T.k3[:, 0:160], T.de[:, 0:160], AF.Copy, ["de", "RH"], ["k3"], scale=-1024.0 + 111.5)
-        act(T.k3[:, 160:C], T.de[:, 160:C], AF.Copy, ["de", "RH"], ["k3"], scale=-1024.0 + 56.0)
-        tt(T.MNd[:], T.k1[:], T.k3[:], AL.add, ["k1", "k3"], ["MNd"])
-        ts(T.MNd[:, 15::16], T.MNd[:, 15::16], bc[:, 6:7], None, AL.add, None, ["MNd", "b6"], ["MNd"])
-        ts(T.MD[:, 111:112], T.MD[:, 111:112], BIG, None, AL.add, None, ["MD"], ["MD"])
-        act(bc[:, 8:9], bc[:, 1:2], AF.Identity, ["g"], ["g6"], bias=-6.0)
-        act(bc[:, 8:9], bc[:, 8:9], AF.Abs, ["g6"], ["g6"])
-        act(bc[:, 9:10], bc[:, 8:9], AF.Relu, ["g6"], ["m6"], bias=1.0, scale=-1.0)
-        act(bc[:, 10:11], bc[:, 9:10], AF.Copy, ["m6", "bn"], ["mb"], scale=bc[:, 3:4])
-        act(bc[:, 11:12], bc[:, 9:10], AF.Identity, ["m6", "mb"], ["c6"], bias=bc[:, 10:11], scale=14096.0)
-        act(bc[:, 11:12], bc[:, 11:12], AF.Identity, ["c6"], ["c6"], bias=-10000.0)
-        act(bc[:, 12:13], bc[:, 9:10], AF.Identity, ["m6", "bn"], ["b7"], bias=bc[:, 3:4], scale=-4096.0)
-        act(bc[:, 13:14], bc[:, 10:11], AF.Copy, ["mb"], ["nb"], scale=-1.0)
-        act(bc[:, 12:13], bc[:, 12:13], AF.Identity, ["b7", "nb"], ["b7"], bias=bc[:, 13:14])
-        quant("ED", 0, 128, eb("ED"), ["EDb"])
-
-    def places(bank, counts, hook):
+    def places(bank, hook):
         S = T[bank]
-        tt(T.t1[:], S[:, 0:C], T.MH[:], AL.min, [bank, "MH"], ["t1"])
-        scan(T.Hd[:], T.RH[:], T.t1[:], -INF, AL.min, AL.max, ["RH", "t1"], ["Hd"])
+        for a, e, k in ((224, C, "h"), (0, 224, "l")):
+            tt(T.t1[:, a:e], S[:, a:e], T.MH[:, a:e], AL.max, [bank, "MH"], ["t1" + k])
+            scan(T.Hd[:, a:e], T.RH[:, a:e], T.t1[:, a:e], INF, AL.max, AL.min, ["RH", "t1" + k], ["Hd" + k])
+
+        def cells(c, a, e):
+            return T.RT[:, slot[c] + 4 * a:slot[c] + 4 * e - 3:4]
+
+        def diff(n):
+            c = ON_ACT[n]
+            act(T["df%d" % (n % 2)][:, 0:16 * c], T.pb7[:, 0:16 * c], AF.Identity,
+                ["pb7", "Hdh" if c > 13 else "Hdl"], ["df%d" % (n % 2)], bias=T.Hd[:, 16 * c + 15:16 * c + 16],
+                scale=-1.0)
+
+        diff(0)
+        for n, c in enumerate(ON_ACT):
+            if n + 1 < len(ON_ACT):
+                diff(n + 1)
+            act(cells(c, 0, 16 * c), T["df%d" % (n % 2)][:, 0:16 * c], AF.Sign, ["df%d" % (n % 2), "tiny"] + zs,
+                ["RT.%s" % c, "J%d" % c], bias=bc[:, 25:26], scale=-1.0,
+                accum_out=T.J[:, 112 * c + 111:112 * c + 112])
+            if c in (14, 2):
+                a, e = (14, 21) if c == 14 else (1, 5)
+                v = T.J[:, 112 * a + 111:112 * e:112]
+                jk = ["J%d" % j for j in range(a, e)]
+                act(v, v, AF.Copy, jk, jk, scale=0.5)
+        hook(-1)
 
         def count(q):
-            n, k = ("C5" if q == 5 else ("Ca", "Cb")[q % 2]), ("ca", "cb")[q % 2]
-            hook(q)
-            quant(k, 0, C, T[n][:], [n + ".0", n + ".1", n + ".2", n + ".3"] + (["C5z"] if q == 5 else []))
-            for st, pb in counts:
-                mm(pb, C, st, 0, k, 0, q == 0, q == 5, [k + "0", "EG0"])
+            blocks, w, st = TILES[q]
+            quant("rq", start[q], start[q] + w, T.RT[:, 4 * start[q]:4 * (start[q] + w)],
+                  ["RT.%s" % c for c in blocks] + ["RTz%d" % q])
+            mm("pb2", w, st, 0, "rq", start[q], q == 0, q == 5, ["rq%d" % start[q]])
 
-        for q in range(6):
-            n = "C5" if q == 5 else ("Ca", "Cb")[q % 2]
-            for k in ((3, 0, 1, 2) if q < 5 else (3,)):
-                c = 4 * q + k if q < 5 else 20
-                m = 16 * (c + 1)
-                D = T.Hd[:, m - 1:m]
-                parts = [(0, m, AL.is_lt, 24), (m, C, AL.is_le, 25)][:1 if c == 20 else 2]
-                if k == 3:
-                    df = "df%d" % (q % 2)
-                    act(T[df][:], T.pb7[:, 0:C], AF.Identity, ["pb7", "Hd"], [df], bias=D, scale=-1.0)
-                    for a, e, o, z in parts:
-                        act(T[n][:, 4 * a + 3:4 * e:4], T[df][:, a:e], AF.Sign, [df, "tiny"], [n + ".3"],
-                            bias=bc[:, z:z + 1])
-                else:
-                    for a, e, o, z in parts:
-                        ts(T[n][:, 4 * a + k:4 * e:4], S[:, a:e], D, None, o, None, [bank, "Hd"], [n + ".%d" % k])
-                    if k == 0 and q:
-                        count(q - 1)
-            if q == 5:
-                tt(T[n][:, 0::4], S[:, 0:C], T.Hd[:], AL.is_equal, [bank, "Hd"], [n + ".0"])
-                count(4)
-                count(5)
+        def sums(c):
+            scan(T.J[:, 112 * c + 112 - 8 * c:112 * c + 112], cells(c, 0, 8 * c), cells(c, 8 * c, 16 * c), 0.0,
+                 AL.add, AL.add, ["RT.%s" % c], ["J%d" % c])
 
-    def to_list(src, key, bias, sign, o, okey):
+        tt(cells("d", 0, C), S[:, 0:C], T.Hd[:], AL.is_gt, [bank, "Hdh", "Hdl"] + zs, ["RT.d"])
+        for c in ON_VE:
+            ts(cells(c, 0, 16 * c), S[:, 0:16 * c], T.Hd[:, 16 * c + 15:16 * c + 16], None, AL.is_ge, None,
+               [bank, "Hdl"] + zs, ["RT.%s" % c])
+            if c == 13:
+                scan(T.DS[:], T.rm[:], cells("d", 0, C), 0.0, AL.mult, AL.add, ["rm", "RT.d"], ["DS"])
+            else:
+                sums(c + 1)
+            if c in (10, 6):
+                count({10: 0, 6: 1}[c])
+        count(3)
+        sums(5)
+        count(2)
+        tt(X2, T.DS[:, 15::16], MC, AL.add, ["DS", "MC"], ["X2"])
+        hook(0)
+        count(4)
+        count(5)
+        tt(T.MNx[:, 15::16], T.J[:, 111::112], X2, AL.add, ["X2"] + ["J%d" % c for c in range(21)], ["MNx"])
+        scan(T.sx[:], T.pb2[:, 0:C], T.MNx[:], 4096.0, AL.min, AL.add, ["pb2", "MNx"], ["sx"])
+
+    def to_list(src, key, o, okey):
         scan(T.sa[:], src, T.MN[:], 4096.0, AL.min, AL.add, [key, "MN"], ["sa"])
-        ts(o, T.sa[:, 15::16], sign, bias, AL.mult, AL.add, ["sa", "bn", "b4", "b5"], [okey])
+        ts(o, T.sa[:, 15::16], -512.0, None, AL.add, None, ["sa"], [okey])
+
+    def pieces(a, n, src, reads, key):
+        hi, lo = T.PT[:, 4 * a:4 * (a + n):4], T.PT[:, 4 * a + 1:4 * (a + n):4]
+        ts(hi, src, M32, -M32, AL.add, AL.add, reads + ["PTz"], [key + "h", "PT"])
+        tt(lo, src, hi, AL.subtract, reads + [key + "h"], [key + "l", "PT"])
+
+    def quant_pt(name, a, n, reads):
+        quant(name, 0, n, T.PT[:, 4 * a:4 * (a + n)], reads)
+        rd.setdefault("PT", {})["ve"] = tick["ve"]
 
     for t in range(R):
-        pc, ls, ll, NL = part(t), T["ls%d" % t], T["ll%d" % t], T["NL%d" % t]
-        lk, X = "ls%d" % t, "x%d" % t
-        places("pb0", [("EG", "pb2"), ("EA", "pb3")], lambda q: consts1(q) if t == 0 else None)
-        if t == 0:
-            consts2()
+        pc, ls, ll, NL = part(t), T["ls%d" % t], T["ll%d" % t], T.NL
+        lk, lr, X = "ls%d" % t, "ll%d" % t, "x%d" % t
+        places("pb0", lambda q: consts_ac(0) if t == 0 and q == -1 else None)
         for pb in ("pb1", "pb7"):
             mm(pb, C, "uu", 128, "rx%d" % t, 0, True, True, ["uuc", "uup", "rx%d" % t])
-        to_list(T.pb2[:, 0:C], "pb2", bc[:, 4:5], 1.0, ls[:, 0:21], lk)
-        cp(T.oW[:].indirect(ls[:, 0:21]), T.ji[:], [lk, "ji"], ["oW"])
-        to_list(T.oW[:], "oW", bc[:, 3:4], 1.0, ls[:, 22:43], lk)
+        sx = T.sx[:, 15::16]
+        ts(ls[:], sx, -float(UP), None, AL.add, None, ["sx"], [lk])
         send(pc, ll[:], ls[:], "la%d" % t, [lk])
-        arrives(["ll%d" % t], "la%d" % t, ne(t))
+        arrives([lr], "la%d" % t, ne(t))
+        ts(T.L0s[:, 0:21], sx, -1.0, 335.0 + UP, AL.mult, AL.add, ["sx"], ["L0s"])
+        act(T.LS[:, 0:21], sx, AF.Identity, ["sx"], ["LSa"], bias=-335.0 - 2 * UP, scale=2.0)
+        dmas("sy", [(T.L0[16 * k:16 * k + 16, 0:21], T.L0s[0:16, 0:21]) for k in range(8)], "l0", ["L0s"], ["L0"])
         if t == 0:
-            sel(eb("ED"), T.W3[:], [[0, 512]], AL.is_ge, 0.0, 111, -1, ["W3"], "EDb")
-            for k in range(8):
-                sel(eb("EP%d" % k), T.W2[:], [[0, 512]], AL.is_equal, 0.0, -16 * k, 1, ["W2"], "EP%db" % k)
-        act(T.va[:], T.pb3[:, 0:C], AF.Copy, ["pb3"], ["va"], scale=512.0)
-        to_list(T.pb3[:, 0:C], "pb3", bc[:, 5:6], -1.0, T.Lg[:, 0:21], "Lg0")
-        tt(T.V0[:], T.va[:], T.JR[:], AL.add, ["va", "JR"], ["V0.0", "V0.1"])
+            consts_gp()
+        for n in range(2):
+            flat(T.XT[:, 4 * C * n:4 * C * (n + 1)], 0, "XTz%d" % n)
+
+        def inverse(q):
+            if q == -1 and t == 0:
+                consts_ac(1)
+            if q == 0:
+                cp(T.oW[:].indirect(ll[:]), T.ji[:], [lr, "ji"], ["oW"])
+                if t == 0:
+                    consts_ve()
+                to_list(T.oW[:], "oW", T.IL[:, 0:21], "IL")
+
+        places("pb1", inverse)
+        IL = T.IL[:, 0:21]
+        tt(T.Bx[:], T.sx[:].indirect(CX), T.de[:], AL.mult, ["sx", "CX", "de"], ["Bx"])
+        act(T.M48[:, 15::16], T.jp[:, 0:48:16], AF.Identity, ["jp", "b21", "M48"], ["M48"], bias=bc[:, 21:22])
         if t == 0:
-            consts3()
-
-        def unpack(q):
-            if q < 4:
-                pb = ("pb4", "pb5", "pb6", "pb0")[q]
-                mm(pb, C, "EU%d" % q, 0, "rx%d" % t, 0, True, True, ["EU00", "rx%d" % t])
-                act(pl("F", q), T[pb][:, 0:C], AF.Copy, [pb], ["F%d" % q])
-
-        places("pb1", [("EG", "pb2")], unpack)
+            quantc("ETp")
+        pieces(0, C, T.Bx[:].indirect(IL), ["Bx", "IL"], "PT")
+        quant_pt("pp", 0, C, ["PTh", "PTl"])
+        mm("pb3", C, "EP0a", 0, "pp", 0, True, False, ["pp0"])
+        mm("pb3", C, "EP0b", 0, "pp", 0, False, True, ["pp0"])
+        mm("pb4", C, "ETp", 0, "pp", 0, True, True, ["pp0"])
+        mm("pb5", C, "ERc", 0, "pp", 0, True, True, ["pp0"])
         if t == 0:
-            for k in (0, 4):
-                quant("EP%d" % k, 0, 512, eb("EP%d" % k, 4), ["EP%db" % (k + i) for i in range(4)])
-        ts(T.hi[:], T.pb2[:, 0:C], MAGIC, -MAGIC, AL.add, AL.add, ["pb2"], ["hi"])
-        tt(T.lo[:], T.pb2[:, 0:C], T.hi[:], AL.subtract, ["pb2", "hi"], ["lo"])
-        act(T.PT[:, 0::4], T.hi[:].indirect(ll[:, 22:43]), AF.Copy, ["hi", "ll%d" % t], ["PT0"])
-        cp(T.PT[:, 1::4], T.lo[:].indirect(ll[:, 22:43]), ["lo", "ll%d" % t], ["PT1"])
-        quant("pp", 0, C, T.PT[:], ["PTz", "PT0", "PT1"])
+            quantc("EX")
+            quantc("EU0")
+        act(T.TT[:, 0:C], T.pb4[:, 0:C], AF.Copy, ["pb4"], ["TTp"])
+        act(T.TT[:, 352:688], T.pb5[:, 0:C], AF.Identity, ["pb5"], ["TTf"], bias=-MID, scale=-1.0)
+        for k in range(1, 8):
+            dmas("sy", [(T.TB[16 * j:16 * j + 16, TW * (k - 1):TW * k], T.TT[16 * k:16 * k + 16, :])
+                        for j in range(7 if t else 8)], "tb%d" % k, ["TTp", "TTf", "TTz"], ["TB%d" % k])
+        tt(T.P0[:], T.nt[:], T.pb3[:, 0:C], AL.subtract, ["pb3", "nt"], ["P0"])
+        tt(T.K1[:, 0:C], T.P0[:].indirect(T.L0[:, 0:21]), T.JR[:], AL.add, ["P0", "L0", "JR"], ["K1"])
+        act(T.G48[:], T.K1[:].indirect(CK), AF.Identity, ["K1", "K1z", "CK"], ["G48"], bias=-2.0 ** 19)
 
-        def table(k):
-            pb = "pb%d" % (4 + k % 4)
-            mm(pb, C, "EP%d" % k, 0, "pp", 0, True, True, ["EP%d0" % (k // 4 * 4), "pp0"])
-            act(pl("P", k), T[pb][:, 0:C], AF.Copy, [pb], ["P%d" % k])
+        def own():
+            scan(T.s48[:], T.G48[:], T.M48[:], 2.0 ** 23, AL.min, AL.add, ["G48", "M48"], ["s48"])
 
         def sort(b):
-            act(pl("G", b), pl("F", b).indirect(ll[:, 22:43]), AF.Copy, ["F%d" % b, "ll%d" % t], ["G%d" % b])
+            act(pl("G", b), pl("F", b).indirect(IL), AF.Copy, ["F%d" % b, "IL"], ["G%d" % b])
 
-        def grow(k):
-            old, new = "V%d" % (k % 2), "V%d" % ((k + 1) % 2)
-            for h in range(2):
-                a, e = HV[h]
-                tt(T[new][:, a:e], pl("P", k).indirect(T.Lg[:, 22 * k + LV[h][0]:22 * k + LV[h][1]]), T[old][:, a:e],
-                   AL.add, ["P%d" % k, "Lg%d.%d" % (k, h) if k else "Lg0", old + ".%d" % h], [new + ".%d" % h])
+        def earlier(k):
+            for pb in VB[(k + 1) % 2]:
+                mm(pb, C, "EK", 0, "xk", 0, True, False, ["xk0"])
+                if k > 4:
+                    mm(pb, C, "EX", 0, "xx", 0, False, False, ["xx0"])
 
-        def hold(k):
-            V = "V%d" % ((k + 1) % 2)
-            for s in range(3):
-                scan(T.SD[:, 112 * s:112 * s + 112], T[V][:, 112 * s:112 * s + 112], T.MD[:], BIG, AL.min, AL.add,
-                     ["MD", V + ".0", V + ".1"][:3 if s else 2], ["SD%d" % s])
-
-        def rows(k):
-            dma("sy", NL[16 * k:16 * k + 16, 0:21], T.Lg[16 * k:16 * k + 16, 22 * k:22 * k + 21], "nl%d" % t, 96,
-                ["Lg%d.0" % k, "Lg%d.1" % k] if k else ["Lg0"], [] if k else ["NLd%d" % t])
-
-        table(0)
-        table(1)
-        grow(0)
-        hold(0)
-        rows(0)
+        own()
         for k in range(1, 8):
-            V = "V%d" % (k % 2)
-            for h, s in ((0, 0), (0, 1), (1, 0)):
-                a, e = HV[h]
-                act(T["CD%d" % h][:, s::4], T[V][:, a:e], AF.Sign, [V + ".%d" % h, "SD%d" % s],
-                    ["CD%d.%d" % (h, s)], bias=T.SD[:, 112 * s + 111:112 * s + 112], scale=-1.0)
-            if k < 7:
-                table(k + 1)
-            if 2 <= k < 6:
-                sort(k - 2)
-
-            def beats(h, s, two):
-                a, e = HV[h]
-                ts(T["CD%d" % h][:, s::4], T[V][:, a:e], T.SD[:, 112 * s + 111:112 * s + 112], two, AL.is_lt,
-                   AL.mult if two else None, [V + ".%d" % h, "SD%d" % s], ["CD%d.%d" % (h, s)])
-
-            beats(1, 1, 2.0)
-            beats(0, 2, None)
-            beats(1, 2, None)
-            for h in range(2):
-                n = HV[h][1] - HV[h][0]
-                quant("cd%d" % h, 0, n, T["CD%d" % h][:], ["CD%d.%d" % (h, s) for s in range(3)] + ["CD%dz" % h])
-                mm("pb%d" % h, n, "ED", 0, "cd%d" % h, 0, True, True, ["ED0", "cd%d0" % h])
-            for h in range(2):
-                a, e = HV[h]
-                scan(T.sc[:, a:e], T["pb%d" % h][:, 0:e - a], T.MNd[:, a:e], 4096.0, AL.min, AL.add,
-                     ["pb%d" % h, "MNd"], ["sc%d" % h])
+            w = SW * (k - 1)
+            sk = "SM%d" % k
+            va, vb = VB[k % 2]
+            V, vk = (T.K1[:, 0:C], "K1") if k == 1 else (T[va][:, 0:C], va)
+            if 1 < k < 7:
+                earlier(k)
+            if k < 5:
+                mm("pb%d" % (3 + k % 3), C, "EU%d" % (k - 1), 0, "rx%d" % t, 0, True, True, ["rx%d" % t])
+            for s in (1, 2, 0)[:3 if k == 1 else 2]:
+                c = w + S0 + s
+                act(pl("jk", s), V, AF.Sign, [vk, "s48"], [sk + ".%d" % s], bias=T.s48[:, 16 * s + 15:16 * s + 16],
+                    scale=-1.0, accum_out=T.SM[:, c:c + 1])
+            if k == 1:
+                ts(T.y1[:], V, bc[:, 14:15], bc[:, 14:15], AL.add, AL.subtract, ["K1", "pc"], ["y1"])
+                ts(T.y2[:], V, bc[:, 13:14], bc[:, 13:14], AL.add, AL.subtract, ["K1", "pc"], ["y2"])
+                ts(T.M48[:, 15::16], T.s48[:, 15::16], bc[:, 7:8], None, AL.add, None, ["s48", "b7"], ["M48"])
+                tt(T.PT[:, 0::4], T.y1[:], T.y2[:], AL.subtract, ["y1", "y2"], ["XK", "PT"])
+            else:
+                ts(T.M48[:, 15::16], T.s48[:, 15::16], bc[:, 7:8], None, AL.add, None, ["s48", "b7"], ["M48"])
+                ts(T.CB[:], T[vb][:, 0:C], T.s48[:, 15:16], 2.0, AL.is_lt, AL.mult, [vb, "s48"], ["CBk"])
+                scan(T.SM[:, w + 8:w + S0 + 1], T.CB[:, 0:168], T.CB[:, 168:C], -335.0, AL.add, AL.add, ["CBk"],
+                     [sk + ".0"])
             if k == 7:
-                tt(T.x7[96:128, 0:21], T.sc[96:128, 15::16], T.x6[96:128, 0:21], AL.max, ["sc0", "sc1", "x6"], ["x7"])
-                ts(NL[96:128, 0:21], T.x7[96:128, 0:21], bc[96:128, 12:13], None, AL.add, None, ["x7", "b7"],
-                   ["NL%d" % t])
-            if k < 7 or t == R - 1:
-                for h in range(2):
-                    a, e = HV[h]
-                    ts(T.Lg[:, 22 * k + LV[h][0]:22 * k + LV[h][1]], T.sc[:, a + 15:e:16], bc[:, 3:4], None, AL.add,
-                       None, ["sc%d" % h, "bn"], ["Lg%d.%d" % (k, h)])
+                break
+            sr = [sk + ".%d" % s for s in range(3)] + ["SMc"]
+            ts(T.OF[:], T.SM[:, w:w + SW].indirect(CW), -0.5, 167.5, AL.mult, AL.add, sr + ["CW"], ["OF"])
+            if k == 1:
+                quant_pt("xk", 0, C, ["XK"])
+                earlier(k)
+            o, tk = TW * (k - 1), ["TB%d" % k]
+            n, e = divmod(k - 1, 4)
+            a, z = 4 * C * n, "XTz%d" % n
+            cp(T.XT[:, a + e + 640:a + 4 * C:4], T.TB[:, o:o + 352].indirect(T.OF[:, 10:21]), ["OF", z] + tk, ["XT1"])
+            act(T.XT[:, a + e:a + 640:4], T.TB[:, o:o + 352].indirect(T.OF[:, 0:10]), AF.Copy, ["OF", z] + tk, ["XT0"])
+            act(T.G48[:], T.TB[:, o + 352:o + TW].indirect(T.OF[:, 32:35]), AF.Identity, ["OF"] + tk, ["G48"],
+                bias=MID * KEY, scale=KEY)
+            quant("xx", C * n, C * n + C, T.XT[:, a:a + 4 * C], ["XT0", "XT1", z])
+            for pb in VB[(k + 1) % 2]:
+                mm(pb, C, "EX", 0, "xx", C * n, False, True, ["xx%d" % (C * n)])
+            own()
+            if k < 5:
+                pb = "pb%d" % (3 + k % 3)
+                act(pl("F", k - 1), T[pb][:, 0:C], AF.Copy, [pb], ["F%d" % (k - 1)])
+            if k in (3, 4, 5, 6):
+                sort(k - 3)
+            if k == 2 and t == 0:
+                consts_ac(2)
+            if k == 4 and t == 0:
+                quantc("EL")
+            if k == 5:
+                pieces(0, 160, T.SM[:, 0:5 * SW].indirect(CB),
+                       ["SM%d.%d" % (a, s) for a in range(1, 6) for s in range(3)] + ["CB"], "LT")
             if k == 6:
-                ts(T.x6[96:128, 0:21], T.sc[96:128, 15::16], bc[96:128, 9:10], bc[96:128, 11:12], AL.mult, AL.add,
-                   ["sc0", "sc1", "m6", "c6"], ["x6"])
-            if k < 7:
-                grow(k)
-                hold(k)
-            if k < 6:
-                rows(k)
-        zk = ["NL%d" % t, "NLd%d" % t]
+                quant_pt("lt", 0, 160, ["LTh", "LTl"])
+                mm("pb2", 160, "EL", 0, "lt", 0, True, True, ["lt0"])
+        pieces(160, 64, T.SM[:].indirect(CF), ["SM%d.%d" % (a, s) for a in (6, 7) for s in range(3)] + ["CB"], "LF")
+        act(T.LS[:, 32:192], T.pb2[:, 0:160], AF.Copy, ["pb2"], ["LSb"])
+        if t == R - 1:
+            act(T.Vs[:], T[VB[1][0]][:, 0:C], AF.Copy, [VB[1][0]], ["Vs"])
+        quant_pt("lf", 160, 128, ["LFh", "LFl"])
+        mm("pb3", 128, "EL", 0, "lf", 0, True, True, ["lf0"])
+        cp(T.LS[:, 192:256], T.pb3[:, 0:64], ["pb3"], ["LSc"])
+        ts(NL[:], T.LS[:].indirect(CP), -0.5, 167.5, AL.mult, AL.add, ["LS0", "LSa", "LSb", "LSc", "CP"], ["NL"])
+        zk = ["NL"]
         for h in range(2):
             a, e = HV[h]
             x, y = LV[h]
@@ -447,43 +549,42 @@ def rank_program(g, core, T, topo):
         def best(h):
             a, e = HV[h]
             for b in range(4):
-                m = T.ym[:, 176 * b:176 * b + e - a]
-                tt(m, T["pb%d" % (2 * b)][:, 0:e - a], T.yt[:, 176 * b:176 * b + e - a], AL.max,
-                   ["pb%d" % (2 * b), "yt%d" % b], ["ym%d" % b])
-                act(pl("Y", b, a, e), m, AF.Copy, ["ym%d" % b], ["Y%d.%d" % (b, h)], scale=0.03125)
+                tt(pl("Ym", b, a, e), T["pb%d" % (2 * b)][:, 0:e - a], T.yt[:, 176 * b:176 * b + e - a], AL.max,
+                   ["pb%d" % (2 * b), "yt%d" % b], ["Y%d.%d" % (b, h)])
 
         layer(0)
         cp(T.iW[:].indirect(NL[:, 0:21]), T.ji[:], ["ji"] + zk, ["iW"])
         best(0)
+        act(T.tm[:], T.iW[:].indirect(ll[:]), AF.Copy, ["iW", lr], ["tm"])
         layer(1)
-        cp(T.tm[:], T.iW[:].indirect(ll[:, 0:21]), ["iW", "ll%d" % t], ["tm"])
-        to_list(T.tm[:], "tm", bc[:, 3:4], 1.0, T.ML[:, 0:21], "ML")
+        to_list(T.tm[:], "tm", T.ML[:, 0:21], "ML")
         best(1)
         for h in range(2):
             a, e = HV[h]
             x, y = LV[h]
             for b in range(4):
-                o, i = T.Yp[:, 4 * a + b:4 * e:4], pl("Y", b).indirect(T.ML[:, x:y])
+                o, i = T.Yp[:, 4 * a + b:4 * e:4], pl("Ym", b).indirect(T.ML[:, x:y])
                 rk = ["ML", "Y%d.0" % b, "Y%d.1" % b]
-                if b < 3 - h:
-                    cp(o, i, rk, ["Yp%d.%d" % (h, b)])
+                if b >= 2:
+                    ts(o, i, 0.03125, None, AL.mult, None, rk, ["Yp%d.%d" % (h, b)])
                 else:
-                    act(o, i, AF.Copy, rk, ["Yp%d.%d" % (h, b)])
+                    act(o, i, AF.Copy, rk, ["Yp%d.%d" % (h, b)], scale=0.03125)
             quant("y%d" % t, a, e, T.Yp[:, 4 * a:4 * e], ["Yp%d.%d" % (h, b) for b in range(4)])
-            k, sm = ["y%d%d" % (t, a)], ("ya%d", "yb%d")[h] % t
-            send(pc, T["ry%dq" % t][:, a:e].bitcast(dt.uint8), T["y%dq" % t][:, a:e].bitcast(dt.uint8), sm, k)
-            send(pc, T["ry%ds" % t][:, a:e], T["y%ds" % t][:, a:e], sm, k)
-            arrives(["ry%d.%d" % (t, h)], sm, 2 * ne(t))
+            k, sem = ["y%d%d" % (t, a)], ("ya%d", "yb%d")[h] % t
+            send(pc, T["ry%dq" % t][:, a:e].bitcast(dt.uint8), T["y%dq" % t][:, a:e].bitcast(dt.uint8), sem, k)
+            send(pc, T["ry%ds" % t][:, a:e], T["y%ds" % t][:, a:e], sem, k)
+            arrives(["ry%d.%d" % (t, h)], sem, 2 * ne(t))
         for h in range(2):
             a, e = HV[h]
             for b in range(4):
-                mm("pb%d" % (4 * h + b), e - a, "EU%d" % b, 0, X, a, True, False, ["EU00", X + "0", X + "160"])
+                mm("pb%d" % (4 * h + b), e - a, "EU%d" % b, 0, X, a, True, False, [X + "0", X + "160"])
         if t == R - 1:
-            grow(7)
-            tt(T.tb[0:1, :], T.V0[0:1, :], T.JR[0:1, :], AL.subtract, ["V0.0", "V0.1", "JR"], ["tb"])
-            ts(T.tb[0:1, :], T.tb[0:1, :], 2.0 ** -9, 9.0 * OFF, AL.mult, AL.add, ["tb"], ["tb"])
-            dma("sy", T.tot[:], T.tb[0:1, :], "out", 0, ["tb"], [])
+            tt(T.tb[:], T.Vs[:], T.JR[:], AL.subtract, ["Vs", "JR"], ["tb"])
             quant("v", 0, 128, T.vin[:], ["vin"])
+            ts(T.tb[:], T.tb[:], 1.0 / KEY, M1, AL.mult, AL.add, ["tb"], ["tb"])
+            ts(T.tb[:], T.tb[:], -M1, 335.0 + MID - 8 * UP, AL.add, AL.add, ["tb"], ["tb"])
+            tt(T.Vs[:], T.TT[:, 352:TW].indirect(NL[:, 0:21]), T.tb[:], AL.add, ["tb", "TTf", "TTz", "NL"], ["Vs"])
+            dmas("sy", [(T.tot[:], T.Vs[112:113, :])], "out", ["Vs"])
         N, xt = "x%d" % (t + 1), T["xt%d" % t]
         for h in range(2):
             a, e = HV[h]
@@ -491,22 +592,21 @@ def rank_program(g, core, T, topo):
                 pb = "pb%d" % (4 * h + b)
                 mm(pb, e - a, "EU%d" % b, 0, "ry%d" % t, a, False, True, ["ry%d.%d" % (t, h)])
                 o = xt[:, 4 * a + b:4 * e:4]
-                if b > 0:
+                if b % 2:
                     cp(o, T[pb][:, 0:e - a], [pb], ["xt%d.%d" % (h, b)])
                 else:
                     act(o, T[pb][:, 0:e - a], AF.Copy, [pb], ["xt%d.%d" % (h, b)])
             quant(N, a, e, xt[:, 4 * a:4 * e], ["xt%d.%d" % (h, b) for b in range(4)])
         if t < R - 1:
-            send_x(t + 1)
             for pb in ("pb0", "pb7"):
                 mm(pb, C, "uu", 0, N, 0, True, True, [N + "0", N + "160"])
+            send_x(t + 1)
     nk = ["x20", "x2160"]
     mm("pb0", C, "v", 0, "x2", 0, True, True, ["v0"] + nk)
-    dma("sy", T.oc[:], T.x2q[:].bitcast(dt.uint8), "out", 0, nk, [])
+    dmas("sy", [(T.oc[:], T.x2q[:].bitcast(dt.uint8))], "out", nk)
     act(T.ysb[:], T.pb0[:, 0:C], AF.Copy, ["pb0"], ["ysb"])
-    for k in range(4):
-        dma("sy", T.osc[4 * k:4 * k + 4, :], T.x2s[32 * k:32 * k + 4, :], "out", 0, nk, [])
-    dma("ac", T.y[:], T.ysb[:], "out", 0, ["ysb"], [])
+    dmas("sy", [(T.osc[4 * k:4 * k + 4, :], T.x2s[32 * k:32 * k + 4, :]) for k in range(4)], "out", nk)
+    dmas("ac", [(T.y[:], T.ysb[:])], "out", ["ysb"])
     for s in tick:
         g.wait_ge(T.sem[s], tick[s])
     for s in dcount:

@@ -12,12 +12,12 @@ KEY = 385.0
 BASE = float(2 ** 18)
 UP = 128
 MID = 168.0 + UP
-SW, TW = 184, 704
-S0 = 175
-TILES = [(("d", 13, 12, 11), 336, "ERc"), ((10, 9, 8, 7), 160, "ERc"), ((6, 5), 128, "ERc"),
-         ((20, 19, 18, 17), 320, "ERb"), ((16, 15, 14, 1), 256, "ERb"), ((4, 3, 2), 128, "ERb")]
-ON_ACT = [20, 19, 18, 17, 16, 15, 14, 1, 4, 3, 2]
-ON_VE = range(13, 4, -1)
+SW, TW = 192, 704
+CELL = (0, 183, 184)
+TILES = [(("d", 13, 12, 11), 336, "ERc"), ((10, 9, 8, 7), 160, "ERc"), ((6, 5, 4, 3), 128, "ERc"),
+         ((2, 1), 128, "ERc"), ((20, 19, 18, 17), 320, "ERb"), ((16, 15, 14), 256, "ERb")]
+ON_ACT = range(20, 13, -1)
+ON_VE = range(13, 0, -1)
 
 SCRATCH = {}
 
@@ -41,14 +41,14 @@ for _n in ("uin", "vin", "ones", "W1"):
     _s(_n, 512, "bfloat16")
 _s("Eb", 512 * len(CONST), "bfloat16")
 _q("E", 128 * len(CONST))
-_s("yt", 4 * 176)
+_s("yt", 4 * C)
 _s("Ym", 4 * C)
 _s("TT", TW, "bfloat16")
 _s("TB", 7 * TW, "bfloat16")
 _s("SM", 7 * SW)
 _s("J", 21 * 112)
 _s("LS", 256)
-_s("K1", 384)
+_s("JR", C)
 for _k in range(8):
     _s("pb%d" % _k, 512, "float32", "psum")
 for _n, _k in (("u", 128), ("v", 128), ("uu", 256), ("wl", 1024), ("z", C), ("pp", C), ("xx", 2 * C), ("xk", C),
@@ -63,13 +63,13 @@ for _t in range(R):
     _s("ll%d" % _t, 21, "uint16")
 for _t in range(R + 1):
     _q("x%d" % _t, C)
-for _n in ("jp", "ji", "d", "de", "k1", "JR", "nt", "MN", "MNx", "MH", "RH", "t1", "Hd", "sa", "sx", "oW", "iW",
+for _n in ("jp", "ji", "d", "de", "k1", "K1", "nt", "MN", "MNx", "MH", "RH", "t1", "Hpb0", "Hpb1", "sa", "sx", "oW", "iW",
            "tm", "tb", "Bx", "P0", "y1", "y2", "Vs", "df0", "df1", "ysb"):
     _s(_n, C)
 for _n in ("rm", "DS", "CB"):
     _s(_n, C, "bfloat16")
 _s("jk", 3 * C, "bfloat16")
-for _n in ("M48", "G48", "s48"):
+for _n in ("M48", "G48", "s48", "J48"):
     _s(_n, 48)
 _s("sm", 128)
 _s("pI", 128, "int32")
@@ -77,8 +77,11 @@ _s("CL", 64, "uint16")
 _s("oU", 16, "uint16")
 _s("OF", 48, "uint16")
 _s("NL", 32, "uint16")
-for _n in ("ML", "IL", "L0s", "L0"):
+for _n in ("ML", "IL"):
     _s(_n, 22, "uint16")
+_s("L0", 48, "uint16")
+_s("L0s", 24)
+_s("L0f", 24)
 _s("bc", 32)
 
 SEMAPHORES = ["ve", "ac", "pe", "gp", "lx", "lu", "lv", "lw", "lz", "out", "loc", "l0"]
@@ -209,7 +212,8 @@ def rank_program(g, core, T, topo):
     dmas("sy", [(T.wls[:], T.ws[:])], "lz", (), ["wsc"])
     f32 = dict(allow_small_or_imprecise_dtypes=True)
     bc, sm, pI, CL = T.bc, T.sm, T.pI, T.CL
-    CX, CW, CK, CP, CB, CF = CL[:, 0:21], CL[:, 22:25], CL[:, 26:29], CL[:, 30:32], CL[:, 32:42], CL[:, 42:46]
+    CX, CWa, CWb, CC = CL[:, 0:21], CL[:, 22:23], CL[:, 24:26], CL[:, 26:27]
+    CP, CB, CF = CL[:, 30:32], CL[:, 32:42], CL[:, 42:46]
     MC, X2 = sm[:, 8:29], sm[:, 32:53]
     start, slot, o = {}, {}, 0
     for q, (blocks, w, _e) in enumerate(TILES):
@@ -260,46 +264,43 @@ def rank_program(g, core, T, topo):
         mm(pb, C, "uu", 0, "x0", 0, True, True, ["uuc", "uup", "x00"])
     act(eb("ERb"), eb("ERc"), AF.Copy, ["ERcb"], ["ERbb"], scale=0.5)
     act(T.MNx[:], T.k1[:], AF.Identity, ["k1"], ["MNx"], bias=-3072.0)
-    act(bc[:, 2:3], T.de[:, 15:16], AF.Identity, ["de", "i"], ["b2"], bias=bc[:, 0:1], scale=-1024.0)
-    for a, e, step, base in ((0, 5, 0, 232), (5, 14, -16, 264 - 80), (14, 21, 0, 160)):
+    ts(bc[:, 2:3], T.de[:, 15:16], -1024.0, bc[:, 0:1], AL.mult, AL.add, ["de", "i"], ["b2"])
+    for a, e, step, base in ((0, 14, -16, 264), (14, 21, 0, 160)):
         iota(sm[:, 64 + a:64 + e], [[step, e - a]], base + UP + 1024, 0, "c15", **f32)
     flat(T.J[:, 111:112], 0, "J0")
-    act(MC, sm[:, 64:85], AF.Identity, ["c15", "b2"], ["MC"], bias=bc[:, 2:3])
+    ts(MC, sm[:, 64:85], bc[:, 2:3], None, AL.add, None, ["c15", "b2"], ["MC"])
     quantc("ERc")
     send_x(0)
     iota(T.ji[:], [[1, C]], 0, 0, "ji", **f32)
     iota(pI[:, 32:53], [[16, 21]], 15, 0, "CXi")
-    iota(pI[:, 64:80], [[0, 8], [16, 2]], 0, 0, "e16")
-    iota(pI[:, 80:94], [[SW, 7], [0, 2]], S0, 0, "w14")
-    iota(sm[:, 88:91], [[16, 3]], 0, 3, "k3", **f32)
-    iota(sm[:, 92:94], [[16, 2]], 0, 2, "p2", **f32)
-    for b in range(4):
-        sel(eb("EU%d" % b), T.ones[:], [[1, 512]], AL.is_equal, 0.0, -b, -4, ["ones"], "EU%db" % b)
+    flat(T.L0s[:, 21:24], 0, "L0z")
+    flat(bc[:, 13:15], 0, "pc")
+    sel(eb("EP0b"), T.W1[:], [[0, 512]], AL.is_ge, 0.0, 15, -1, ["W1"], "EP0bb")
+    for k, (pat, base, big) in enumerate(((-1, 1, 1.5 * 2.0 ** 43), (1, -14, 1.5 * 2.0 ** 38), (0, 0, 1.5 * 2.0 ** 33),
+                                          (0, 0, M32))):
+        sel(bc[:, 13:15], bc[:, 13:15], [[8, 2]], AL.not_equal, big, -8 * k, 1, ["pc"], "pc")
+        sel(eb("ETp", 1, k, 4), eb("ERc", 1, k, 4), [[0, 8], [pat, 16]], AL.is_ge, 0.0, base, 0, ["ERcb"], "ETpb")
+    iota(T.nt[:], [[-int(KEY), C]], 0, 0, "nt", **f32)
 
     def consts_gp():
-        sel(eb("EP0b"), T.W1[:], [[0, 512]], AL.is_ge, 0.0, 15, -1, ["W1"], "EP0bb")
         flat(T.PT[:], 0, "PTz")
-        iota(T.nt[:], [[-int(KEY), C]], 0, 0, "nt", **f32)
         iota(T.JR[:], [[-1, C]], int(BASE) + 335, 0, "JR", **f32)
-        for ap, val, key in ((T.K1[:, C:384], 0, "K1z"), (T.TT[:, C:352], 0, "TTz"), (T.TT[:, 688:TW], 0, "TTz"),
-                             (T.SM[:, S0 + 3::SW], -337, "SMc"), (T.SM[:, S0 + 4::SW], 0, "SMc"),
-                             (T.LS[:, 21:32], 0, "LS0"), (bc[:, 13:15], 0, "pc")):
+        iota(T.J48[:, 0:32], [[-128, 2], [0, 16]], int(BASE) + 335 - 2 ** 19, -1, "J48", **f32)
+        iota(T.J48[:, 32:48], [[0, 16]], int(BASE) + 335 - 2 ** 19 - 240, -1, "J48", **f32)
+        for ap, val, key in ((T.TT[:, C:352], 0, "TTz"), (T.TT[:, 688:TW], 0, "TTz"),
+                             (T.SM[:, 1::SW], -337, "SMc"), (T.SM[:, 2::SW], 0, "SMc"),
+                             (T.LS[:, 21:32], 0, "LS0")):
             flat(ap, val, key)
-        for j, big in enumerate((1.5 * 2.0 ** 43, 1.5 * 2.0 ** 38, 1.5 * 2.0 ** 33, M32)):
-            sel(bc[:, 13:15], bc[:, 13:15], [[8, 2]], AL.not_equal, big, -8 * j, 1, ["pc"], "pc")
+        iota(sm[:, 92:94], [[16, 2]], 0, 2, "p2", **f32)
+        iota(sm[:, 94:96], [[16, 2]], 0, 0, "h2", **f32)
+        iota(sm[:, 104:111], [[SW, 7]], 2, 0, "w7", **f32)
 
     def consts_ac(q):
         if q == 0:
             act(T.MN[:], T.k1[:], AF.Identity, ["k1"], ["MN"], bias=-3072.0)
-            act(T.M48[:], T.MN[:, 0:48], AF.Copy, ["MN"], ["M48"], scale=2048.0)
-            act(T.MN[:, 15::16], T.MN[:, 15::16], AF.Identity, ["MN"], ["MN"], bias=1536.0)
-            act(eb("ETp"), eb("ERc"), AF.Copy, ["ERcb"], ["ETpb"], scale=-1.0)
-            sel(eb("ETp", 1, 0, 4), eb("ETp", 1, 0, 4), [[0, 8], [-1, 16]], AL.is_ge, 0.0, 1, 0, ["ETpb"], "ETpb")
-            sel(eb("ETp", 1, 1, 4), eb("ETp", 1, 1, 4), [[0, 8], [1, 16]], AL.is_ge, 0.0, -14, 0, ["ETpb"], "ETpb")
         if q == 1:
+            act(T.M48[:], T.k1[:, 0:48], AF.Identity, ["k1"], ["M48"], bias=-3072.0 * 2048, scale=2048.0)
             act(eb("EP0a"), eb("EP0b"), AF.Copy, ["EP0bb"], ["EP0ab"], scale=KEY - 1)
-            act(bc[:, 7:8], T.de[:, 15:16], AF.Identity, ["de"], ["b7"], bias=2.0 ** 21, scale=-2.0 ** 21)
-            act(bc[:, 21:22], bc[:, 7:8], AF.Identity, ["b7"], ["b21"], bias=2.0 ** 19)
             act(bc[:, 16:18], T.de[:, 0:15:14], AF.Copy, ["de"], ["b8"], scale=KEY - 1, accum_out=bc[:, 8:9])
             act(bc[:, 18:20], T.de[:, 1:16:14], AF.Copy, ["de"], ["b9"], accum_out=bc[:, 9:10])
             act(bc[:, 26:27], bc[:, 13:14], AF.Sign, ["pc"], ["b26"])
@@ -307,51 +308,63 @@ def rank_program(g, core, T, topo):
             act(eb("EK"), T.ones[:], AF.Copy, ["ones", "b26"], ["EKb"], scale=bc[:, 26:27])
             act(eb("EX"), T.ones[:], AF.Copy, ["ones", "b8"], ["EXb"], scale=bc[:, 8:9])
             act(eb("EK", 1, 1, 4), T.ones[:, 0:128], AF.Copy, ["ones", "EKb"], ["EKb"], scale=0.0)
+
+    def consts_ve(q):
+        i, gr = bc[:, 0:1], bc[:, 1:2]
+        if q == 0:
+            ts(bc[:, 3:4], i, gr, None, AL.subtract, None, ["i"], ["b3"])
+            cp(CX, pI[:, 32:53], ["CXi"], ["CX"])
+            ts(T.MN[:, 15::16], T.MN[:, 15::16], 1536.0, None, AL.add, None, ["MN"], ["MN"])
+            ts(bc[:, 4:5], bc[:, 3:4], 0.0, CELL[1] - 1.0, AL.is_equal, AL.mult, ["b3"], ["b4"])
+            ts(bc[:, 5:6], bc[:, 3:4], 8.0, CELL[2] - 1.0, AL.is_equal, AL.mult, ["b3"], ["b5"])
+            ts(bc[:, 6:7], i, 8.0, 15.0, AL.mult, AL.min, ["i"], ["b6"])
+            ts(bc[:, 7:8], T.de[:, 15:16], -2.0 ** 21, 2.0 ** 21, AL.mult, AL.add, ["de"], ["b7"])
+            ts(bc[:, 21:22], T.de[:, 15:16], -2.0 ** 21, 2.0 ** 21 + 2.0 ** 19, AL.mult, AL.add, ["de"], ["b21"])
+            ts(CWa, bc[:, 3:4], 0.0, None, AL.not_equal, None, ["b3"], ["CW"])
+            ts(CL[:, 24:25], bc[:, 5:6], bc[:, 4:5], 1.0, AL.add, AL.add, ["b4", "b5"], ["CW"])
+            ts(CL[:, 25:26], i, float(CELL[1]), float(CELL[2]), AL.mult, AL.min, ["i"], ["CW"])
+            ts(CC, bc[:, 6:7], gr, None, AL.add, None, ["b6", "i"], ["CC"])
+        e, m = sm[:, 88:90], [sm[:, 96 + 2 * s:98 + 2 * s] for s in range(3)]
+        if q == 1:
+            ts(e, sm[:, 94:96], bc[:, 3:4], None, AL.add, None, ["h2", "b3"], ["e"])
+            ts(bc[:, 10:11], gr, 7.0, CELL[1] - 2.0, AL.is_lt, AL.mult, ["i"], ["b10"])
+            ts(CP, sm[:, 92:94], i, None, AL.subtract, None, ["p2", "i"], ["CP"])
+            for s, (val, w) in enumerate(((0.0, -2.0), (8.0, bc[:, 10:11]), (15.0, CELL[2] - 2.0))):
+                ts(m[s], e, val, w, AL.is_equal, AL.mult, ["e", "b10"], ["m%d" % s])
         if q == 2:
-            for k in range(4):
-                act(eb("EL", 1, k, 4), T.de[:, 0:128], AF.Copy, ["de"], ["ELb"])
+            tt(m[0], m[0], m[2], AL.add, ["m0", "m2"], ["m0"])
+            tt(m[0], m[0], m[1], AL.add, ["m0", "m1"], ["m0"])
+            for h in range(2):
+                ts(CL[:, 32 + h:46:2], sm[:, 104:111], sm[:, 96 + h:97 + h], None, AL.add, None, ["w7", "m0"], ["CB"])
 
-    def consts_ve():
-        v, z = pI[:, 64:80], pI[:, 96:110]
-        ts(bc[:, 3:4], bc[:, 1:2], -3.0, bc[:, 0:1], AL.mult, AL.add, ["i"], ["b3"])
-        cp(CX, pI[:, 32:53], ["CXi"], ["CX"])
-        ts(v, v, bc[:, 3:4], None, AL.add, None, ["e16", "b3"], ["e16"])
-        ts(CK, sm[:, 88:91], bc[:, 0:1], bc[:, 0:1], AL.subtract, AL.subtract, ["k3", "i"], ["CK"])
-        ts(v, v, 63, None, AL.bitwise_and, None, ["e16"], ["e16"])
-        ts(CP, sm[:, 92:94], bc[:, 0:1], None, AL.subtract, None, ["p2", "i"], ["CP"])
-        ts(z, pI[:, 64:78], 3.0, 1.2, AL.min, AL.mult, ["e16"], ["z14"])
-        ts(CL[:, 22:24], pI[:, 64:66], 3.0, float(S0), AL.min, AL.add, ["e16"], ["CW"])
-        ts(CL[:, 24:25], bc[:, 0:1], 3.0, float(S0), AL.min, AL.add, ["i"], ["CW"])
-        tt(z, z, pI[:, 80:94], AL.add, ["z14", "w14"], ["z14"])
-        cp(CL[:, 32:46], z, ["z14"], ["CB"])
+    def cells(c, a, e):
+        return T.RT[:, slot[c] + 4 * a:slot[c] + 4 * e - 3:4]
 
-    def places(bank, hook):
-        S = T[bank]
-        for a, e, k in ((224, C, "h"), (0, 224, "l")):
+    def held(bank):
+        S, H = T[bank], "H" + bank
+        parts = ((224, C, "h"), (0, 224, "l"))
+        for a, e, k in parts:
             tt(T.t1[:, a:e], S[:, a:e], T.MH[:, a:e], AL.max, [bank, "MH"], ["t1" + k])
-            scan(T.Hd[:, a:e], T.RH[:, a:e], T.t1[:, a:e], INF, AL.max, AL.min, ["RH", "t1" + k], ["Hd" + k])
+        for a, e, k in parts:
+            scan(T[H][:, a:e], T.RH[:, a:e], T.t1[:, a:e], INF, AL.max, AL.min, ["RH", "t1" + k], [H + k])
+        for a, e, k in parts:
+            tt(cells("d", a, e), S[:, a:e], T[H][:, a:e], AL.is_gt, [bank, H + k] + zs, ["RT.d"])
 
-        def cells(c, a, e):
-            return T.RT[:, slot[c] + 4 * a:slot[c] + 4 * e - 3:4]
+    def places(bank, twin, hook):
+        S, H = T[bank], "H" + bank
 
         def diff(n):
             c = ON_ACT[n]
-            act(T["df%d" % (n % 2)][:, 0:16 * c], T.pb7[:, 0:16 * c], AF.Identity,
-                ["pb7", "Hdh" if c > 13 else "Hdl"], ["df%d" % (n % 2)], bias=T.Hd[:, 16 * c + 15:16 * c + 16],
-                scale=-1.0)
+            act(T["df%d" % (n % 2)][:, 0:16 * c], T[twin][:, 0:16 * c], AF.Identity, [twin, H + "h"],
+                ["df%d" % (n % 2)], bias=T[H][:, 16 * c + 15:16 * c + 16], scale=-1.0)
 
         diff(0)
         for n, c in enumerate(ON_ACT):
             if n + 1 < len(ON_ACT):
                 diff(n + 1)
             act(cells(c, 0, 16 * c), T["df%d" % (n % 2)][:, 0:16 * c], AF.Sign, ["df%d" % (n % 2), "tiny"] + zs,
-                ["RT.%s" % c, "J%d" % c], bias=bc[:, 25:26], scale=-1.0,
-                accum_out=T.J[:, 112 * c + 111:112 * c + 112])
-            if c in (14, 2):
-                a, e = (14, 21) if c == 14 else (1, 5)
-                v = T.J[:, 112 * a + 111:112 * e:112]
-                jk = ["J%d" % j for j in range(a, e)]
-                act(v, v, AF.Copy, jk, jk, scale=0.5)
+                ["RT.%s" % c, "AC"], bias=bc[:, 25:26], scale=-1.0, accum_out=sm[:, c - 14:c - 13])
+        act(T.J[:, 112 * 14 + 111::112], sm[:, 0:7], AF.Copy, ["AC"], ["J%d" % c for c in ON_ACT], scale=0.5)
         hook(-1)
 
         def count(q):
@@ -364,22 +377,21 @@ def rank_program(g, core, T, topo):
             scan(T.J[:, 112 * c + 112 - 8 * c:112 * c + 112], cells(c, 0, 8 * c), cells(c, 8 * c, 16 * c), 0.0,
                  AL.add, AL.add, ["RT.%s" % c], ["J%d" % c])
 
-        tt(cells("d", 0, C), S[:, 0:C], T.Hd[:], AL.is_gt, [bank, "Hdh", "Hdl"] + zs, ["RT.d"])
         for c in ON_VE:
-            ts(cells(c, 0, 16 * c), S[:, 0:16 * c], T.Hd[:, 16 * c + 15:16 * c + 16], None, AL.is_ge, None,
-               [bank, "Hdl"] + zs, ["RT.%s" % c])
+            ts(cells(c, 0, 16 * c), S[:, 0:16 * c], T[H][:, 16 * c + 15:16 * c + 16], None, AL.is_ge, None,
+               [bank, H + "l"] + zs, ["RT.%s" % c])
             if c == 13:
                 scan(T.DS[:], T.rm[:], cells("d", 0, C), 0.0, AL.mult, AL.add, ["rm", "RT.d"], ["DS"])
             else:
                 sums(c + 1)
-            if c in (10, 6):
-                count({10: 0, 6: 1}[c])
+            if c in (10, 6, 2):
+                count({10: 0, 6: 1, 2: 2}[c])
+        hook(1)
+        count(4)
+        sums(1)
         count(3)
-        sums(5)
-        count(2)
         tt(X2, T.DS[:, 15::16], MC, AL.add, ["DS", "MC"], ["X2"])
         hook(0)
-        count(4)
         count(5)
         tt(T.MNx[:, 15::16], T.J[:, 111::112], X2, AL.add, ["X2"] + ["J%d" % c for c in range(21)], ["MNx"])
         scan(T.sx[:], T.pb2[:, 0:C], T.MNx[:], 4096.0, AL.min, AL.add, ["pb2", "MNx"], ["sx"])
@@ -388,77 +400,114 @@ def rank_program(g, core, T, topo):
         scan(T.sa[:], src, T.MN[:], 4096.0, AL.min, AL.add, [key, "MN"], ["sa"])
         ts(o, T.sa[:, 15::16], -512.0, None, AL.add, None, ["sa"], [okey])
 
-    def pieces(a, n, src, reads, key):
+    def piece(j, a, n, src, reads, key):
         hi, lo = T.PT[:, 4 * a:4 * (a + n):4], T.PT[:, 4 * a + 1:4 * (a + n):4]
-        ts(hi, src, M32, -M32, AL.add, AL.add, reads + ["PTz"], [key + "h", "PT"])
-        tt(lo, src, hi, AL.subtract, reads + [key + "h"], [key + "l", "PT"])
+        if j == 0:
+            ts(hi, src, M32, -M32, AL.add, AL.add, reads + ["PTz"], [key + "h", "PT"])
+        else:
+            tt(lo, src, hi, AL.subtract, reads + [key + "h"], [key + "l", "PT"])
 
-    def quant_pt(name, a, n, reads):
-        quant(name, 0, n, T.PT[:, 4 * a:4 * (a + n)], reads)
+    def quant_pt(name, o, a, n, key):
+        quant(name, o, o + n, T.PT[:, 4 * a:4 * (a + n)], [key + "h", key + "l"])
         rd.setdefault("PT", {})["ve"] = tick["ve"]
 
     for t in range(R):
         pc, ls, ll, NL = part(t), T["ls%d" % t], T["ll%d" % t], T.NL
         lk, lr, X = "ls%d" % t, "ll%d" % t, "x%d" % t
-        places("pb0", lambda q: consts_ac(0) if t == 0 and q == -1 else None)
-        for pb in ("pb1", "pb7"):
-            mm(pb, C, "uu", 128, "rx%d" % t, 0, True, True, ["uuc", "uup", "rx%d" % t])
+        def ahead(q):
+            if q == -1 and t == 0:
+                consts_ac(0)
+            if q == 1:
+                for pb in ("pb1", "pb6"):
+                    mm(pb, C, "uu", 128, "rx%d" % t, 0, True, True, ["uuc", "uup", "rx%d" % t])
+            if q == 0:
+                held("pb1")
+
+        held("pb0")
+        places("pb0", "pb7", ahead)
         sx = T.sx[:, 15::16]
         ts(ls[:], sx, -float(UP), None, AL.add, None, ["sx"], [lk])
         send(pc, ll[:], ls[:], "la%d" % t, [lk])
         arrives([lr], "la%d" % t, ne(t))
         ts(T.L0s[:, 0:21], sx, -1.0, 335.0 + UP, AL.mult, AL.add, ["sx"], ["L0s"])
-        act(T.LS[:, 0:21], sx, AF.Identity, ["sx"], ["LSa"], bias=-335.0 - 2 * UP, scale=2.0)
-        dmas("sy", [(T.L0[16 * k:16 * k + 16, 0:21], T.L0s[0:16, 0:21]) for k in range(8)], "l0", ["L0s"], ["L0"])
+        ts(T.LS[:, 0:21], sx, 2.0, -335.0 - 2 * UP, AL.mult, AL.add, ["sx"], ["LSa"])
+        dmas("sy", [(T.L0f[16 * k:16 * k + 16, :], T.L0s[0:16, :]) for k in range(8)], "l0", ["L0s", "L0z"], ["L0f"])
         if t == 0:
             consts_gp()
         for n in range(2):
             flat(T.XT[:, 4 * C * n:4 * C * (n + 1)], 0, "XTz%d" % n)
+            if t == 0 and n == 0:
+                for b in range(4):
+                    sel(eb("EU%d" % b), T.ones[:], [[1, 512]], AL.is_equal, 0.0, -b, -4, ["ones"], "EU%db" % b)
+        if t == 0:
+            for k in range(4):
+                sel(eb("EL", 1, k, 4), T.de[:, 0:128], [[0, 128]], AL.is_ge, 0.0, 0, 0, ["de"], "ELb")
+
+        IL = T.IL[:, 0:21]
+
+        def unpack(b, e):
+            pb = "pb%d" % (3, 4, 5, 7 if t else 3)[b]
+            if e == "pe":
+                mm(pb, C, "EU%d" % b, 0, "rx%d" % t, 0, True, True, ["rx%d" % t])
+            elif e == "ve":
+                cp(pl("F", b), T[pb][:, 0:C], [pb], ["F%d" % b])
+            else:
+                act(pl("F", b), T[pb][:, 0:C], AF.Copy, [pb], ["F%d" % b])
+
+        def sort(b):
+            act(pl("G", b), pl("F", b).indirect(IL), AF.Copy, ["F%d" % b, "IL"], ["G%d" % b])
 
         def inverse(q):
             if q == -1 and t == 0:
                 consts_ac(1)
+            if q == -1 and t:
+                for e in ("pe", "ac"):
+                    for b in range(4):
+                        unpack(b, e)
             if q == 0:
                 cp(T.oW[:].indirect(ll[:]), T.ji[:], [lr, "ji"], ["oW"])
                 if t == 0:
-                    consts_ve()
+                    consts_ve(0)
+                cp(T.L0[:, 0:21], T.L0f[:, 0:21], ["L0f"], ["L0"])
+                cp(T.L0[:, 32:48], T.L0f[:].indirect(CC), ["L0f", "CC"], ["L0"])
                 to_list(T.oW[:], "oW", T.IL[:, 0:21], "IL")
 
-        places("pb1", inverse)
-        IL = T.IL[:, 0:21]
+        places("pb1", "pb6", inverse)
         tt(T.Bx[:], T.sx[:].indirect(CX), T.de[:], AL.mult, ["sx", "CX", "de"], ["Bx"])
-        act(T.M48[:, 15::16], T.jp[:, 0:48:16], AF.Identity, ["jp", "b21", "M48"], ["M48"], bias=bc[:, 21:22])
+        ts(T.M48[:, 15::16], T.jp[:, 0:48:16], bc[:, 21:22], None, AL.add, None, ["jp", "b21", "M48"], ["M48"])
         if t == 0:
             quantc("ETp")
-        pieces(0, C, T.Bx[:].indirect(IL), ["Bx", "IL"], "PT")
-        quant_pt("pp", 0, C, ["PTh", "PTl"])
-        mm("pb3", C, "EP0a", 0, "pp", 0, True, False, ["pp0"])
-        mm("pb3", C, "EP0b", 0, "pp", 0, False, True, ["pp0"])
-        mm("pb4", C, "ETp", 0, "pp", 0, True, True, ["pp0"])
-        mm("pb5", C, "ERc", 0, "pp", 0, True, True, ["pp0"])
-        if t == 0:
-            quantc("EX")
-            quantc("EU0")
-        act(T.TT[:, 0:C], T.pb4[:, 0:C], AF.Copy, ["pb4"], ["TTp"])
+        else:
+            for b in range(3):
+                sort(b)
+        for j in range(2):
+            for h in range(2):
+                (a, e), (x, y) = HV[h], LV[h]
+                piece(j, a, e - a, T.Bx[:].indirect(T.IL[:, x:y]), ["Bx", "IL"], "PT%d" % h)
+        for h in range(2):
+            quant_pt("pp", HV[h][0], HV[h][0], HV[h][1] - HV[h][0], "PT%d" % h)
+        pk = ["pp0", "pp160"]
+        mm("pb3", C, "EP0a", 0, "pp", 0, True, False, pk)
+        mm("pb3", C, "EP0b", 0, "pp", 0, False, True, pk)
+        mm("pb4", C, "ETp", 0, "pp", 0, True, True, pk)
+        mm("pb5", C, "ERc", 0, "pp", 0, True, True, pk)
+        act(T.TT[:, 0:C], T.pb4[:, 0:C], AF.Copy, ["pb4"], ["TTp"], scale=-1.0)
         act(T.TT[:, 352:688], T.pb5[:, 0:C], AF.Identity, ["pb5"], ["TTf"], bias=-MID, scale=-1.0)
         for k in range(1, 8):
             dmas("sy", [(T.TB[16 * j:16 * j + 16, TW * (k - 1):TW * k], T.TT[16 * k:16 * k + 16, :])
-                        for j in range(7 if t else 8)], "tb%d" % k, ["TTp", "TTf", "TTz"], ["TB%d" % k])
+                        for j in range(8)], "tb%d" % k, ["TTp", "TTf", "TTz"], ["TB%d" % k])
         tt(T.P0[:], T.nt[:], T.pb3[:, 0:C], AL.subtract, ["pb3", "nt"], ["P0"])
-        tt(T.K1[:, 0:C], T.P0[:].indirect(T.L0[:, 0:21]), T.JR[:], AL.add, ["P0", "L0", "JR"], ["K1"])
-        act(T.G48[:], T.K1[:].indirect(CK), AF.Identity, ["K1", "K1z", "CK"], ["G48"], bias=-2.0 ** 19)
+        tt(T.G48[:], T.P0[:].indirect(T.L0[:, 32:35]), T.J48[:], AL.add, ["P0", "L0", "J48"], ["G48"])
+        tt(T.K1[:], T.P0[:].indirect(T.L0[:, 0:21]), T.JR[:, 0:C], AL.add, ["P0", "L0", "JR"], ["K1"])
 
         def own():
             scan(T.s48[:], T.G48[:], T.M48[:], 2.0 ** 23, AL.min, AL.add, ["G48", "M48"], ["s48"])
-
-        def sort(b):
-            act(pl("G", b), pl("F", b).indirect(IL), AF.Copy, ["F%d" % b, "IL"], ["G%d" % b])
 
         def earlier(k):
             for pb in VB[(k + 1) % 2]:
                 mm(pb, C, "EK", 0, "xk", 0, True, False, ["xk0"])
                 if k > 4:
-                    mm(pb, C, "EX", 0, "xx", 0, False, False, ["xx0"])
+                    mm(pb, C, "EX", 0, "xx", 0, False, False, ["xx0", "xx128"])
 
         own()
         for k in range(1, 8):
@@ -468,107 +517,113 @@ def rank_program(g, core, T, topo):
             V, vk = (T.K1[:, 0:C], "K1") if k == 1 else (T[va][:, 0:C], va)
             if 1 < k < 7:
                 earlier(k)
-            if k < 5:
-                mm("pb%d" % (3 + k % 3), C, "EU%d" % (k - 1), 0, "rx%d" % t, 0, True, True, ["rx%d" % t])
-            for s in (1, 2, 0)[:3 if k == 1 else 2]:
-                c = w + S0 + s
+            if t == 0 and 1 < k < 6:
+                unpack(k - 2, "pe")
+            for s in (0, 2, 1)[:3 if k == 1 else 2]:
+                c = w + CELL[s]
                 act(pl("jk", s), V, AF.Sign, [vk, "s48"], [sk + ".%d" % s], bias=T.s48[:, 16 * s + 15:16 * s + 16],
                     scale=-1.0, accum_out=T.SM[:, c:c + 1])
             if k == 1:
                 ts(T.y1[:], V, bc[:, 14:15], bc[:, 14:15], AL.add, AL.subtract, ["K1", "pc"], ["y1"])
                 ts(T.y2[:], V, bc[:, 13:14], bc[:, 13:14], AL.add, AL.subtract, ["K1", "pc"], ["y2"])
                 ts(T.M48[:, 15::16], T.s48[:, 15::16], bc[:, 7:8], None, AL.add, None, ["s48", "b7"], ["M48"])
-                tt(T.PT[:, 0::4], T.y1[:], T.y2[:], AL.subtract, ["y1", "y2"], ["XK", "PT"])
+                if t == 0:
+                    quantc("EX")
+                tt(T.PT[:, 0::4], T.y1[:], T.y2[:], AL.subtract, ["y1", "y2"], ["XKh", "PT"])
             else:
-                ts(T.M48[:, 15::16], T.s48[:, 15::16], bc[:, 7:8], None, AL.add, None, ["s48", "b7"], ["M48"])
-                ts(T.CB[:], T[vb][:, 0:C], T.s48[:, 15:16], 2.0, AL.is_lt, AL.mult, [vb, "s48"], ["CBk"])
-                scan(T.SM[:, w + 8:w + S0 + 1], T.CB[:, 0:168], T.CB[:, 168:C], -335.0, AL.add, AL.add, ["CBk"],
-                     [sk + ".0"])
+                ts(T.CB[:], T[vb][:, 0:C], T.s48[:, 31:32], 2.0, AL.is_lt, AL.mult, [vb, "s48"], ["CBk"])
+            if k < 7:
+                ts(T.OF[:, 0:16], T.SM[:, w:w + 8].indirect(CWa), -0.5, 167.5, AL.mult, AL.add,
+                   [sk + ".0", "SMc", "CW"], ["OFa"])
+            else:
+                quant_pt("lt", 0, 0, 160, "LT")
+                mm("pb2", 160, "EL", 0, "lt", 0, True, True, ["lt0"])
+            if k > 1:
+                scan(T.SM[:, w + 16:w + CELL[1] + 1], T.CB[:, 0:168], T.CB[:, 168:C], -335.0, AL.add, AL.add, ["CBk"],
+                     [sk + ".1"])
             if k == 7:
                 break
-            sr = [sk + ".%d" % s for s in range(3)] + ["SMc"]
-            ts(T.OF[:], T.SM[:, w:w + SW].indirect(CW), -0.5, 167.5, AL.mult, AL.add, sr + ["CW"], ["OF"])
-            if k == 1:
-                quant_pt("xk", 0, C, ["XK"])
-                earlier(k)
             o, tk = TW * (k - 1), ["TB%d" % k]
             n, e = divmod(k - 1, 4)
             a, z = 4 * C * n, "XTz%d" % n
-            cp(T.XT[:, a + e + 640:a + 4 * C:4], T.TB[:, o:o + 352].indirect(T.OF[:, 10:21]), ["OF", z] + tk, ["XT1"])
-            act(T.XT[:, a + e:a + 640:4], T.TB[:, o:o + 352].indirect(T.OF[:, 0:10]), AF.Copy, ["OF", z] + tk, ["XT0"])
-            act(T.G48[:], T.TB[:, o + 352:o + TW].indirect(T.OF[:, 32:35]), AF.Identity, ["OF"] + tk, ["G48"],
+            win = T.TB[:, o:o + 352]
+            act(T.XT[:, a + e:a + 512:4], win.indirect(T.OF[:, 0:8]), AF.Copy, ["OFa", z] + tk, ["XT0"])
+            if k > 1:
+                ts(T.M48[:, 15::16], T.s48[:, 15::16], bc[:, 7:8], None, AL.add, None, ["s48", "b7"], ["M48"])
+            sr = [sk + ".%d" % s for s in range(3)] + ["SMc"]
+            ts(T.OF[:, 16:48], T.SM[:, w:w + SW].indirect(CWb), -0.5, 167.5, AL.mult, AL.add, sr + ["CW"], ["OFb"])
+            if k == 1:
+                quant_pt("xk", 0, 0, C, "XK")
+                earlier(k)
+            act(T.XT[:, a + e + 960:a + 4 * C:4], win.indirect(T.OF[:, 24:30]), AF.Copy, ["OFb", z] + tk, ["XT2"])
+            act(T.G48[:], T.TB[:, o + 352:o + TW].indirect(T.OF[:, 32:35]), AF.Identity, ["OFb"] + tk, ["G48"],
                 bias=MID * KEY, scale=KEY)
-            quant("xx", C * n, C * n + C, T.XT[:, a:a + 4 * C], ["XT0", "XT1", z])
+            quant("xx", C * n, C * n + 128, T.XT[:, a:a + 512], ["XT0", z])
+            cp(T.XT[:, a + e + 512:a + 960:4], win.indirect(T.OF[:, 16:23]), ["OFb", z] + tk, ["XT1"])
+            quant("xx", C * n + 128, C * n + C, T.XT[:, a + 512:a + 4 * C], ["XT1", "XT2", z])
             for pb in VB[(k + 1) % 2]:
-                mm(pb, C, "EX", 0, "xx", C * n, False, True, ["xx%d" % (C * n)])
+                mm(pb, C, "EX", 0, "xx", C * n, False, True, ["xx%d" % (C * n), "xx%d" % (C * n + 128)])
             own()
-            if k < 5:
-                pb = "pb%d" % (3 + k % 3)
-                act(pl("F", k - 1), T[pb][:, 0:C], AF.Copy, [pb], ["F%d" % (k - 1)])
-            if k in (3, 4, 5, 6):
-                sort(k - 3)
-            if k == 2 and t == 0:
-                consts_ac(2)
-            if k == 4 and t == 0:
+            if t == 0 and k in (1, 2, 3):
+                quantc("EU0") if k == 1 else consts_ve(k - 1)
+            if t == 0 and 1 < k < 6:
+                unpack(k - 2, "ve")
+            if t == 0 and k > 2 or t and k == 2:
+                sort(k - 3 if t == 0 else 3)
+            if k > 4:
+                piece(k - 5, 0, 160, T.SM[:, 0:5 * SW].indirect(CB),
+                      ["SM%d.%d" % (a, s) for a in range(1, 6) for s in range(3)] + ["CB"], "LT")
+            if k == 6 and t == 0:
                 quantc("EL")
-            if k == 5:
-                pieces(0, 160, T.SM[:, 0:5 * SW].indirect(CB),
-                       ["SM%d.%d" % (a, s) for a in range(1, 6) for s in range(3)] + ["CB"], "LT")
-            if k == 6:
-                quant_pt("lt", 0, 160, ["LTh", "LTl"])
-                mm("pb2", 160, "EL", 0, "lt", 0, True, True, ["lt0"])
-        pieces(160, 64, T.SM[:].indirect(CF), ["SM%d.%d" % (a, s) for a in (6, 7) for s in range(3)] + ["CB"], "LF")
+        for j in range(2):
+            piece(j, 160, 64, T.SM[:].indirect(CF), ["SM%d.%d" % (a, s) for a in (6, 7) for s in range(3)] + ["CB"],
+                  "LF")
         act(T.LS[:, 32:192], T.pb2[:, 0:160], AF.Copy, ["pb2"], ["LSb"])
         if t == R - 1:
             act(T.Vs[:], T[VB[1][0]][:, 0:C], AF.Copy, [VB[1][0]], ["Vs"])
-        quant_pt("lf", 160, 128, ["LFh", "LFl"])
+        quant_pt("lf", 0, 160, 128, "LF")
         mm("pb3", 128, "EL", 0, "lf", 0, True, True, ["lf0"])
         cp(T.LS[:, 192:256], T.pb3[:, 0:64], ["pb3"], ["LSc"])
         ts(NL[:], T.LS[:].indirect(CP), -0.5, 167.5, AL.mult, AL.add, ["LS0", "LSa", "LSb", "LSc", "CP"], ["NL"])
         zk = ["NL"]
-        for h in range(2):
-            a, e = HV[h]
-            x, y = LV[h]
-            for b in range(4):
-                o, i = T.Z[:, 4 * a + b:4 * e:4], pl("G", b).indirect(NL[:, x:y])
-                if b < 2:
-                    cp(o, i, ["G%d" % b] + zk, ["Z%d.%d" % (h, b)])
-                else:
-                    act(o, i, AF.Copy, ["G%d" % b] + zk, ["Z%d.%d" % (h, b)])
-            quant("z", a, e, T.Z[:, 4 * a:4 * e], ["Z%d.%d" % (h, b) for b in range(4)])
-
-        def layer(h):
-            a, e = HV[h]
-            for b in range(4):
-                for j in (1, 0):
-                    mm("pb%d" % (2 * b + j), e - a, "wl", 128 * (b + 4 * j), "z", a, True, True,
-                       ["w0", "wsc", "z%d" % a])
-                act(T.yt[:, 176 * b:176 * b + e - a], T["pb%d" % (2 * b + 1)][:, 0:e - a], AF.Copy,
-                    ["pb%d" % (2 * b + 1)], ["yt%d" % b])
-
-        def best(h):
-            a, e = HV[h]
-            for b in range(4):
-                tt(pl("Ym", b, a, e), T["pb%d" % (2 * b)][:, 0:e - a], T.yt[:, 176 * b:176 * b + e - a], AL.max,
-                   ["pb%d" % (2 * b), "yt%d" % b], ["Y%d.%d" % (b, h)])
-
-        layer(0)
+        for b in range(4):
+            o, i = T.Z[:, b::4], pl("G", b).indirect(NL[:, 0:21])
+            if b < 1:
+                cp(o, i, ["G%d" % b] + zk, ["Z%d" % b])
+            else:
+                act(o, i, AF.Copy, ["G%d" % b] + zk, ["Z%d" % b])
         cp(T.iW[:].indirect(NL[:, 0:21]), T.ji[:], ["ji"] + zk, ["iW"])
-        best(0)
-        act(T.tm[:], T.iW[:].indirect(ll[:]), AF.Copy, ["iW", lr], ["tm"])
-        layer(1)
+        quant("z", 0, C, T.Z[:], ["Z%d" % b for b in range(4)])
+        for b in range(4):
+            for j in (1, 0):
+                mm("pb%d" % (2 * b + j), C, "wl", 128 * (b + 4 * j), "z", 0, True, True, ["w0", "wsc", "z0"])
+            act(pl("yt", b), T["pb%d" % (2 * b + 1)][:, 0:C], AF.Copy, ["pb%d" % (2 * b + 1)], ["yt%d" % b])
+
+        def best(b):
+            tt(pl("Ym", b), T["pb%d" % (2 * b)][:, 0:C], pl("yt", b), AL.max, ["pb%d" % (2 * b), "yt%d" % b],
+               ["Y%d" % b])
+
+        def back(h, b, e):
+            (a, z), (x, y) = HV[h], LV[h]
+            o, i = T.Yp[:, 4 * a + b:4 * z:4], pl("Ym", b).indirect(T.ML[:, x:y])
+            rk = ["ML", "Y%d" % b]
+            if e == "ve":
+                ts(o, i, 0.03125, None, AL.mult, None, rk, ["Yp%d.%d" % (h, b)])
+            else:
+                act(o, i, AF.Copy, rk, ["Yp%d.%d" % (h, b)], scale=0.03125)
+
+        cp(T.tm[:], T.iW[:].indirect(ll[:]), ["iW", lr], ["tm"])
         to_list(T.tm[:], "tm", T.ML[:, 0:21], "ML")
+        best(0)
         best(1)
+        back(0, 0, "ve")
+        best(2)
+        back(0, 1, "ve")
+        best(3)
+        for h, b, e in ((1, 0, "ac"), (0, 2, "ve"), (1, 1, "ac"), (0, 3, "ve"), (1, 2, "ac"), (1, 3, "ac")):
+            back(h, b, e)
         for h in range(2):
             a, e = HV[h]
-            x, y = LV[h]
-            for b in range(4):
-                o, i = T.Yp[:, 4 * a + b:4 * e:4], pl("Ym", b).indirect(T.ML[:, x:y])
-                rk = ["ML", "Y%d.0" % b, "Y%d.1" % b]
-                if b >= 2:
-                    ts(o, i, 0.03125, None, AL.mult, None, rk, ["Yp%d.%d" % (h, b)])
-                else:
-                    act(o, i, AF.Copy, rk, ["Yp%d.%d" % (h, b)], scale=0.03125)
             quant("y%d" % t, a, e, T.Yp[:, 4 * a:4 * e], ["Yp%d.%d" % (h, b) for b in range(4)])
             k, sem = ["y%d%d" % (t, a)], ("ya%d", "yb%d")[h] % t
             send(pc, T["ry%dq" % t][:, a:e].bitcast(dt.uint8), T["y%dq" % t][:, a:e].bitcast(dt.uint8), sem, k)
@@ -579,7 +634,7 @@ def rank_program(g, core, T, topo):
             for b in range(4):
                 mm("pb%d" % (4 * h + b), e - a, "EU%d" % b, 0, X, a, True, False, [X + "0", X + "160"])
         if t == R - 1:
-            tt(T.tb[:], T.Vs[:], T.JR[:], AL.subtract, ["Vs", "JR"], ["tb"])
+            tt(T.tb[:], T.Vs[:], T.JR[:, 0:C], AL.subtract, ["Vs", "JR"], ["tb"])
             quant("v", 0, 128, T.vin[:], ["vin"])
             ts(T.tb[:], T.tb[:], 1.0 / KEY, M1, AL.mult, AL.add, ["tb"], ["tb"])
             ts(T.tb[:], T.tb[:], -M1, 335.0 + MID - 8 * UP, AL.add, AL.add, ["tb"], ["tb"])
@@ -601,12 +656,18 @@ def rank_program(g, core, T, topo):
             for pb in ("pb0", "pb7"):
                 mm(pb, C, "uu", 0, N, 0, True, True, [N + "0", N + "160"])
             send_x(t + 1)
-    nk = ["x20", "x2160"]
-    mm("pb0", C, "v", 0, "x2", 0, True, True, ["v0"] + nk)
-    dmas("sy", [(T.oc[:], T.x2q[:].bitcast(dt.uint8))], "out", nk)
-    act(T.ysb[:], T.pb0[:, 0:C], AF.Copy, ["pb0"], ["ysb"])
-    dmas("sy", [(T.osc[4 * k:4 * k + 4, :], T.x2s[32 * k:32 * k + 4, :]) for k in range(4)], "out", nk)
-    dmas("ac", [(T.y[:], T.ysb[:])], "out", ["ysb"])
+    for h in range(2):
+        a, e = HV[h]
+        pb, nk = "pb%d" % h, ["x2%d" % a]
+        mm(pb, e - a, "v", 0, "x2", a, True, True, ["v0"] + nk)
+        dmas("sy", [(T.oc[:, 4 * a:4 * e], T.x2q[:, a:e].bitcast(dt.uint8))], "out", nk)
+        if h:
+            cp(T.ysb[:, a:e], T[pb][:, 0:e - a], [pb], ["ysb%d" % h])
+            dmas("ac", [(T.osc[4 * k:4 * k + 4, :], T.x2s[32 * k:32 * k + 4, :]) for k in range(4)], "out",
+                 ["x20"] + nk)
+        else:
+            act(T.ysb[:, a:e], T[pb][:, 0:e - a], AF.Copy, [pb], ["ysb%d" % h])
+        dmas("sy" if h else "ac", [(T.y[:, a:e], T.ysb[:, a:e])], "out", ["ysb%d" % h])
     for s in tick:
         g.wait_ge(T.sem[s], tick[s])
     for s in dcount:

@@ -16,8 +16,8 @@ SW, TW = 192, 704
 CELL = (0, 183, 184)
 TILES = [(("d", 13, 12, 11), 336, "ERc"), ((10, 9, 8, 7), 160, "ERc"), ((6, 5, 4, 3), 128, "ERc"),
          ((2, 1), 128, "ERc"), ((20, 19, 18, 17), 320, "ERb"), ((16, 15, 14), 256, "ERb")]
-ON_ACT = range(20, 13, -1)
-ON_VE = range(13, 0, -1)
+LOW = 14
+ON_ACT, ON_VE = range(20, LOW - 1, -1), range(LOW - 1, 0, -1)
 
 SCRATCH = {}
 
@@ -31,11 +31,12 @@ def _q(name, n):
     _s(name + "s", n, "uint8")
 
 
-CONST = ["ERc", "ERb", "EL", "EU0", "EU1", "EU2", "EU3", "ETp", "EP0a", "EP0b", "EX", "EK"]
-BATCH = {"ERc": 2, "EL": 1, "EU0": 4, "ETp": 3, "EX": 2}
+CONST = ["ERc", "ERb", "EL", "EU0", "EU1", "EU2", "EU3", "ETp", "EP0", "EX", "EK", "EP1"]
+BATCH = {"ERc": 2, "EL": 1, "EU0": 4, "ETp": 4, "EP1": 1}
+SHARE = {"xk": ("xx", C), "xe": ("xx", 2 * C), "xl": ("xx", 3 * C), "lf": ("lt", 160)}
 VB = [("pb0", "pb1"), ("pb6", "pb7")]
 _s("XT", 8 * C, "bfloat16")
-for _n in ("xin", "xt0", "xt1", "Z", "Yp", "PT", "F", "G"):
+for _n in ("xin", "xt0", "xt1", "Z", "Yp", "PT", "ZT", "F", "G"):
     _s(_n, 4 * C, "bfloat16")
 for _n in ("uin", "vin", "ones", "W1"):
     _s(_n, 512, "bfloat16")
@@ -51,8 +52,8 @@ _s("LS", 256)
 _s("JR", C)
 for _k in range(8):
     _s("pb%d" % _k, 512, "float32", "psum")
-for _n, _k in (("u", 128), ("v", 128), ("uu", 256), ("wl", 1024), ("z", C), ("pp", C), ("xx", 2 * C), ("xk", C),
-               ("lt", 160), ("lf", 128), ("rq", sum(_t[1] for _t in TILES))):
+for _n, _k in (("u", 128), ("v", 128), ("uu", 256), ("wl", 1024), ("z", C), ("pp", C), ("xx", 3 * C + 208),
+               ("lt", 288), ("rq", sum(_t[1] for _t in TILES))):
     _q(_n, _k)
 _s("RT", 4 * sum(_t[1] for _t in TILES), "bfloat16")
 for _t in range(R):
@@ -84,7 +85,7 @@ _s("L0s", 24)
 _s("L0f", 24)
 _s("bc", 32)
 
-SEMAPHORES = ["ve", "ac", "pe", "gp", "lx", "lu", "lv", "lw", "lz", "out", "loc", "l0"]
+SEMAPHORES = ["ve", "ac", "pe", "gp", "lx", "lu", "lv", "lw", "lz", "out", "loc", "l0", "zp", "zx"]
 SEMAPHORES += ["tb%d" % _g for _g in range(1, 8)]
 SEMAPHORES += ["%s%d" % (a, t) for a in ("xa", "la", "ya", "yb") for t in range(R)]
 
@@ -155,7 +156,7 @@ def rank_program(g, core, T, topo):
         op("ac", lambda q: q.activation(out, a, f, **k), reads, writes)
 
     def at(n):
-        return ("E", 128 * CONST.index(n)) if n in CONST else (n, 0)
+        return ("E", 128 * CONST.index(n)) if n in CONST else SHARE.get(n, (n, 0))
 
     def eb(n, m=1, a=0, step=1):
         k = 512 * CONST.index(n)
@@ -176,6 +177,8 @@ def rank_program(g, core, T, topo):
     def mm(bank, n, st, sa, mv, ma, start, stop, reads):
         w, o = at(st)
         o += sa
+        mv, mo = at(mv)
+        ma += mo
         if st in CONST:
             reads = reads + [[b for b in CONST[:CONST.index(st) + 1] if b in BATCH][-1] + "0"]
         op("pe", lambda q: q.matmul_mx(T[bank][:, 0:n], T[w + "q"][:, o:o + 128], T[w + "s"][:, o:o + 128],
@@ -207,7 +210,7 @@ def rank_program(g, core, T, topo):
 
     dmas("sy", [(T.xin[:], T.x[:])], "lx", (), ["xin"])
     dmas("ac", [(T.uin[:], T.u[:])], "lu", (), ["uin"])
-    dmas("sy", [(T.wlq[:].bitcast(dt.uint8), T.wc[:])], "lw", (), ["w0"])
+    dmas("sy", [(T.wlq[:].bitcast(dt.uint8), T.wc[:])], "lw", ["xin"], ["w0"])
     dmas("sy", [(T.vin[:], T.v[:])], "lv", (), ["vin"])
     dmas("sy", [(T.wls[:], T.ws[:])], "lz", (), ["wsc"])
     f32 = dict(allow_small_or_imprecise_dtypes=True)
@@ -265,7 +268,7 @@ def rank_program(g, core, T, topo):
     act(eb("ERb"), eb("ERc"), AF.Copy, ["ERcb"], ["ERbb"], scale=0.5)
     act(T.MNx[:], T.k1[:], AF.Identity, ["k1"], ["MNx"], bias=-3072.0)
     ts(bc[:, 2:3], T.de[:, 15:16], -1024.0, bc[:, 0:1], AL.mult, AL.add, ["de", "i"], ["b2"])
-    for a, e, step, base in ((0, 14, -16, 264), (14, 21, 0, 160)):
+    for a, e, step, base in ((0, LOW, -16, 320 - 8 * len(ON_ACT)), (LOW, 21, 0, 160)):
         iota(sm[:, 64 + a:64 + e], [[step, e - a]], base + UP + 1024, 0, "c15", **f32)
     flat(T.J[:, 111:112], 0, "J0")
     ts(MC, sm[:, 64:85], bc[:, 2:3], None, AL.add, None, ["c15", "b2"], ["MC"])
@@ -275,7 +278,7 @@ def rank_program(g, core, T, topo):
     iota(pI[:, 32:53], [[16, 21]], 15, 0, "CXi")
     flat(T.L0s[:, 21:24], 0, "L0z")
     flat(bc[:, 13:15], 0, "pc")
-    sel(eb("EP0b"), T.W1[:], [[0, 512]], AL.is_ge, 0.0, 15, -1, ["W1"], "EP0bb")
+    sel(eb("EP0"), T.W1[:], [[0, 512]], AL.is_ge, 0.0, 15, -1, ["W1"], "EP0b")
     for k, (pat, base, big) in enumerate(((-1, 1, 1.5 * 2.0 ** 43), (1, -14, 1.5 * 2.0 ** 38), (0, 0, 1.5 * 2.0 ** 33),
                                           (0, 0, M32))):
         sel(bc[:, 13:15], bc[:, 13:15], [[8, 2]], AL.not_equal, big, -8 * k, 1, ["pc"], "pc")
@@ -283,10 +286,16 @@ def rank_program(g, core, T, topo):
     iota(T.nt[:], [[-int(KEY), C]], 0, 0, "nt", **f32)
 
     def consts_gp():
-        flat(T.PT[:], 0, "PTz")
+        flat(T.ZT[:], 0, "ZT")
+        dmas("sy", [(T.PT[:], T.ZT[:])], "zp", ["ZT"], ["PTz"])
+        sel(eb("EP1"), T.W1[:], [[0, 512]], AL.is_ge, 0.0, -16, 1, ["W1"], "EP1b")
+        flat(T.TB[:, C:352], 0, "TBz")
+        sel(eb("EP1"), eb("EP1"), [[0, 512]], AL.is_ge, 0.0, 31, -1, ["EP1b"], "EP1b")
         iota(T.JR[:], [[-1, C]], int(BASE) + 335, 0, "JR", **f32)
-        iota(T.J48[:, 0:32], [[-128, 2], [0, 16]], int(BASE) + 335 - 2 ** 19, -1, "J48", **f32)
-        iota(T.J48[:, 32:48], [[0, 16]], int(BASE) + 335 - 2 ** 19 - 240, -1, "J48", **f32)
+        for k, pat, base in ((0, -1, 1), (1, 1, -14)):
+            sel(eb("EP1", 1, k, 4), eb("EP1", 1, k, 4), [[0, 8], [pat, 16]], AL.is_ge, 0.0, base, 0, ["EP1b"], "EP1b")
+        iota(T.J48[:, 0:16], [[0, 16]], int(BASE) + 335 - 2 ** 19 - 208, -1, "J48", **f32)
+        iota(T.J48[:, 16:48], [[-112, 2], [0, 16]], int(BASE) + 335 - 2 ** 19, -1, "J48", **f32)
         for ap, val, key in ((T.TT[:, C:352], 0, "TTz"), (T.TT[:, 688:TW], 0, "TTz"),
                              (T.SM[:, 1::SW], -337, "SMc"), (T.SM[:, 2::SW], 0, "SMc"),
                              (T.LS[:, 21:32], 0, "LS0")):
@@ -300,7 +309,6 @@ def rank_program(g, core, T, topo):
             act(T.MN[:], T.k1[:], AF.Identity, ["k1"], ["MN"], bias=-3072.0)
         if q == 1:
             act(T.M48[:], T.k1[:, 0:48], AF.Identity, ["k1"], ["M48"], bias=-3072.0 * 2048, scale=2048.0)
-            act(eb("EP0a"), eb("EP0b"), AF.Copy, ["EP0bb"], ["EP0ab"], scale=KEY - 1)
             act(bc[:, 16:18], T.de[:, 0:15:14], AF.Copy, ["de"], ["b8"], scale=KEY - 1, accum_out=bc[:, 8:9])
             act(bc[:, 18:20], T.de[:, 1:16:14], AF.Copy, ["de"], ["b9"], accum_out=bc[:, 9:10])
             act(bc[:, 26:27], bc[:, 13:14], AF.Sign, ["pc"], ["b26"])
@@ -314,22 +322,24 @@ def rank_program(g, core, T, topo):
         if q == 0:
             ts(bc[:, 3:4], i, gr, None, AL.subtract, None, ["i"], ["b3"])
             cp(CX, pI[:, 32:53], ["CXi"], ["CX"])
+            ts(bc[:, 22:24], bc[:, 13:15], -2.0 ** 20, None, AL.add, None, ["pc"], ["pd"])
             ts(T.MN[:, 15::16], T.MN[:, 15::16], 1536.0, None, AL.add, None, ["MN"], ["MN"])
             ts(bc[:, 4:5], bc[:, 3:4], 0.0, CELL[1] - 1.0, AL.is_equal, AL.mult, ["b3"], ["b4"])
             ts(bc[:, 5:6], bc[:, 3:4], 8.0, CELL[2] - 1.0, AL.is_equal, AL.mult, ["b3"], ["b5"])
-            ts(bc[:, 6:7], i, 8.0, 15.0, AL.mult, AL.min, ["i"], ["b6"])
+            ts(bc[:, 6:7], T.de[:, 0:1], 13.0, gr, AL.mult, AL.add, ["de", "i"], ["b6"])
             ts(bc[:, 7:8], T.de[:, 15:16], -2.0 ** 21, 2.0 ** 21, AL.mult, AL.add, ["de"], ["b7"])
             ts(bc[:, 21:22], T.de[:, 15:16], -2.0 ** 21, 2.0 ** 21 + 2.0 ** 19, AL.mult, AL.add, ["de"], ["b21"])
             ts(CWa, bc[:, 3:4], 0.0, None, AL.not_equal, None, ["b3"], ["CW"])
             ts(CL[:, 24:25], bc[:, 5:6], bc[:, 4:5], 1.0, AL.add, AL.add, ["b4", "b5"], ["CW"])
             ts(CL[:, 25:26], i, float(CELL[1]), float(CELL[2]), AL.mult, AL.min, ["i"], ["CW"])
-            ts(CC, bc[:, 6:7], gr, None, AL.add, None, ["b6", "i"], ["CC"])
+            ts(CC, T.de[:, 2:3], 7.0, bc[:, 6:7], AL.mult, AL.add, ["b6", "de"], ["CC"])
         e, m = sm[:, 88:90], [sm[:, 96 + 2 * s:98 + 2 * s] for s in range(3)]
         if q == 1:
             ts(e, sm[:, 94:96], bc[:, 3:4], None, AL.add, None, ["h2", "b3"], ["e"])
             ts(bc[:, 10:11], gr, 7.0, CELL[1] - 2.0, AL.is_lt, AL.mult, ["i"], ["b10"])
+            ts(bc[:, 11:12], gr, 6.0, CELL[2] - 2.0, AL.is_lt, AL.mult, ["i"], ["b10"])
             ts(CP, sm[:, 92:94], i, None, AL.subtract, None, ["p2", "i"], ["CP"])
-            for s, (val, w) in enumerate(((0.0, -2.0), (8.0, bc[:, 10:11]), (15.0, CELL[2] - 2.0))):
+            for s, (val, w) in enumerate(((13.0, -2.0), (0.0, bc[:, 10:11]), (7.0, bc[:, 11:12]))):
                 ts(m[s], e, val, w, AL.is_equal, AL.mult, ["e", "b10"], ["m%d" % s])
         if q == 2:
             tt(m[0], m[0], m[2], AL.add, ["m0", "m2"], ["m0"])
@@ -342,7 +352,7 @@ def rank_program(g, core, T, topo):
 
     def held(bank):
         S, H = T[bank], "H" + bank
-        parts = ((224, C, "h"), (0, 224, "l"))
+        parts = ((16 * LOW, C, "h"), (0, 16 * LOW, "l"))
         for a, e, k in parts:
             tt(T.t1[:, a:e], S[:, a:e], T.MH[:, a:e], AL.max, [bank, "MH"], ["t1" + k])
         for a, e, k in parts:
@@ -350,7 +360,20 @@ def rank_program(g, core, T, topo):
         for a, e, k in parts:
             tt(cells("d", a, e), S[:, a:e], T[H][:, a:e], AL.is_gt, [bank, H + k] + zs, ["RT.d"])
 
-    def places(bank, twin, hook):
+    def sums(c):
+        scan(T.J[:, 112 * c + 112 - 8 * c:112 * c + 112], cells(c, 0, 8 * c), cells(c, 8 * c, 16 * c), 0.0,
+             AL.add, AL.add, ["RT.%s" % c], ["J%d" % c])
+
+    def block(bank, c):
+        H = "H" + bank
+        ts(cells(c, 0, 16 * c), T[bank][:, 0:16 * c], T[H][:, 16 * c + 15:16 * c + 16], None, AL.is_ge, None,
+           [bank, H + "l"] + zs, ["RT.%s" % c])
+        if c == LOW - 1:
+            scan(T.DS[:], T.rm[:], cells("d", 0, C), 0.0, AL.mult, AL.add, ["rm", "RT.d"], ["DS"])
+        else:
+            sums(c + 1)
+
+    def places(bank, twin, done, hook):
         S, H = T[bank], "H" + bank
 
         def diff(n):
@@ -363,8 +386,9 @@ def rank_program(g, core, T, topo):
             if n + 1 < len(ON_ACT):
                 diff(n + 1)
             act(cells(c, 0, 16 * c), T["df%d" % (n % 2)][:, 0:16 * c], AF.Sign, ["df%d" % (n % 2), "tiny"] + zs,
-                ["RT.%s" % c, "AC"], bias=bc[:, 25:26], scale=-1.0, accum_out=sm[:, c - 14:c - 13])
-        act(T.J[:, 112 * 14 + 111::112], sm[:, 0:7], AF.Copy, ["AC"], ["J%d" % c for c in ON_ACT], scale=0.5)
+                ["RT.%s" % c, "AC"], bias=bc[:, 25:26], scale=-1.0, accum_out=sm[:, 100 + c:101 + c])
+        act(T.J[:, 112 * LOW + 111::112], sm[:, 100 + LOW:121], AF.Copy, ["AC"], ["J%d" % c for c in ON_ACT],
+            scale=0.5)
         hook(-1)
 
         def count(q):
@@ -373,17 +397,8 @@ def rank_program(g, core, T, topo):
                   ["RT.%s" % c for c in blocks] + ["RTz%d" % q])
             mm("pb2", w, st, 0, "rq", start[q], q == 0, q == 5, ["rq%d" % start[q]])
 
-        def sums(c):
-            scan(T.J[:, 112 * c + 112 - 8 * c:112 * c + 112], cells(c, 0, 8 * c), cells(c, 8 * c, 16 * c), 0.0,
-                 AL.add, AL.add, ["RT.%s" % c], ["J%d" % c])
-
-        for c in ON_VE:
-            ts(cells(c, 0, 16 * c), S[:, 0:16 * c], T[H][:, 16 * c + 15:16 * c + 16], None, AL.is_ge, None,
-               [bank, H + "l"] + zs, ["RT.%s" % c])
-            if c == 13:
-                scan(T.DS[:], T.rm[:], cells("d", 0, C), 0.0, AL.mult, AL.add, ["rm", "RT.d"], ["DS"])
-            else:
-                sums(c + 1)
+        for c in ON_VE[done:]:
+            block(bank, c)
             if c in (10, 6, 2):
                 count({10: 0, 6: 1, 2: 2}[c])
         hook(1)
@@ -394,6 +409,7 @@ def rank_program(g, core, T, topo):
         hook(0)
         count(5)
         tt(T.MNx[:, 15::16], T.J[:, 111::112], X2, AL.add, ["X2"] + ["J%d" % c for c in range(21)], ["MNx"])
+        hook(2)
         scan(T.sx[:], T.pb2[:, 0:C], T.MNx[:], 4096.0, AL.min, AL.add, ["pb2", "MNx"], ["sx"])
 
     def to_list(src, key, o, okey):
@@ -422,9 +438,12 @@ def rank_program(g, core, T, topo):
                     mm(pb, C, "uu", 128, "rx%d" % t, 0, True, True, ["uuc", "uup", "rx%d" % t])
             if q == 0:
                 held("pb1")
+            if q == 2:
+                block("pb1", ON_VE[0])
 
         held("pb0")
-        places("pb0", "pb7", ahead)
+        places("pb0", "pb7", 0, ahead)
+        block("pb1", ON_VE[1])
         sx = T.sx[:, 15::16]
         ts(ls[:], sx, -float(UP), None, AL.add, None, ["sx"], [lk])
         send(pc, ll[:], ls[:], "la%d" % t, [lk])
@@ -434,12 +453,10 @@ def rank_program(g, core, T, topo):
         dmas("sy", [(T.L0f[16 * k:16 * k + 16, :], T.L0s[0:16, :]) for k in range(8)], "l0", ["L0s", "L0z"], ["L0f"])
         if t == 0:
             consts_gp()
-        for n in range(2):
-            flat(T.XT[:, 4 * C * n:4 * C * (n + 1)], 0, "XTz%d" % n)
-            if t == 0 and n == 0:
-                for b in range(4):
-                    sel(eb("EU%d" % b), T.ones[:], [[1, 512]], AL.is_equal, 0.0, -b, -4, ["ones"], "EU%db" % b)
+        dmas("sy", [(T.XT[:, 4 * C * n:4 * C * (n + 1)], T.ZT[:]) for n in range(2)], "zx", ["ZT"], ["XTz0", "XTz1"])
         if t == 0:
+            for b in range(4):
+                sel(eb("EU%d" % b), T.ones[:], [[1, 512]], AL.is_equal, 0.0, -b, -4, ["ones"], "EU%db" % b)
             for k in range(4):
                 sel(eb("EL", 1, k, 4), T.de[:, 0:128], [[0, 128]], AL.is_ge, 0.0, 0, 0, ["de"], "ELb")
 
@@ -468,15 +485,18 @@ def rank_program(g, core, T, topo):
                 cp(T.oW[:].indirect(ll[:]), T.ji[:], [lr, "ji"], ["oW"])
                 if t == 0:
                     consts_ve(0)
+            if q == 2:
+                scan(T.sa[:], T.oW[:], T.MN[:], 4096.0, AL.min, AL.add, ["oW", "MN"], ["sa"])
                 cp(T.L0[:, 0:21], T.L0f[:, 0:21], ["L0f"], ["L0"])
                 cp(T.L0[:, 32:48], T.L0f[:].indirect(CC), ["L0f", "CC"], ["L0"])
-                to_list(T.oW[:], "oW", T.IL[:, 0:21], "IL")
 
-        places("pb1", "pb6", inverse)
+        places("pb1", "pb6", 2, inverse)
+        ts(T.IL[:, 0:21], T.sa[:, 15::16], -512.0, None, AL.add, None, ["sa"], ["IL"])
         tt(T.Bx[:], T.sx[:].indirect(CX), T.de[:], AL.mult, ["sx", "CX", "de"], ["Bx"])
         ts(T.M48[:, 15::16], T.jp[:, 0:48:16], bc[:, 21:22], None, AL.add, None, ["jp", "b21", "M48"], ["M48"])
         if t == 0:
             quantc("ETp")
+            quantc("EP1")
         else:
             for b in range(3):
                 sort(b)
@@ -487,18 +507,24 @@ def rank_program(g, core, T, topo):
         for h in range(2):
             quant_pt("pp", HV[h][0], HV[h][0], HV[h][1] - HV[h][0], "PT%d" % h)
         pk = ["pp0", "pp160"]
-        mm("pb3", C, "EP0a", 0, "pp", 0, True, False, pk)
-        mm("pb3", C, "EP0b", 0, "pp", 0, False, True, pk)
+        mm("pb3", C, "EP0", 0, "pp", 0, True, True, pk)
         mm("pb4", C, "ETp", 0, "pp", 0, True, True, pk)
         mm("pb5", C, "ERc", 0, "pp", 0, True, True, pk)
+        mm("pb7", C, "EP1", 0, "pp", 0, True, True, pk)
+        tt(T.y1[:], T.nt[:].indirect(T.L0[:, 0:21]), T.JR[:], AL.add, ["nt", "L0", "JR"], ["y1"])
+        tt(T.s48[:], T.nt[:].indirect(T.L0[:, 32:35]), T.J48[:], AL.add, ["nt", "L0", "J48"], ["s48"])
         act(T.TT[:, 0:C], T.pb4[:, 0:C], AF.Copy, ["pb4"], ["TTp"], scale=-1.0)
         act(T.TT[:, 352:688], T.pb5[:, 0:C], AF.Identity, ["pb5"], ["TTf"], bias=-MID, scale=-1.0)
+        act(T.TB[:, 0:C], T.pb7[:, 0:C], AF.Copy, ["pb7", "TBz"], ["TB0"], scale=-1.0)
         for k in range(1, 8):
-            dmas("sy", [(T.TB[16 * j:16 * j + 16, TW * (k - 1):TW * k], T.TT[16 * k:16 * k + 16, :])
+            a = 352 if k == 1 else 0
+            dmas("sy", [(T.TB[16 * j:16 * j + 16, TW * (k - 1) + a:TW * k], T.TT[16 * k:16 * k + 16, a:TW])
                         for j in range(8)], "tb%d" % k, ["TTp", "TTf", "TTz"], ["TB%d" % k])
-        tt(T.P0[:], T.nt[:], T.pb3[:, 0:C], AL.subtract, ["pb3", "nt"], ["P0"])
-        tt(T.G48[:], T.P0[:].indirect(T.L0[:, 32:35]), T.J48[:], AL.add, ["P0", "L0", "J48"], ["G48"])
-        tt(T.K1[:], T.P0[:].indirect(T.L0[:, 0:21]), T.JR[:, 0:C], AL.add, ["P0", "L0", "JR"], ["K1"])
+        ts(T.P0[:], T.pb3[:, 0:C], -KEY, None, AL.mult, None, ["pb3"], ["P0"])
+        if t == 0:
+            quant("xe", 0, 208, T.XT[:, 0:832], ["XTz0"])
+        tt(T.G48[:], T.P0[:].indirect(T.L0[:, 32:35]), T.s48[:], AL.add, ["P0", "L0", "s48"], ["G48"])
+        tt(T.K1[:], T.P0[:].indirect(T.L0[:, 0:21]), T.y1[:], AL.add, ["P0", "L0", "y1"], ["K1"])
 
         def own():
             scan(T.s48[:], T.G48[:], T.M48[:], 2.0 ** 23, AL.min, AL.add, ["G48", "M48"], ["s48"])
@@ -507,7 +533,7 @@ def rank_program(g, core, T, topo):
             for pb in VB[(k + 1) % 2]:
                 mm(pb, C, "EK", 0, "xk", 0, True, False, ["xk0"])
                 if k > 4:
-                    mm(pb, C, "EX", 0, "xx", 0, False, False, ["xx0", "xx128"])
+                    mm(pb, C, "EX", 0, "xx", 0, False, False, ["xx0"])
 
         own()
         for k in range(1, 8):
@@ -524,12 +550,10 @@ def rank_program(g, core, T, topo):
                 act(pl("jk", s), V, AF.Sign, [vk, "s48"], [sk + ".%d" % s], bias=T.s48[:, 16 * s + 15:16 * s + 16],
                     scale=-1.0, accum_out=T.SM[:, c:c + 1])
             if k == 1:
-                ts(T.y1[:], V, bc[:, 14:15], bc[:, 14:15], AL.add, AL.subtract, ["K1", "pc"], ["y1"])
-                ts(T.y2[:], V, bc[:, 13:14], bc[:, 13:14], AL.add, AL.subtract, ["K1", "pc"], ["y2"])
+                ts(T.y1[:], V, bc[:, 14:15], bc[:, 23:24], AL.add, AL.subtract, ["K1", "pc", "pd"], ["y1"])
+                ts(T.y2[:], V, bc[:, 13:14], bc[:, 22:23], AL.add, AL.subtract, ["K1", "pc", "pd"], ["y2"])
                 ts(T.M48[:, 15::16], T.s48[:, 15::16], bc[:, 7:8], None, AL.add, None, ["s48", "b7"], ["M48"])
-                if t == 0:
-                    quantc("EX")
-                tt(T.PT[:, 0::4], T.y1[:], T.y2[:], AL.subtract, ["y1", "y2"], ["XKh", "PT"])
+                scan(T.PT[:, 0::4], T.y1[:], T.y2[:], 0.0, AL.max, AL.subtract, ["y1", "y2"], ["XKh", "PT"])
             else:
                 ts(T.CB[:], T[vb][:, 0:C], T.s48[:, 31:32], 2.0, AL.is_lt, AL.mult, [vb, "s48"], ["CBk"])
             if k < 7:
@@ -538,32 +562,36 @@ def rank_program(g, core, T, topo):
             else:
                 quant_pt("lt", 0, 0, 160, "LT")
                 mm("pb2", 160, "EL", 0, "lt", 0, True, True, ["lt0"])
-            if k > 1:
+            if k == 1:
+                quant_pt("xk", 0, 0, C, "XK")
+                earlier(k)
+            else:
                 scan(T.SM[:, w + 16:w + CELL[1] + 1], T.CB[:, 0:168], T.CB[:, 168:C], -335.0, AL.add, AL.add, ["CBk"],
                      [sk + ".1"])
             if k == 7:
                 break
-            o, tk = TW * (k - 1), ["TB%d" % k]
+            o, tk = TW * (k - 1), ["TB%d" % (k if k > 1 else 0)]
             n, e = divmod(k - 1, 4)
             a, z = 4 * C * n, "XTz%d" % n
             win = T.TB[:, o:o + 352]
-            act(T.XT[:, a + e:a + 512:4], win.indirect(T.OF[:, 0:8]), AF.Copy, ["OFa", z] + tk, ["XT0"])
+            act(T.XT[:, a + e + 832:a + 4 * C:4], win.indirect(T.OF[:, 0:8]), AF.Copy, ["OFa", z] + tk, ["XT0"])
             if k > 1:
                 ts(T.M48[:, 15::16], T.s48[:, 15::16], bc[:, 7:8], None, AL.add, None, ["s48", "b7"], ["M48"])
             sr = [sk + ".%d" % s for s in range(3)] + ["SMc"]
             ts(T.OF[:, 16:48], T.SM[:, w:w + SW].indirect(CWb), -0.5, 167.5, AL.mult, AL.add, sr + ["CW"], ["OFb"])
-            if k == 1:
-                quant_pt("xk", 0, 0, C, "XK")
-                earlier(k)
-            act(T.XT[:, a + e + 960:a + 4 * C:4], win.indirect(T.OF[:, 24:30]), AF.Copy, ["OFb", z] + tk, ["XT2"])
-            act(T.G48[:], T.TB[:, o + 352:o + TW].indirect(T.OF[:, 32:35]), AF.Identity, ["OFb"] + tk, ["G48"],
+            act(T.XT[:, a + e + 448:a + 832:4], win.indirect(T.OF[:, 24:30]), AF.Copy, ["OFb", z] + tk, ["XT2"])
+            act(T.G48[:], T.TB[:, o + 352:o + TW].indirect(T.OF[:, 32:35]), AF.Identity, ["OFb", "TB%d" % k], ["G48"],
                 bias=MID * KEY, scale=KEY)
-            quant("xx", C * n, C * n + 128, T.XT[:, a:a + 512], ["XT0", z])
-            cp(T.XT[:, a + e + 512:a + 960:4], win.indirect(T.OF[:, 16:23]), ["OFb", z] + tk, ["XT1"])
-            quant("xx", C * n + 128, C * n + C, T.XT[:, a + 512:a + 4 * C], ["XT1", "XT2", z])
+            quant("xe", 208, C, T.XT[:, a + 832:a + 4 * C], ["XT0", z])
             for pb in VB[(k + 1) % 2]:
-                mm(pb, C, "EX", 0, "xx", C * n, False, True, ["xx%d" % (C * n), "xx%d" % (C * n + 128)])
+                mm(pb, C, "EX", 0, "xe", 0, False, False, ["xe0", "xe208"])
+            cp(T.XT[:, a + e:a + 448:4], win.indirect(T.OF[:, 16:23]), ["OFb", z] + tk, ["XT1"])
+            quant("xl", 0, 208, T.XT[:, a:a + 832], ["XT1", "XT2", z])
+            for pb in VB[(k + 1) % 2]:
+                mm(pb, 208, "EX", 0, "xl", 0, False, True, ["xl0"])
             own()
+            if k == 4:
+                quant("xx", 0, C, T.XT[:, 0:4 * C], ["XT0", "XT1", "XT2", z])
             if t == 0 and k in (1, 2, 3):
                 quantc("EU0") if k == 1 else consts_ve(k - 1)
             if t == 0 and 1 < k < 6:
@@ -586,49 +614,73 @@ def rank_program(g, core, T, topo):
         cp(T.LS[:, 192:256], T.pb3[:, 0:64], ["pb3"], ["LSc"])
         ts(NL[:], T.LS[:].indirect(CP), -0.5, 167.5, AL.mult, AL.add, ["LS0", "LSa", "LSb", "LSc", "CP"], ["NL"])
         zk = ["NL"]
-        for b in range(4):
-            o, i = T.Z[:, b::4], pl("G", b).indirect(NL[:, 0:21])
-            if b < 1:
-                cp(o, i, ["G%d" % b] + zk, ["Z%d" % b])
+
+        def pick(h, b):
+            (a, e), (x, y) = HV[h], LV[h]
+            o, i = T.Z[:, 4 * a + b:4 * e:4], pl("G", b).indirect(NL[:, x:y])
+            if b < 2:
+                cp(o, i, ["G%d" % b] + zk, ["Z%d.%d" % (h, b)])
             else:
-                act(o, i, AF.Copy, ["G%d" % b] + zk, ["Z%d" % b])
-        cp(T.iW[:].indirect(NL[:, 0:21]), T.ji[:], ["ji"] + zk, ["iW"])
-        quant("z", 0, C, T.Z[:], ["Z%d" % b for b in range(4)])
+                act(o, i, AF.Copy, ["G%d" % b] + zk, ["Z%d.%d" % (h, b)])
+
+        def pack(h):
+            a, e = HV[h]
+            quant("z", a, e, T.Z[:, 4 * a:4 * e], ["Z%d.%d" % (h, b) for b in range(4)])
+
+        def layer(h, b, j):
+            a, e = HV[h]
+            pb = "pb%d" % (2 * b + j)
+            mm(pb, e - a, "wl", 128 * (b + 4 * j), "z", a, True, True, ["w0", "wsc", "z%d" % a])
+            if j:
+                act(pl("yt", b, a, e), T[pb][:, 0:e - a], AF.Copy, [pb], ["yt%d.%d" % (h, b)])
+
+        def best(h, b):
+            a, e = HV[h]
+            tt(pl("Ym", b, a, e), T["pb%d" % (2 * b)][:, 0:e - a], pl("yt", b, a, e), AL.max,
+               ["pb%d" % (2 * b), "yt%d.%d" % (h, b)], ["Y%d.%d" % (h, b)])
+
+        for h, b in ((0, 0), (0, 2), (0, 1), (0, 3), (1, 0), (1, 2), (1, 3)):
+            pick(h, b)
+        pack(0)
+        pick(1, 1)
         for b in range(4):
             for j in (1, 0):
-                mm("pb%d" % (2 * b + j), C, "wl", 128 * (b + 4 * j), "z", 0, True, True, ["w0", "wsc", "z0"])
-            act(pl("yt", b), T["pb%d" % (2 * b + 1)][:, 0:C], AF.Copy, ["pb%d" % (2 * b + 1)], ["yt%d" % b])
-
-        def best(b):
-            tt(pl("Ym", b), T["pb%d" % (2 * b)][:, 0:C], pl("yt", b), AL.max, ["pb%d" % (2 * b), "yt%d" % b],
-               ["Y%d" % b])
+                layer(0, b, j)
+        cp(T.iW[:].indirect(NL[:, 0:21]), T.ji[:], ["ji"] + zk, ["iW"])
+        pack(1)
+        act(T.tm[:], T.iW[:].indirect(ll[:]), AF.Copy, ["iW", lr], ["tm"])
+        for b in range(4):
+            best(0, b)
+        for b, j in ((0, 1), (1, 1), (0, 0), (2, 1), (1, 0), (3, 1), (2, 0), (3, 0)):
+            layer(1, b, j)
 
         def back(h, b, e):
             (a, z), (x, y) = HV[h], LV[h]
             o, i = T.Yp[:, 4 * a + b:4 * z:4], pl("Ym", b).indirect(T.ML[:, x:y])
-            rk = ["ML", "Y%d" % b]
+            rk = ["ML", "Y0.%d" % b, "Y1.%d" % b]
             if e == "ve":
                 ts(o, i, 0.03125, None, AL.mult, None, rk, ["Yp%d.%d" % (h, b)])
             else:
                 act(o, i, AF.Copy, rk, ["Yp%d.%d" % (h, b)], scale=0.03125)
 
-        cp(T.tm[:], T.iW[:].indirect(ll[:]), ["iW", lr], ["tm"])
-        to_list(T.tm[:], "tm", T.ML[:, 0:21], "ML")
-        best(0)
-        best(1)
-        back(0, 0, "ve")
-        best(2)
-        back(0, 1, "ve")
-        best(3)
-        for h, b, e in ((1, 0, "ac"), (0, 2, "ve"), (1, 1, "ac"), (0, 3, "ve"), (1, 2, "ac"), (1, 3, "ac")):
+        scan(T.sa[:], T.tm[:], T.MN[:], 4096.0, AL.min, AL.add, ["tm", "MN"], ["sa"])
+        best(1, 0)
+        ts(T.ML[:, 0:21], T.sa[:, 15::16], -512.0, None, AL.add, None, ["sa"], ["ML"])
+        for b in range(1, 4):
+            best(1, b)
+        for h, b, e in ((0, 0, "ac"), (0, 1, "ac"), (0, 2, "ve"), (1, 0, "ac"), (0, 3, "ve"), (1, 1, "ac"),
+                        (1, 2, "ve"), (1, 3, "ac")):
             back(h, b, e)
         for h in range(2):
             a, e = HV[h]
             quant("y%d" % t, a, e, T.Yp[:, 4 * a:4 * e], ["Yp%d.%d" % (h, b) for b in range(4)])
+        for h in range(2):
+            a, e = HV[h]
             k, sem = ["y%d%d" % (t, a)], ("ya%d", "yb%d")[h] % t
             send(pc, T["ry%dq" % t][:, a:e].bitcast(dt.uint8), T["y%dq" % t][:, a:e].bitcast(dt.uint8), sem, k)
-            send(pc, T["ry%ds" % t][:, a:e], T["y%ds" % t][:, a:e], sem, k)
-            arrives(["ry%d.%d" % (t, h)], sem, 2 * ne(t))
+            if h == 0:
+                send(pc, T["ry%ds" % t][:], T["y%ds" % t][:], sem, k + ["y%d160" % t])
+            arrives(["ry%d.%d" % (t, h)], sem, (2 - h) * ne(t))
         for h in range(2):
             a, e = HV[h]
             for b in range(4):

@@ -18,6 +18,7 @@ TILES = [(("d", 13, 12, 11), 336, "ERc"), ((10, 9, 8, 7), 160, "ERc"), ((6, 5, 4
          ((2, 1), 128, "ERc"), ((20, 19, 18, 17), 320, "ERb"), ((16, 15, 14), 256, "ERb")]
 LOW = 14
 ON_ACT, ON_VE = range(20, LOW - 1, -1), range(LOW - 1, 0, -1)
+AC_SUMS = {"pb0": 1, "pb1": 1}
 
 SCRATCH = {}
 
@@ -32,11 +33,12 @@ def _q(name, n):
 
 
 CONST = ["ERc", "ERb", "EL", "EU0", "EU1", "EU2", "EU3", "ETp", "EP0", "EX", "EK", "EP1"]
-BATCH = {"ERc": 2, "EL": 1, "EU0": 4, "ETp": 4, "EP1": 1}
+BATCH = {"ERc": 2, "EL": 1, "EU0": 4, "ETp": 2, "EX": 2, "EP1": 1}
 SHARE = {"xk": ("xx", C), "xe": ("xx", 2 * C), "xl": ("xx", 3 * C), "lf": ("lt", 160)}
 VB = [("pb0", "pb1"), ("pb6", "pb7")]
 _s("XT", 8 * C, "bfloat16")
-for _n in ("xin", "xt0", "xt1", "Z", "Yp", "PT", "ZT", "F", "G"):
+_s("ZT", 448, "bfloat16")
+for _n in ("xin", "xt0", "xt1", "Z", "Yp", "PT", "F", "G"):
     _s(_n, 4 * C, "bfloat16")
 for _n in ("uin", "vin", "ones", "W1"):
     _s(_n, 512, "bfloat16")
@@ -47,7 +49,7 @@ _s("Ym", 4 * C)
 _s("TT", TW, "bfloat16")
 _s("TB", 7 * TW, "bfloat16")
 _s("SM", 7 * SW)
-_s("J", 21 * 112)
+_s("J", 21 * 112, "bfloat16")
 _s("LS", 256)
 _s("JR", C)
 for _k in range(8):
@@ -65,8 +67,9 @@ for _t in range(R):
 for _t in range(R + 1):
     _q("x%d" % _t, C)
 for _n in ("jp", "ji", "d", "de", "k1", "K1", "nt", "MN", "MNx", "MH", "RH", "t1", "Hpb0", "Hpb1", "sa", "sx", "oW", "iW",
-           "tm", "tb", "Bx", "P0", "y1", "y2", "Vs", "df0", "df1", "ysb"):
+           "tm", "tb", "Bx", "P0", "y1", "y2", "Vs", "ysb"):
     _s(_n, C)
+_s("df", 3 * C)
 for _n in ("rm", "DS", "CB"):
     _s(_n, C, "bfloat16")
 _s("jk", 3 * C, "bfloat16")
@@ -241,38 +244,51 @@ def rank_program(g, core, T, topo):
     iota(pI[:, 16:32], [[1, 2], [16, 8]], 0, 0, "oI")
     sel(eb("ERc"), T.W1[:], [[-16, 8], [0, 64]], AL.is_ge, 0.0, 0, 1, ["W1"], "ERcb")
     sel(eb("ERc"), eb("ERc"), [[16, 8], [0, 64]], AL.is_ge, 0.0, 15, -1, ["ERcb"], "ERcb")
-    fill(T.ones[:], 1.0, "ones")
     ts(pI[:, 1:2], pI[:, 0:1], 15, None, AL.bitwise_and, None, ["pI"], ["pI1"])
     ts(pI[:, 2:3], pI[:, 0:1], 4, None, AL.arith_shift_right, None, ["pI"], ["pI2"])
     fill(bc[:, 25:26], TINY, "tiny")
-    cp(bc[:, 0:2], pI[:, 1:3], ["pI1", "pI2"], ["i"])
+    act(T.ones[:], T.W1[:], AF.Copy, ["W1"], ["ones"], scale=-1.0)
     act(T.rm[:], T.jp[:], AF.Sign, ["jp"], ["rm"])
     act(T.RH[:], T.rm[:], AF.Identity, ["rm"], ["RH"], bias=INF, scale=-2 * INF)
     for q, (blocks, w, _e) in enumerate(TILES):
-        z = min([16 * c for c in blocks if c != "d"]) if len(blocks) == 4 else 0
+        z = min([16 * c for c in blocks if c != "d"]) if len(blocks) > 2 else 0
         fill(T.RT[:, 4 * (start[q] + z):4 * (start[q] + w)], 0.0, "RTz%d" % q)
+        if len(blocks) == 3:
+            fill(T.RT[:, 4 * start[q] + 3:4 * (start[q] + z):4], 0.0, "RTz%d" % q)
         if q == 0:
+            cp(bc[:, 0:2], pI[:, 1:3], ["pI1", "pI2"], ["i"])
+        if q == 1:
             ts(T.d[:], T.jp[:], bc[:, 0:1], None, AL.subtract, None, ["jp", "i"], ["d"])
             cp(T.oU[:], pI[:, 16:32], ["oI"], ["oU"])
-        if q == 1:
+        if q == 2:
             ts(T.de[:], T.d[:], 0.0, None, AL.is_equal, None, ["d"], ["de"])
     act(T.k1[:], T.d[:], AF.Sign, ["d"], ["k1"], scale=-1.0)
     act(T.MH[:], T.de[:], AF.Identity, ["de"], ["MH"], bias=INF, scale=-2 * INF)
     act(T.k1[:], T.k1[:], AF.Abs, ["k1"], ["k1"], bias=2048.0, scale=5120.0)
+    i16, gr = bc[:, 0:1], bc[:, 1:2]
     quant("u", 0, 128, T.uin[:], ["uin"])
+    ts(bc[:, 3:4], i16, gr, None, AL.subtract, None, ["i"], ["b3"])
+    ts(bc[:, 6:7], T.de[:, 0:1], 13.0, gr, AL.mult, AL.add, ["de", "i"], ["b6"])
     cp(T.uuq[:].bitcast(dt.uint32), T.uq[:].bitcast(dt.uint32).indirect(T.oU[:]), ["u0", "oU"], ["uuc"])
     act(T.uus[:], T.us[:].indirect(T.oU[:]), AF.Copy, ["u0", "oU"], ["uup"])
+    ts(bc[:, 4:5], bc[:, 3:4], 0.0, CELL[1] - 1.0, AL.is_equal, AL.mult, ["b3"], ["b4"])
+    ts(bc[:, 5:6], bc[:, 3:4], 8.0, CELL[2] - 1.0, AL.is_equal, AL.mult, ["b3"], ["b5"])
     quant("x0", 0, C, T.xin[:], ["xin"])
+    ts(bc[:, 2:3], T.de[:, 15:16], -1024.0, i16, AL.mult, AL.add, ["de", "i"], ["b2"])
+    ts(CWa, bc[:, 3:4], 0.0, None, AL.not_equal, None, ["b3"], ["CW"])
+    ts(CL[:, 24:25], bc[:, 5:6], bc[:, 4:5], 1.0, AL.add, AL.add, ["b4", "b5"], ["CW"])
+    ts(CL[:, 25:26], i16, float(CELL[1]), float(CELL[2]), AL.mult, AL.min, ["i"], ["CW"])
+    ts(CC, T.de[:, 2:3], 7.0, bc[:, 6:7], AL.mult, AL.add, ["b6", "de"], ["CC"])
+    ts(bc[:, 7:8], T.de[:, 15:16], -2.0 ** 21, 2.0 ** 21, AL.mult, AL.add, ["de"], ["b7"])
+    ts(bc[:, 21:22], T.de[:, 15:16], -2.0 ** 21, 2.0 ** 21 + 2.0 ** 19, AL.mult, AL.add, ["de"], ["b21"])
     for pb in ("pb0", "pb7"):
         mm(pb, C, "uu", 0, "x0", 0, True, True, ["uuc", "uup", "x00"])
     act(eb("ERb"), eb("ERc"), AF.Copy, ["ERcb"], ["ERbb"], scale=0.5)
     act(T.MNx[:], T.k1[:], AF.Identity, ["k1"], ["MNx"], bias=-3072.0)
-    ts(bc[:, 2:3], T.de[:, 15:16], -1024.0, bc[:, 0:1], AL.mult, AL.add, ["de", "i"], ["b2"])
     for a, e, step, base in ((0, LOW, -16, 320 - 8 * len(ON_ACT)), (LOW, 21, 0, 160)):
         iota(sm[:, 64 + a:64 + e], [[step, e - a]], base + UP + 1024, 0, "c15", **f32)
     flat(T.J[:, 111:112], 0, "J0")
     ts(MC, sm[:, 64:85], bc[:, 2:3], None, AL.add, None, ["c15", "b2"], ["MC"])
-    quantc("ERc")
     send_x(0)
     iota(T.ji[:], [[1, C]], 0, 0, "ji", **f32)
     iota(pI[:, 32:53], [[16, 21]], 15, 0, "CXi")
@@ -283,19 +299,19 @@ def rank_program(g, core, T, topo):
                                           (0, 0, M32))):
         sel(bc[:, 13:15], bc[:, 13:15], [[8, 2]], AL.not_equal, big, -8 * k, 1, ["pc"], "pc")
         sel(eb("ETp", 1, k, 4), eb("ERc", 1, k, 4), [[0, 8], [pat, 16]], AL.is_ge, 0.0, base, 0, ["ERcb"], "ETpb")
-    iota(T.nt[:], [[-int(KEY), C]], 0, 0, "nt", **f32)
+    flat(T.ZT[:], 0, "ZT")
 
     def consts_gp():
-        flat(T.ZT[:], 0, "ZT")
-        dmas("sy", [(T.PT[:], T.ZT[:])], "zp", ["ZT"], ["PTz"])
+        iota(T.nt[:], [[-int(KEY), C]], 0, 0, "nt", **f32)
+        dmas("sy", [(T.PT[:, a:a + 448], T.ZT[:]) for a in range(0, 4 * C, 448)], "zp", ["ZT"], ["PTz"])
         sel(eb("EP1"), T.W1[:], [[0, 512]], AL.is_ge, 0.0, -16, 1, ["W1"], "EP1b")
         flat(T.TB[:, C:352], 0, "TBz")
         sel(eb("EP1"), eb("EP1"), [[0, 512]], AL.is_ge, 0.0, 31, -1, ["EP1b"], "EP1b")
-        iota(T.JR[:], [[-1, C]], int(BASE) + 335, 0, "JR", **f32)
-        for k, pat, base in ((0, -1, 1), (1, 1, -14)):
-            sel(eb("EP1", 1, k, 4), eb("EP1", 1, k, 4), [[0, 8], [pat, 16]], AL.is_ge, 0.0, base, 0, ["EP1b"], "EP1b")
         iota(T.J48[:, 0:16], [[0, 16]], int(BASE) + 335 - 2 ** 19 - 208, -1, "J48", **f32)
         iota(T.J48[:, 16:48], [[-112, 2], [0, 16]], int(BASE) + 335 - 2 ** 19, -1, "J48", **f32)
+        for k, pat, base in ((0, -1, 1), (1, 1, -14)):
+            sel(eb("EP1", 1, k, 4), eb("EP1", 1, k, 4), [[0, 8], [pat, 16]], AL.is_ge, 0.0, base, 0, ["EP1b"], "EP1b")
+        iota(T.JR[:], [[-1, C]], int(BASE) + 335, 0, "JR", **f32)
         for ap, val, key in ((T.TT[:, C:352], 0, "TTz"), (T.TT[:, 688:TW], 0, "TTz"),
                              (T.SM[:, 1::SW], -337, "SMc"), (T.SM[:, 2::SW], 0, "SMc"),
                              (T.LS[:, 21:32], 0, "LS0")):
@@ -307,6 +323,8 @@ def rank_program(g, core, T, topo):
     def consts_ac(q):
         if q == 0:
             act(T.MN[:], T.k1[:], AF.Identity, ["k1"], ["MN"], bias=-3072.0)
+            act(bc[:, 22:24], bc[:, 13:15], AF.Identity, ["pc"], ["pd"], bias=-2.0 ** 20)
+            act(T.MN[:, 15::16], T.MN[:, 15::16], AF.Identity, ["MN"], ["MN"], bias=1536.0)
         if q == 1:
             act(T.M48[:], T.k1[:, 0:48], AF.Identity, ["k1"], ["M48"], bias=-3072.0 * 2048, scale=2048.0)
             act(bc[:, 16:18], T.de[:, 0:15:14], AF.Copy, ["de"], ["b8"], scale=KEY - 1, accum_out=bc[:, 8:9])
@@ -318,21 +336,9 @@ def rank_program(g, core, T, topo):
             act(eb("EK", 1, 1, 4), T.ones[:, 0:128], AF.Copy, ["ones", "EKb"], ["EKb"], scale=0.0)
 
     def consts_ve(q):
-        i, gr = bc[:, 0:1], bc[:, 1:2]
+        i = i16
         if q == 0:
-            ts(bc[:, 3:4], i, gr, None, AL.subtract, None, ["i"], ["b3"])
             cp(CX, pI[:, 32:53], ["CXi"], ["CX"])
-            ts(bc[:, 22:24], bc[:, 13:15], -2.0 ** 20, None, AL.add, None, ["pc"], ["pd"])
-            ts(T.MN[:, 15::16], T.MN[:, 15::16], 1536.0, None, AL.add, None, ["MN"], ["MN"])
-            ts(bc[:, 4:5], bc[:, 3:4], 0.0, CELL[1] - 1.0, AL.is_equal, AL.mult, ["b3"], ["b4"])
-            ts(bc[:, 5:6], bc[:, 3:4], 8.0, CELL[2] - 1.0, AL.is_equal, AL.mult, ["b3"], ["b5"])
-            ts(bc[:, 6:7], T.de[:, 0:1], 13.0, gr, AL.mult, AL.add, ["de", "i"], ["b6"])
-            ts(bc[:, 7:8], T.de[:, 15:16], -2.0 ** 21, 2.0 ** 21, AL.mult, AL.add, ["de"], ["b7"])
-            ts(bc[:, 21:22], T.de[:, 15:16], -2.0 ** 21, 2.0 ** 21 + 2.0 ** 19, AL.mult, AL.add, ["de"], ["b21"])
-            ts(CWa, bc[:, 3:4], 0.0, None, AL.not_equal, None, ["b3"], ["CW"])
-            ts(CL[:, 24:25], bc[:, 5:6], bc[:, 4:5], 1.0, AL.add, AL.add, ["b4", "b5"], ["CW"])
-            ts(CL[:, 25:26], i, float(CELL[1]), float(CELL[2]), AL.mult, AL.min, ["i"], ["CW"])
-            ts(CC, T.de[:, 2:3], 7.0, bc[:, 6:7], AL.mult, AL.add, ["b6", "de"], ["CC"])
         e, m = sm[:, 88:90], [sm[:, 96 + 2 * s:98 + 2 * s] for s in range(3)]
         if q == 1:
             ts(e, sm[:, 94:96], bc[:, 3:4], None, AL.add, None, ["h2", "b3"], ["e"])
@@ -350,15 +356,17 @@ def rank_program(g, core, T, topo):
     def cells(c, a, e):
         return T.RT[:, slot[c] + 4 * a:slot[c] + 4 * e - 3:4]
 
-    def held(bank):
-        S, H = T[bank], "H" + bank
-        parts = ((16 * LOW, C, "h"), (0, 16 * LOW, "l"))
-        for a, e, k in parts:
-            tt(T.t1[:, a:e], S[:, a:e], T.MH[:, a:e], AL.max, [bank, "MH"], ["t1" + k])
-        for a, e, k in parts:
-            scan(T[H][:, a:e], T.RH[:, a:e], T.t1[:, a:e], INF, AL.max, AL.min, ["RH", "t1" + k], [H + k])
-        for a, e, k in parts:
-            tt(cells("d", a, e), S[:, a:e], T[H][:, a:e], AL.is_gt, [bank, H + k] + zs, ["RT.d"])
+    def held(bank, H, parts, steps=(0, 1, 2)):
+        S = T[bank]
+        for step in steps:
+            for a, e, ks in parts:
+                t1, hk = ["t1" + k for k in ks], [H + k for k in ks]
+                if step == 0:
+                    tt(T.t1[:, a:e], S[:, a:e], T.MH[:, a:e], AL.max, [bank, "MH"], t1)
+                elif step == 1:
+                    scan(T[H][:, a:e], T.RH[:, a:e], T.t1[:, a:e], INF, AL.max, AL.min, ["RH"] + t1, hk)
+                else:
+                    tt(cells("d", a, e), S[:, a:e], T[H][:, a:e], AL.is_gt, [bank] + hk + zs, ["RT.d"])
 
     def sums(c):
         scan(T.J[:, 112 * c + 112 - 8 * c:112 * c + 112], cells(c, 0, 8 * c), cells(c, 8 * c, 16 * c), 0.0,
@@ -367,10 +375,10 @@ def rank_program(g, core, T, topo):
     def block(bank, c):
         H = "H" + bank
         ts(cells(c, 0, 16 * c), T[bank][:, 0:16 * c], T[H][:, 16 * c + 15:16 * c + 16], None, AL.is_ge, None,
-           [bank, H + "l"] + zs, ["RT.%s" % c])
+           [bank, H + "l", H + "a", H + "b"] + zs, ["RT.%s" % c])
         if c == LOW - 1:
             scan(T.DS[:], T.rm[:], cells("d", 0, C), 0.0, AL.mult, AL.add, ["rm", "RT.d"], ["DS"])
-        else:
+        elif c + 1 < LOW - AC_SUMS[bank]:
             sums(c + 1)
 
     def places(bank, twin, done, hook):
@@ -378,18 +386,24 @@ def rank_program(g, core, T, topo):
 
         def diff(n):
             c = ON_ACT[n]
-            act(T["df%d" % (n % 2)][:, 0:16 * c], T[twin][:, 0:16 * c], AF.Identity, [twin, H + "h"],
-                ["df%d" % (n % 2)], bias=T[H][:, 16 * c + 15:16 * c + 16], scale=-1.0)
+            act(pl("df", n % 3, 0, 16 * c), T[twin][:, 0:16 * c], AF.Identity, [twin, H + "h"],
+                ["df%d" % (n % 3)], bias=T[H][:, 16 * c + 15:16 * c + 16], scale=-1.0)
 
         diff(0)
         for n, c in enumerate(ON_ACT):
             if n + 1 < len(ON_ACT):
                 diff(n + 1)
-            act(cells(c, 0, 16 * c), T["df%d" % (n % 2)][:, 0:16 * c], AF.Sign, ["df%d" % (n % 2), "tiny"] + zs,
+            act(cells(c, 0, 16 * c), pl("df", n % 3, 0, 16 * c), AF.Sign, ["df%d" % (n % 3), "tiny"] + zs,
                 ["RT.%s" % c, "AC"], bias=bc[:, 25:26], scale=-1.0, accum_out=sm[:, 100 + c:101 + c])
-        act(T.J[:, 112 * LOW + 111::112], sm[:, 100 + LOW:121], AF.Copy, ["AC"], ["J%d" % c for c in ON_ACT],
-            scale=0.5)
-        hook(-1)
+
+        def sums_ac():
+            low = LOW - AC_SUMS[bank]
+            for n, c in enumerate(range(LOW - 1, low - 1, -1)):
+                act(pl("jk", n, 0, 16 * c), cells(c, 0, 16 * c), AF.Copy, ["RT.%s" % c], ["AC", "jk%d" % n], scale=2.0,
+                    accum_out=sm[:, 100 + c:101 + c])
+            act(T.J[:, 112 * low + 111::112], sm[:, 100 + low:121], AF.Copy, ["AC"],
+                ["J%d" % c for c in range(low, 21)], scale=0.5)
+            hook(-1)
 
         def count(q):
             blocks, w, st = TILES[q]
@@ -397,17 +411,25 @@ def rank_program(g, core, T, topo):
                   ["RT.%s" % c for c in blocks] + ["RTz%d" % q])
             mm("pb2", w, st, 0, "rq", start[q], q == 0, q == 5, ["rq%d" % start[q]])
 
+        last = [q for q in range(6) if 1 in TILES[q][0]][0]
         for c in ON_VE[done:]:
             block(bank, c)
-            if c in (10, 6, 2):
-                count({10: 0, 6: 1, 2: 2}[c])
-        hook(1)
-        count(4)
+            if c == LOW - 3:
+                sums_ac()
+            if c == 4:
+                hook(1)
+            for q in range(last):
+                if c == TILES[q][0][-1] - 1:
+                    count(q)
+        count(last + 1)
         sums(1)
-        count(3)
+        hook(3)
+        count(last)
         tt(X2, T.DS[:, 15::16], MC, AL.add, ["DS", "MC"], ["X2"])
         hook(0)
-        count(5)
+        for q in range(last + 2, 6):
+            count(q)
+        hook(4)
         tt(T.MNx[:, 15::16], T.J[:, 111::112], X2, AL.add, ["X2"] + ["J%d" % c for c in range(21)], ["MNx"])
         hook(2)
         scan(T.sx[:], T.pb2[:, 0:C], T.MNx[:], 4096.0, AL.min, AL.add, ["pb2", "MNx"], ["sx"])
@@ -431,17 +453,17 @@ def rank_program(g, core, T, topo):
         pc, ls, ll, NL = part(t), T["ls%d" % t], T["ll%d" % t], T.NL
         lk, lr, X = "ls%d" % t, "ll%d" % t, "x%d" % t
         def ahead(q):
-            if q == -1 and t == 0:
-                consts_ac(0)
             if q == 1:
                 for pb in ("pb1", "pb6"):
                     mm(pb, C, "uu", 128, "rx%d" % t, 0, True, True, ["uuc", "uup", "rx%d" % t])
-            if q == 0:
-                held("pb1")
+            if q in (3, 0, 4):
+                held("pb1", "Hpb1", ((0, C, "hlab"),), [(3, 0, 4).index(q)])
             if q == 2:
                 block("pb1", ON_VE[0])
 
-        held("pb0")
+        held("pb0", "Hpb0", ((16 * LOW, C, "h"), (HV[1][0] if t else 0, 16 * LOW, "l")))
+        if t == 0:
+            quantc("ERc")
         places("pb0", "pb7", 0, ahead)
         block("pb1", ON_VE[1])
         sx = T.sx[:, 15::16]
@@ -449,11 +471,10 @@ def rank_program(g, core, T, topo):
         send(pc, ll[:], ls[:], "la%d" % t, [lk])
         arrives([lr], "la%d" % t, ne(t))
         ts(T.L0s[:, 0:21], sx, -1.0, 335.0 + UP, AL.mult, AL.add, ["sx"], ["L0s"])
-        ts(T.LS[:, 0:21], sx, 2.0, -335.0 - 2 * UP, AL.mult, AL.add, ["sx"], ["LSa"])
         dmas("sy", [(T.L0f[16 * k:16 * k + 16, :], T.L0s[0:16, :]) for k in range(8)], "l0", ["L0s", "L0z"], ["L0f"])
         if t == 0:
             consts_gp()
-        dmas("sy", [(T.XT[:, 4 * C * n:4 * C * (n + 1)], T.ZT[:]) for n in range(2)], "zx", ["ZT"], ["XTz0", "XTz1"])
+        dmas("sy", [(T.XT[:, a:a + 448], T.ZT[:]) for a in range(0, 8 * C, 448)], "zx", ["ZT"], ["XTz0", "XTz1"])
         if t == 0:
             for b in range(4):
                 sel(eb("EU%d" % b), T.ones[:], [[1, 512]], AL.is_equal, 0.0, -b, -4, ["ones"], "EU%db" % b)
@@ -476,6 +497,7 @@ def rank_program(g, core, T, topo):
 
         def inverse(q):
             if q == -1 and t == 0:
+                consts_ac(0)
                 consts_ac(1)
             if q == -1 and t:
                 for e in ("pe", "ac"):
@@ -493,7 +515,7 @@ def rank_program(g, core, T, topo):
         places("pb1", "pb6", 2, inverse)
         ts(T.IL[:, 0:21], T.sa[:, 15::16], -512.0, None, AL.add, None, ["sa"], ["IL"])
         tt(T.Bx[:], T.sx[:].indirect(CX), T.de[:], AL.mult, ["sx", "CX", "de"], ["Bx"])
-        ts(T.M48[:, 15::16], T.jp[:, 0:48:16], bc[:, 21:22], None, AL.add, None, ["jp", "b21", "M48"], ["M48"])
+        tt(T.s48[:], T.nt[:].indirect(T.L0[:, 32:35]), T.J48[:], AL.add, ["nt", "L0", "J48"], ["s48"])
         if t == 0:
             quantc("ETp")
             quantc("EP1")
@@ -508,21 +530,21 @@ def rank_program(g, core, T, topo):
             quant_pt("pp", HV[h][0], HV[h][0], HV[h][1] - HV[h][0], "PT%d" % h)
         pk = ["pp0", "pp160"]
         mm("pb3", C, "EP0", 0, "pp", 0, True, True, pk)
-        mm("pb4", C, "ETp", 0, "pp", 0, True, True, pk)
         mm("pb5", C, "ERc", 0, "pp", 0, True, True, pk)
+        mm("pb4", C, "ETp", 0, "pp", 0, True, True, pk)
         mm("pb7", C, "EP1", 0, "pp", 0, True, True, pk)
         tt(T.y1[:], T.nt[:].indirect(T.L0[:, 0:21]), T.JR[:], AL.add, ["nt", "L0", "JR"], ["y1"])
-        tt(T.s48[:], T.nt[:].indirect(T.L0[:, 32:35]), T.J48[:], AL.add, ["nt", "L0", "J48"], ["s48"])
-        act(T.TT[:, 0:C], T.pb4[:, 0:C], AF.Copy, ["pb4"], ["TTp"], scale=-1.0)
         act(T.TT[:, 352:688], T.pb5[:, 0:C], AF.Identity, ["pb5"], ["TTf"], bias=-MID, scale=-1.0)
+        act(T.TT[:, 0:C], T.pb4[:, 0:C], AF.Copy, ["pb4"], ["TTp"], scale=-1.0)
         act(T.TB[:, 0:C], T.pb7[:, 0:C], AF.Copy, ["pb7", "TBz"], ["TB0"], scale=-1.0)
         for k in range(1, 8):
             a = 352 if k == 1 else 0
             dmas("sy", [(T.TB[16 * j:16 * j + 16, TW * (k - 1) + a:TW * k], T.TT[16 * k:16 * k + 16, a:TW])
-                        for j in range(8)], "tb%d" % k, ["TTp", "TTf", "TTz"], ["TB%d" % k])
+                        for j in range(8)], "tb%d" % k, ["TTf", "TTz"] + ["TTp"] * (k > 1), ["TB%d" % k])
         ts(T.P0[:], T.pb3[:, 0:C], -KEY, None, AL.mult, None, ["pb3"], ["P0"])
+        ts(T.M48[:, 15::16], T.jp[:, 0:48:16], bc[:, 21:22], None, AL.add, None, ["jp", "b21", "M48"], ["M48"])
         if t == 0:
-            quant("xe", 0, 208, T.XT[:, 0:832], ["XTz0"])
+            quantc("EX")
         tt(T.G48[:], T.P0[:].indirect(T.L0[:, 32:35]), T.s48[:], AL.add, ["P0", "L0", "s48"], ["G48"])
         tt(T.K1[:], T.P0[:].indirect(T.L0[:, 0:21]), T.y1[:], AL.add, ["P0", "L0", "y1"], ["K1"])
 
@@ -536,6 +558,8 @@ def rank_program(g, core, T, topo):
                     mm(pb, C, "EX", 0, "xx", 0, False, False, ["xx0"])
 
         own()
+        if t == 0:
+            quant("xe", 0, 208, T.XT[:, 0:832], ["XTz0"])
         for k in range(1, 8):
             w = SW * (k - 1)
             sk = "SM%d" % k
@@ -547,7 +571,7 @@ def rank_program(g, core, T, topo):
                 unpack(k - 2, "pe")
             for s in (0, 2, 1)[:3 if k == 1 else 2]:
                 c = w + CELL[s]
-                act(pl("jk", s), V, AF.Sign, [vk, "s48"], [sk + ".%d" % s], bias=T.s48[:, 16 * s + 15:16 * s + 16],
+                act(pl("jk", s), V, AF.Sign, [vk, "s48"], [sk + ".%d" % s, "jk%d" % s], bias=T.s48[:, 16 * s + 15:16 * s + 16],
                     scale=-1.0, accum_out=T.SM[:, c:c + 1])
             if k == 1:
                 ts(T.y1[:], V, bc[:, 14:15], bc[:, 23:24], AL.add, AL.subtract, ["K1", "pc", "pd"], ["y1"])
@@ -591,13 +615,14 @@ def rank_program(g, core, T, topo):
                 mm(pb, 208, "EX", 0, "xl", 0, False, True, ["xl0"])
             own()
             if k == 4:
+                ts(T.LS[:, 0:21], T.L0f[:, 0:21], -2.0, 335.0, AL.mult, AL.add, ["L0f"], ["LSa"])
                 quant("xx", 0, C, T.XT[:, 0:4 * C], ["XT0", "XT1", "XT2", z])
             if t == 0 and k in (1, 2, 3):
                 quantc("EU0") if k == 1 else consts_ve(k - 1)
             if t == 0 and 1 < k < 6:
-                unpack(k - 2, "ve")
-            if t == 0 and k > 2 or t and k == 2:
-                sort(k - 3 if t == 0 else 3)
+                unpack(k - 2, "ac" if k < 4 else "ve")
+            if t == 0 and k > 3 or t and k == 2:
+                sort(k - 4 if t == 0 else 3)
             if k > 4:
                 piece(k - 5, 0, 160, T.SM[:, 0:5 * SW].indirect(CB),
                       ["SM%d.%d" % (a, s) for a in range(1, 6) for s in range(3)] + ["CB"], "LT")
@@ -609,6 +634,8 @@ def rank_program(g, core, T, topo):
         act(T.LS[:, 32:192], T.pb2[:, 0:160], AF.Copy, ["pb2"], ["LSb"])
         if t == R - 1:
             act(T.Vs[:], T[VB[1][0]][:, 0:C], AF.Copy, [VB[1][0]], ["Vs"])
+        if t == 0:
+            sort(3)
         quant_pt("lf", 0, 160, 128, "LF")
         mm("pb3", 128, "EL", 0, "lf", 0, True, True, ["lf0"])
         cp(T.LS[:, 192:256], T.pb3[:, 0:64], ["pb3"], ["LSc"])
@@ -618,7 +645,7 @@ def rank_program(g, core, T, topo):
         def pick(h, b):
             (a, e), (x, y) = HV[h], LV[h]
             o, i = T.Z[:, 4 * a + b:4 * e:4], pl("G", b).indirect(NL[:, x:y])
-            if b < 2:
+            if b < 2 - h:
                 cp(o, i, ["G%d" % b] + zk, ["Z%d.%d" % (h, b)])
             else:
                 act(o, i, AF.Copy, ["G%d" % b] + zk, ["Z%d.%d" % (h, b)])
@@ -631,7 +658,9 @@ def rank_program(g, core, T, topo):
             a, e = HV[h]
             pb = "pb%d" % (2 * b + j)
             mm(pb, e - a, "wl", 128 * (b + 4 * j), "z", a, True, True, ["w0", "wsc", "z%d" % a])
-            if j:
+            if j and (h, b) == (1, 0):
+                cp(pl("yt", b, a, e), T[pb][:, 0:e - a], [pb], ["yt%d.%d" % (h, b)])
+            elif j:
                 act(pl("yt", b, a, e), T[pb][:, 0:e - a], AF.Copy, [pb], ["yt%d.%d" % (h, b)])
 
         def best(h, b):
@@ -704,10 +733,16 @@ def rank_program(g, core, T, topo):
                 else:
                     act(o, T[pb][:, 0:e - a], AF.Copy, [pb], ["xt%d.%d" % (h, b)])
             quant(N, a, e, xt[:, 4 * a:4 * e], ["xt%d.%d" % (h, b) for b in range(4)])
+            if t < R - 1:
+                send(part(t + 1), T["r" + N + "q"][:, a:e].bitcast(dt.uint8), T[N + "q"][:, a:e].bitcast(dt.uint8),
+                     "xa%d" % (t + 1), [N + str(a)])
         if t < R - 1:
+            mm("pb1", HV[0][1], "uu", 0, N, 0, True, True, [N + "0"])
             for pb in ("pb0", "pb7"):
                 mm(pb, C, "uu", 0, N, 0, True, True, [N + "0", N + "160"])
-            send_x(t + 1)
+            send(part(t + 1), T["r" + N + "s"][:], T[N + "s"][:], "xa%d" % (t + 1), [N + "0", N + "160"])
+            arrives(["r" + N], "xa%d" % (t + 1), 3 * ne(t + 1))
+            held("pb1", "Hpb0", ((0, 80, "a"), (80, HV[0][1], "b")))
     for h in range(2):
         a, e = HV[h]
         pb, nk = "pb%d" % h, ["x2%d" % a]

from concourse.mybir import dt, AluOpType, ActivationFunctionType

AL, AF = AluOpType, ActivationFunctionType
C, R = 336, 2
HV = [(0, 160), (160, 336)]
LV = [(0, 10), (10, 21)]
INF = float(2 ** 90)
TINY = float(2.0 ** -120)
M32 = 1.5 * 2.0 ** 28
M1 = 1.5 * 2.0 ** 23
KEY = 385.0
BASE = float(2 ** 18)
UP = 128
MID = 168.0 + UP
SW, TW = 192, 704
CELL = (0, 183, 184)
TILES = [(("d", 13, 12, 11), 336, "ERc"), ((10, 9, 8, 7), 160, "ERc"), ((6, 5, 4, 3), 128, "ERc"),
         ((2, 1), 128, "ERc"), ((20, 19, 18, 17), 320, "ERb"), ((16, 15, 14), 256, "ERb")]
LOW = 14
ON_ACT, ON_VE = range(20, LOW - 1, -1), range(LOW - 1, 0, -1)
AC_SUMS = {"pb0": 1, "pb1": 1}

SCRATCH = {}


def _s(name, n, d="float32", where="sbuf"):
    SCRATCH[name] = (where, [128, n], d)


def _q(name, n):
    _s(name + "q", n, "float8_e4m3fn_x4")
    _s(name + "s", n, "uint8")


CONST = ["ERc", "ERb", "EL", "EU0", "EU1", "EU2", "EU3", "ETp", "EP0", "EX", "EK", "EP1"]
BATCH = {"ERc": 2, "EL": 1, "EU0": 4, "ETp": 2, "EX": 2, "EP1": 1}
SHARE = {"xk": ("xx", C), "xe": ("xx", 2 * C), "xl": ("xx", 3 * C), "lf": ("lt", 160)}
VB = [("pb0", "pb1"), ("pb6", "pb7")]
_s("XT", 8 * C, "bfloat16")
_s("ZT", 448, "bfloat16")
for _n in ("xin", "xt0", "xt1", "Z", "Yp", "PT", "F", "G"):
    _s(_n, 4 * C, "bfloat16")
for _n in ("uin", "vin", "ones", "W1"):
    _s(_n, 512, "bfloat16")
_s("Eb", 512 * len(CONST), "bfloat16")
_q("E", 128 * len(CONST))
_s("yt", 4 * C)
_s("Ym", 4 * C)
_s("TT", TW, "bfloat16")
_s("TB", 7 * TW, "bfloat16")
_s("SM", 7 * SW)
_s("J", 21 * 112, "bfloat16")
_s("LS", 256)
_s("JR", C)
for _k in range(8):
    _s("pb%d" % _k, 512, "float32", "psum")
for _n, _k in (("u", 128), ("v", 128), ("uu", 256), ("wl", 1024), ("z", C), ("pp", C), ("xx", 3 * C + 208),
               ("lt", 288), ("rq", sum(_t[1] for _t in TILES))):
    _q(_n, _k)
_s("RT", 4 * sum(_t[1] for _t in TILES), "bfloat16")
for _t in range(R):
    _q("rx%d" % _t, C)
    _q("ry%d" % _t, C)
    _q("y%d" % _t, C)
    _s("ls%d" % _t, 21, "uint16")
    _s("ll%d" % _t, 21, "uint16")
for _t in range(R + 1):
    _q("x%d" % _t, C)
for _n in ("jp", "ji", "d", "de", "k1", "K1", "nt", "MN", "MNx", "MH", "RH", "t1", "Hpb0", "Hpb1", "sa", "sx", "oW", "iW",
           "tm", "tb", "Bx", "P0", "y1", "y2", "Vs", "ysb"):
    _s(_n, C)
_s("df", 3 * C)
for _n in ("rm", "DS", "CB"):
    _s(_n, C, "bfloat16")
_s("jk", 3 * C, "bfloat16")
for _n in ("M48", "G48", "s48", "J48"):
    _s(_n, 48)
_s("sm", 128)
_s("pI", 128, "int32")
_s("CL", 64, "uint16")
_s("oU", 16, "uint16")
_s("OF", 48, "uint16")
_s("NL", 32, "uint16")
for _n in ("ML", "IL"):
    _s(_n, 22, "uint16")
_s("L0", 48, "uint16")
_s("L0s", 24)
_s("L0f", 24)
_s("bc", 32)

SEMAPHORES = ["ve", "ac", "pe", "gp", "lx", "lu", "lv", "lw", "lz", "out", "loc", "l0", "zp", "zx"]
SEMAPHORES += ["tb%d" % _g for _g in range(1, 8)]
SEMAPHORES += ["%s%d" % (a, t) for a in ("xa", "la", "ya", "yb") for t in range(R)]


def rank_program(g, core, T, topo):
    r = T.rank_of(core)
    if r is None:
        return
    queue = {"ve": g.vector, "ac": g.scalar, "pe": g.tensor, "gp": g, "sy": g.sync}
    tick = {"ve": 0, "ac": 0, "pe": 0, "gp": 0}
    known = {e: {} for e in queue}
    wr, rd, dcount, arr, sent = {}, {}, {}, {}, [0]

    def deps(e, reads, writes):
        want = {}
        for k in reads:
            for s, v in wr.get(k, {}).items():
                want[s] = max(v, want.get(s, 0))
        for k in list(writes) + [k for k in reads if k[:2] == "pb"]:
            for tab in (wr, rd):
                for s, v in tab.get(k, {}).items():
                    if s != e or tab is rd and e != "pe" and k in writes:
                        want[s] = max(v, want.get(s, 0))
        for s, v in want.items():
            if known[e].get(s, 0) < v:
                queue[e].wait_ge(T.sem[s], v)
                known[e][s] = v

    def op(e, fn, reads, writes):
        deps(e, reads, writes)
        fn(queue[e]).then_inc(T.sem[e], 1)
        tick[e] += 1
        for k in reads:
            rd.setdefault(k, {})[e] = tick[e]
        for k in writes:
            wr.setdefault(k, {})[e] = tick[e]

    def dmas(e, pairs, sem, reads=(), writes=()):
        deps(e, reads, writes)
        for out, in_ in pairs:
            queue[e].dma_start(out, in_).then_inc(T.sem[sem], 16)
        dcount[sem] = dcount.get(sem, 0) + 16 * len(pairs)
        for k in writes:
            wr.setdefault(k, {})[sem] = dcount[sem]
        if sem != "out":
            for k in reads:
                rd.setdefault(k, {})[sem] = dcount[sem]

    def tt(out, a, b, o, reads, writes):
        op("ve", lambda q: q.tensor_tensor(out, a, b, o), reads, writes)

    def ts(out, a, s1, s2, o0, o1, reads, writes):
        if o1 is None:
            op("ve", lambda q: q.tensor_scalar(out, a, s1, None, o0), reads, writes)
        else:
            op("ve", lambda q: q.tensor_scalar(out, a, s1, s2, o0, o1), reads, writes)

    def cp(out, a, reads, writes):
        op("ve", lambda q: q.tensor_copy(out, a), reads, writes)

    def fill(ap, c, key):
        op("ve", lambda q: q.memset(ap, c), [], [key])

    def scan(out, a, b, ini, o0, o1, reads, writes):
        op("ve", lambda q: q.tensor_tensor_scan(out, a, b, ini, o0, o1), reads, writes)

    def act(out, a, f, reads, writes, **k):
        op("ac", lambda q: q.activation(out, a, f, **k), reads, writes)

    def at(n):
        return ("E", 128 * CONST.index(n)) if n in CONST else SHARE.get(n, (n, 0))

    def eb(n, m=1, a=0, step=1):
        k = 512 * CONST.index(n)
        return T.Eb[:, k + a:k + 512 * m:step]

    def pl(n, b, a=0, e=C):
        return T[n][:, C * b + a:C * b + e]

    def quant(name, a, b, src, reads):
        n, o = at(name)
        op("ve", lambda q: q.quantize_mx(T[n + "q"][:, o + a:o + b], T[n + "s"][:, o + a:o + b], src),
           reads, [name + str(a)])

    def quantc(name):
        k, m = CONST.index(name), BATCH[name]
        quant(name, 0, 128 * m, eb(name, m), [n + "b" for n in CONST[k:k + m]])

    def mm(bank, n, st, sa, mv, ma, start, stop, reads):
        w, o = at(st)
        o += sa
        mv, mo = at(mv)
        ma += mo
        if st in CONST:
            reads = reads + [[b for b in CONST[:CONST.index(st) + 1] if b in BATCH][-1] + "0"]
        op("pe", lambda q: q.matmul_mx(T[bank][:, 0:n], T[w + "q"][:, o:o + 128], T[w + "s"][:, o:o + 128],
                                       T[mv + "q"][:, ma:ma + n], T[mv + "s"][:, ma:ma + n], start, stop),
           reads, [bank])

    def send(pc, out, in_, rsem, reads):
        deps("gp", reads, ())
        rid, pid, _e = topo.addr(pc)
        g.remote_dma(out, in_, T.sem[rsem], T.sem.loc, pid, rid, topo.mask(core, pc))
        sent[0] += len(topo.engines(core, pc))

    def arrives(keys, sem, val):
        for k in keys:
            wr.setdefault(k, {})[sem] = val
        arr[sem] = val

    def part(t):
        return T.cores[r ^ (1 << t)]

    def ne(t):
        return len(topo.engines(part(t), core))

    def send_x(t):
        send(part(t), T["rx%dq" % t][:].bitcast(dt.uint8), T["x%dq" % t][:].bitcast(dt.uint8), "xa%d" % t,
             ["x%d0" % t, "x%d160" % t])
        send(part(t), T["rx%ds" % t][:], T["x%ds" % t][:], "xa%d" % t, ["x%d0" % t])
        arrives(["rx%d" % t], "xa%d" % t, 2 * ne(t))

    dmas("sy", [(T.xin[:], T.x[:])], "lx", (), ["xin"])
    dmas("ac", [(T.uin[:], T.u[:])], "lu", (), ["uin"])
    dmas("sy", [(T.wlq[:].bitcast(dt.uint8), T.wc[:])], "lw", ["xin"], ["w0"])
    dmas("sy", [(T.vin[:], T.v[:])], "lv", (), ["vin"])
    dmas("sy", [(T.wls[:], T.ws[:])], "lz", (), ["wsc"])
    f32 = dict(allow_small_or_imprecise_dtypes=True)
    bc, sm, pI, CL = T.bc, T.sm, T.pI, T.CL
    CX, CWa, CWb, CC = CL[:, 0:21], CL[:, 22:23], CL[:, 24:26], CL[:, 26:27]
    CP, CB, CF = CL[:, 30:32], CL[:, 32:42], CL[:, 42:46]
    MC, X2 = sm[:, 8:29], sm[:, 32:53]
    start, slot, o = {}, {}, 0
    for q, (blocks, w, _e) in enumerate(TILES):
        start[q] = o
        for k, c in enumerate(blocks):
            slot[c] = 4 * o + k
        o += w
    zs = ["RTz%d" % q for q in start]

    def iota(ap, pat, base, cm, key, **k):
        op("gp", lambda q: q.iota(ap, pat, base, cm, **k), [], [key])

    def flat(ap, val, key):
        iota(ap, [[0, ap.shape[1]]], val, 0, key, **f32)

    def sel(ap, src, pat, o, fl, base, cm, reads, key):
        op("gp", lambda q: q.affine_select(ap, src, pat, o, fl, base, cm), reads, [key])

    fill(T.W1[:], -1.0, "W1")
    iota(pI[:, 0:1], [[1, 1]], 0, 1, "pI")
    iota(T.jp[:], [[0, 21], [1, 16]], 0, 0, "jp", **f32)
    iota(pI[:, 16:32], [[1, 2], [16, 8]], 0, 0, "oI")
    sel(eb("ERc"), T.W1[:], [[-16, 8], [0, 64]], AL.is_ge, 0.0, 0, 1, ["W1"], "ERcb")
    sel(eb("ERc"), eb("ERc"), [[16, 8], [0, 64]], AL.is_ge, 0.0, 15, -1, ["ERcb"], "ERcb")
    ts(pI[:, 1:2], pI[:, 0:1], 15, None, AL.bitwise_and, None, ["pI"], ["pI1"])
    ts(pI[:, 2:3], pI[:, 0:1], 4, None, AL.arith_shift_right, None, ["pI"], ["pI2"])
    fill(bc[:, 25:26], TINY, "tiny")
    act(T.ones[:], T.W1[:], AF.Copy, ["W1"], ["ones"], scale=-1.0)
    act(T.rm[:], T.jp[:], AF.Sign, ["jp"], ["rm"])
    act(T.RH[:], T.rm[:], AF.Identity, ["rm"], ["RH"], bias=INF, scale=-2 * INF)
    for q, (blocks, w, _e) in enumerate(TILES):
        z = min([16 * c for c in blocks if c != "d"]) if len(blocks) > 2 else 0
        fill(T.RT[:, 4 * (start[q] + z):4 * (start[q] + w)], 0.0, "RTz%d" % q)
        if len(blocks) == 3:
            fill(T.RT[:, 4 * start[q] + 3:4 * (start[q] + z):4], 0.0, "RTz%d" % q)
        if q == 0:
            cp(bc[:, 0:2], pI[:, 1:3], ["pI1", "pI2"], ["i"])
        if q == 1:
            ts(T.d[:], T.jp[:], bc[:, 0:1], None, AL.subtract, None, ["jp", "i"], ["d"])
            cp(T.oU[:], pI[:, 16:32], ["oI"], ["oU"])
        if q == 2:
            ts(T.de[:], T.d[:], 0.0, None, AL.is_equal, None, ["d"], ["de"])
    act(T.k1[:], T.d[:], AF.Sign, ["d"], ["k1"], scale=-1.0)
    act(T.MH[:], T.de[:], AF.Identity, ["de"], ["MH"], bias=INF, scale=-2 * INF)
    act(T.k1[:], T.k1[:], AF.Abs, ["k1"], ["k1"], bias=2048.0, scale=5120.0)
    i16, gr = bc[:, 0:1], bc[:, 1:2]
    quant("u", 0, 128, T.uin[:], ["uin"])
    ts(bc[:, 3:4], i16, gr, None, AL.subtract, None, ["i"], ["b3"])
    ts(bc[:, 6:7], T.de[:, 0:1], 13.0, gr, AL.mult, AL.add, ["de", "i"], ["b6"])
    cp(T.uuq[:].bitcast(dt.uint32), T.uq[:].bitcast(dt.uint32).indirect(T.oU[:]), ["u0", "oU"], ["uuc"])
    act(T.uus[:], T.us[:].indirect(T.oU[:]), AF.Copy, ["u0", "oU"], ["uup"])
    ts(bc[:, 4:5], bc[:, 3:4], 0.0, CELL[1] - 1.0, AL.is_equal, AL.mult, ["b3"], ["b4"])
    ts(bc[:, 5:6], bc[:, 3:4], 8.0, CELL[2] - 1.0, AL.is_equal, AL.mult, ["b3"], ["b5"])
    quant("x0", 0, C, T.xin[:], ["xin"])
    ts(bc[:, 2:3], T.de[:, 15:16], -1024.0, i16, AL.mult, AL.add, ["de", "i"], ["b2"])
    ts(CWa, bc[:, 3:4], 0.0, None, AL.not_equal, None, ["b3"], ["CW"])
    ts(CL[:, 24:25], bc[:, 5:6], bc[:, 4:5], 1.0, AL.add, AL.add, ["b4", "b5"], ["CW"])
    ts(CL[:, 25:26], i16, float(CELL[1]), float(CELL[2]), AL.mult, AL.min, ["i"], ["CW"])
    ts(CC, T.de[:, 2:3], 7.0, bc[:, 6:7], AL.mult, AL.add, ["b6", "de"], ["CC"])
    ts(bc[:, 7:8], T.de[:, 15:16], -2.0 ** 21, 2.0 ** 21, AL.mult, AL.add, ["de"], ["b7"])
    ts(bc[:, 21:22], T.de[:, 15:16], -2.0 ** 21, 2.0 ** 21 + 2.0 ** 19, AL.mult, AL.add, ["de"], ["b21"])
    for pb in ("pb0", "pb7"):
        mm(pb, C, "uu", 0, "x0", 0, True, True, ["uuc", "uup", "x00"])
    act(eb("ERb"), eb("ERc"), AF.Copy, ["ERcb"], ["ERbb"], scale=0.5)
    act(T.MNx[:], T.k1[:], AF.Identity, ["k1"], ["MNx"], bias=-3072.0)
    for a, e, step, base in ((0, LOW, -16, 320 - 8 * len(ON_ACT)), (LOW, 21, 0, 160)):
        iota(sm[:, 64 + a:64 + e], [[step, e - a]], base + UP + 1024, 0, "c15", **f32)
    flat(T.J[:, 111:112], 0, "J0")
    ts(MC, sm[:, 64:85], bc[:, 2:3], None, AL.add, None, ["c15", "b2"], ["MC"])
    send_x(0)
    iota(T.ji[:], [[1, C]], 0, 0, "ji", **f32)
    iota(pI[:, 32:53], [[16, 21]], 15, 0, "CXi")
    flat(T.L0s[:, 21:24], 0, "L0z")
    flat(bc[:, 13:15], 0, "pc")
    sel(eb("EP0"), T.W1[:], [[0, 512]], AL.is_ge, 0.0, 15, -1, ["W1"], "EP0b")
    for k, (pat, base, big) in enumerate(((-1, 1, 1.5 * 2.0 ** 43), (1, -14, 1.5 * 2.0 ** 38), (0, 0, 1.5 * 2.0 ** 33),
                                          (0, 0, M32))):
        sel(bc[:, 13:15], bc[:, 13:15], [[8, 2]], AL.not_equal, big, -8 * k, 1, ["pc"], "pc")
        sel(eb("ETp", 1, k, 4), eb("ERc", 1, k, 4), [[0, 8], [pat, 16]], AL.is_ge, 0.0, base, 0, ["ERcb"], "ETpb")
    flat(T.ZT[:], 0, "ZT")

    def consts_gp():
        iota(T.nt[:], [[-int(KEY), C]], 0, 0, "nt", **f32)
        dmas("sy", [(T.PT[:, a:a + 448], T.ZT[:]) for a in range(0, 4 * C, 448)], "zp", ["ZT"], ["PTz"])
        sel(eb("EP1"), T.W1[:], [[0, 512]], AL.is_ge, 0.0, -16, 1, ["W1"], "EP1b")
        flat(T.TB[:, C:352], 0, "TBz")
        sel(eb("EP1"), eb("EP1"), [[0, 512]], AL.is_ge, 0.0, 31, -1, ["EP1b"], "EP1b")
        iota(T.J48[:, 0:16], [[0, 16]], int(BASE) + 335 - 2 ** 19 - 208, -1, "J48", **f32)
        iota(T.J48[:, 16:48], [[-112, 2], [0, 16]], int(BASE) + 335 - 2 ** 19, -1, "J48", **f32)
        for k, pat, base in ((0, -1, 1), (1, 1, -14)):
            sel(eb("EP1", 1, k, 4), eb("EP1", 1, k, 4), [[0, 8], [pat, 16]], AL.is_ge, 0.0, base, 0, ["EP1b"], "EP1b")
        iota(T.JR[:], [[-1, C]], int(BASE) + 335, 0, "JR", **f32)
        for ap, val, key in ((T.TT[:, C:352], 0, "TTz"), (T.TT[:, 688:TW], 0, "TTz"),
                             (T.SM[:, 1::SW], -337, "SMc"), (T.SM[:, 2::SW], 0, "SMc"),
                             (T.LS[:, 21:32], 0, "LS0")):
            flat(ap, val, key)
        iota(sm[:, 92:94], [[16, 2]], 0, 2, "p2", **f32)
        iota(sm[:, 94:96], [[16, 2]], 0, 0, "h2", **f32)
        iota(sm[:, 104:111], [[SW, 7]], 2, 0, "w7", **f32)

    def consts_ac(q):
        if q == 0:
            act(T.MN[:], T.k1[:], AF.Identity, ["k1"], ["MN"], bias=-3072.0)
            act(bc[:, 22:24], bc[:, 13:15], AF.Identity, ["pc"], ["pd"], bias=-2.0 ** 20)
            act(T.MN[:, 15::16], T.MN[:, 15::16], AF.Identity, ["MN"], ["MN"], bias=1536.0)
        if q == 1:
            act(T.M48[:], T.k1[:, 0:48], AF.Identity, ["k1"], ["M48"], bias=-3072.0 * 2048, scale=2048.0)
            act(bc[:, 16:18], T.de[:, 0:15:14], AF.Copy, ["de"], ["b8"], scale=KEY - 1, accum_out=bc[:, 8:9])
            act(bc[:, 18:20], T.de[:, 1:16:14], AF.Copy, ["de"], ["b9"], accum_out=bc[:, 9:10])
            act(bc[:, 26:27], bc[:, 13:14], AF.Sign, ["pc"], ["b26"])
            act(bc[:, 8:9], bc[:, 8:9], AF.Identity, ["b8", "b9"], ["b8"], bias=bc[:, 9:10])
            act(eb("EK"), T.ones[:], AF.Copy, ["ones", "b26"], ["EKb"], scale=bc[:, 26:27])
            act(eb("EX"), T.ones[:], AF.Copy, ["ones", "b8"], ["EXb"], scale=bc[:, 8:9])
            act(eb("EK", 1, 1, 4), T.ones[:, 0:128], AF.Copy, ["ones", "EKb"], ["EKb"], scale=0.0)

    def consts_ve(q):
        i = i16
        if q == 0:
            cp(CX, pI[:, 32:53], ["CXi"], ["CX"])
        e, m = sm[:, 88:90], [sm[:, 96 + 2 * s:98 + 2 * s] for s in range(3)]
        if q == 1:
            ts(e, sm[:, 94:96], bc[:, 3:4], None, AL.add, None, ["h2", "b3"], ["e"])
            ts(bc[:, 10:11], gr, 7.0, CELL[1] - 2.0, AL.is_lt, AL.mult, ["i"], ["b10"])
            ts(bc[:, 11:12], gr, 6.0, CELL[2] - 2.0, AL.is_lt, AL.mult, ["i"], ["b10"])
            ts(CP, sm[:, 92:94], i, None, AL.subtract, None, ["p2", "i"], ["CP"])
            for s, (val, w) in enumerate(((13.0, -2.0), (0.0, bc[:, 10:11]), (7.0, bc[:, 11:12]))):
                ts(m[s], e, val, w, AL.is_equal, AL.mult, ["e", "b10"], ["m%d" % s])
        if q == 2:
            tt(m[0], m[0], m[2], AL.add, ["m0", "m2"], ["m0"])
            tt(m[0], m[0], m[1], AL.add, ["m0", "m1"], ["m0"])
            for h in range(2):
                ts(CL[:, 32 + h:46:2], sm[:, 104:111], sm[:, 96 + h:97 + h], None, AL.add, None, ["w7", "m0"], ["CB"])

    def cells(c, a, e):
        return T.RT[:, slot[c] + 4 * a:slot[c] + 4 * e - 3:4]

    def held(bank, H, parts, steps=(0, 1, 2)):
        S = T[bank]
        for step in steps:
            for a, e, ks in parts:
                t1, hk = ["t1" + k for k in ks], [H + k for k in ks]
                if step == 0:
                    tt(T.t1[:, a:e], S[:, a:e], T.MH[:, a:e], AL.max, [bank, "MH"], t1)
                elif step == 1:
                    scan(T[H][:, a:e], T.RH[:, a:e], T.t1[:, a:e], INF, AL.max, AL.min, ["RH"] + t1, hk)
                else:
                    tt(cells("d", a, e), S[:, a:e], T[H][:, a:e], AL.is_gt, [bank] + hk + zs, ["RT.d"])

    def sums(c):
        scan(T.J[:, 112 * c + 112 - 8 * c:112 * c + 112], cells(c, 0, 8 * c), cells(c, 8 * c, 16 * c), 0.0,
             AL.add, AL.add, ["RT.%s" % c], ["J%d" % c])

    def block(bank, c):
        H = "H" + bank
        ts(cells(c, 0, 16 * c), T[bank][:, 0:16 * c], T[H][:, 16 * c + 15:16 * c + 16], None, AL.is_ge, None,
           [bank, H + "l", H + "a", H + "b"] + zs, ["RT.%s" % c])
        if c == LOW - 1:
            scan(T.DS[:], T.rm[:], cells("d", 0, C), 0.0, AL.mult, AL.add, ["rm", "RT.d"], ["DS"])
        elif c + 1 < LOW - AC_SUMS[bank]:
            sums(c + 1)

    def places(bank, twin, done, hook):
        S, H = T[bank], "H" + bank

        def diff(n):
            c = ON_ACT[n]
            act(pl("df", n % 3, 0, 16 * c), T[twin][:, 0:16 * c], AF.Identity, [twin, H + "h"],
                ["df%d" % (n % 3)], bias=T[H][:, 16 * c + 15:16 * c + 16], scale=-1.0)

        diff(0)
        for n, c in enumerate(ON_ACT):
            if n + 1 < len(ON_ACT):
                diff(n + 1)
            act(cells(c, 0, 16 * c), pl("df", n % 3, 0, 16 * c), AF.Sign, ["df%d" % (n % 3), "tiny"] + zs,
                ["RT.%s" % c, "AC"], bias=bc[:, 25:26], scale=-1.0, accum_out=sm[:, 100 + c:101 + c])

        def sums_ac():
            low = LOW - AC_SUMS[bank]
            for n, c in enumerate(range(LOW - 1, low - 1, -1)):
                act(pl("jk", n, 0, 16 * c), cells(c, 0, 16 * c), AF.Copy, ["RT.%s" % c], ["AC", "jk%d" % n], scale=2.0,
                    accum_out=sm[:, 100 + c:101 + c])
            act(T.J[:, 112 * low + 111::112], sm[:, 100 + low:121], AF.Copy, ["AC"],
                ["J%d" % c for c in range(low, 21)], scale=0.5)
            hook(-1)

        def count(q):
            blocks, w, st = TILES[q]
            quant("rq", start[q], start[q] + w, T.RT[:, 4 * start[q]:4 * (start[q] + w)],
                  ["RT.%s" % c for c in blocks] + ["RTz%d" % q])
            mm("pb2", w, st, 0, "rq", start[q], q == 0, q == 5, ["rq%d" % start[q]])

        last = [q for q in range(6) if 1 in TILES[q][0]][0]
        for c in ON_VE[done:]:
            block(bank, c)
            if c == LOW - 3:
                sums_ac()
            if c == 4:
                hook(1)
            for q in range(last):
                if c == TILES[q][0][-1] - 1:
                    count(q)
        count(last + 1)
        sums(1)
        hook(3)
        count(last)
        tt(X2, T.DS[:, 15::16], MC, AL.add, ["DS", "MC"], ["X2"])
        hook(0)
        for q in range(last + 2, 6):
            count(q)
        hook(4)
        tt(T.MNx[:, 15::16], T.J[:, 111::112], X2, AL.add, ["X2"] + ["J%d" % c for c in range(21)], ["MNx"])
        hook(2)
        scan(T.sx[:], T.pb2[:, 0:C], T.MNx[:], 4096.0, AL.min, AL.add, ["pb2", "MNx"], ["sx"])

    def to_list(src, key, o, okey):
        scan(T.sa[:], src, T.MN[:], 4096.0, AL.min, AL.add, [key, "MN"], ["sa"])
        ts(o, T.sa[:, 15::16], -512.0, None, AL.add, None, ["sa"], [okey])

    def piece(j, a, n, src, reads, key):
        hi, lo = T.PT[:, 4 * a:4 * (a + n):4], T.PT[:, 4 * a + 1:4 * (a + n):4]
        if j == 0:
            ts(hi, src, M32, -M32, AL.add, AL.add, reads + ["PTz"], [key + "h", "PT"])
        else:
            tt(lo, src, hi, AL.subtract, reads + [key + "h"], [key + "l", "PT"])

    def quant_pt(name, o, a, n, key):
        quant(name, o, o + n, T.PT[:, 4 * a:4 * (a + n)], [key + "h", key + "l"])
        rd.setdefault("PT", {})["ve"] = tick["ve"]

    for t in range(R):
        pc, ls, ll, NL = part(t), T["ls%d" % t], T["ll%d" % t], T.NL
        lk, lr, X = "ls%d" % t, "ll%d" % t, "x%d" % t
        def ahead(q):
            if q == 1:
                for pb in ("pb1", "pb6"):
                    mm(pb, C, "uu", 128, "rx%d" % t, 0, True, True, ["uuc", "uup", "rx%d" % t])
            if q in (3, 0, 4):
                held("pb1", "Hpb1", ((0, C, "hlab"),), [(3, 0, 4).index(q)])
            if q == 2:
                block("pb1", ON_VE[0])

        held("pb0", "Hpb0", ((16 * LOW, C, "h"), (HV[1][0] if t else 0, 16 * LOW, "l")))
        if t == 0:
            quantc("ERc")
        places("pb0", "pb7", 0, ahead)
        block("pb1", ON_VE[1])
        sx = T.sx[:, 15::16]
        ts(ls[:], sx, -float(UP), None, AL.add, None, ["sx"], [lk])
        send(pc, ll[:], ls[:], "la%d" % t, [lk])
        arrives([lr], "la%d" % t, ne(t))
        ts(T.L0s[:, 0:21], sx, -1.0, 335.0 + UP, AL.mult, AL.add, ["sx"], ["L0s"])
        dmas("sy", [(T.L0f[16 * k:16 * k + 16, :], T.L0s[0:16, :]) for k in range(8)], "l0", ["L0s", "L0z"], ["L0f"])
        if t == 0:
            consts_gp()
        dmas("sy", [(T.XT[:, a:a + 448], T.ZT[:]) for a in range(0, 8 * C, 448)], "zx", ["ZT"], ["XTz0", "XTz1"])
        if t == 0:
            for b in range(4):
                sel(eb("EU%d" % b), T.ones[:], [[1, 512]], AL.is_equal, 0.0, -b, -4, ["ones"], "EU%db" % b)
            for k in range(4):
                sel(eb("EL", 1, k, 4), T.de[:, 0:128], [[0, 128]], AL.is_ge, 0.0, 0, 0, ["de"], "ELb")

        IL = T.IL[:, 0:21]

        def unpack(b, e):
            pb = "pb%d" % (3, 4, 5, 7 if t else 3)[b]
            if e == "pe":
                mm(pb, C, "EU%d" % b, 0, "rx%d" % t, 0, True, True, ["rx%d" % t])
            elif e == "ve":
                cp(pl("F", b), T[pb][:, 0:C], [pb], ["F%d" % b])
            else:
                act(pl("F", b), T[pb][:, 0:C], AF.Copy, [pb], ["F%d" % b])

        def sort(b):
            act(pl("G", b), pl("F", b).indirect(IL), AF.Copy, ["F%d" % b, "IL"], ["G%d" % b])

        def inverse(q):
            if q == -1 and t == 0:
                consts_ac(0)
                consts_ac(1)
            if q == -1 and t:
                for e in ("pe", "ac"):
                    for b in range(4):
                        unpack(b, e)
            if q == 0:
                cp(T.oW[:].indirect(ll[:]), T.ji[:], [lr, "ji"], ["oW"])
                if t == 0:
                    consts_ve(0)
            if q == 2:
                scan(T.sa[:], T.oW[:], T.MN[:], 4096.0, AL.min, AL.add, ["oW", "MN"], ["sa"])
                cp(T.L0[:, 0:21], T.L0f[:, 0:21], ["L0f"], ["L0"])
                cp(T.L0[:, 32:48], T.L0f[:].indirect(CC), ["L0f", "CC"], ["L0"])

        places("pb1", "pb6", 2, inverse)
        ts(T.IL[:, 0:21], T.sa[:, 15::16], -512.0, None, AL.add, None, ["sa"], ["IL"])
        tt(T.Bx[:], T.sx[:].indirect(CX), T.de[:], AL.mult, ["sx", "CX", "de"], ["Bx"])
        tt(T.s48[:], T.nt[:].indirect(T.L0[:, 32:35]), T.J48[:], AL.add, ["nt", "L0", "J48"], ["s48"])
        if t == 0:
            quantc("ETp")
            quantc("EP1")
        else:
            for b in range(3):
                sort(b)
        for j in range(2):
            for h in range(2):
                (a, e), (x, y) = HV[h], LV[h]
                piece(j, a, e - a, T.Bx[:].indirect(T.IL[:, x:y]), ["Bx", "IL"], "PT%d" % h)
        for h in range(2):
            quant_pt("pp", HV[h][0], HV[h][0], HV[h][1] - HV[h][0], "PT%d" % h)
        pk = ["pp0", "pp160"]
        mm("pb3", C, "EP0", 0, "pp", 0, True, True, pk)
        mm("pb5", C, "ERc", 0, "pp", 0, True, True, pk)
        mm("pb4", C, "ETp", 0, "pp", 0, True, True, pk)
        mm("pb7", C, "EP1", 0, "pp", 0, True, True, pk)
        tt(T.y1[:], T.nt[:].indirect(T.L0[:, 0:21]), T.JR[:], AL.add, ["nt", "L0", "JR"], ["y1"])
        act(T.TT[:, 352:688], T.pb5[:, 0:C], AF.Identity, ["pb5"], ["TTf"], bias=-MID, scale=-1.0)
        act(T.TT[:, 0:C], T.pb4[:, 0:C], AF.Copy, ["pb4"], ["TTp"], scale=-1.0)
        act(T.TB[:, 0:C], T.pb7[:, 0:C], AF.Copy, ["pb7", "TBz"], ["TB0"], scale=-1.0)
        for k in range(1, 8):
            a = 352 if k == 1 else 0
            dmas("sy", [(T.TB[16 * j:16 * j + 16, TW * (k - 1) + a:TW * k], T.TT[16 * k:16 * k + 16, a:TW])
                        for j in range(8)], "tb%d" % k, ["TTf", "TTz"] + ["TTp"] * (k > 1), ["TB%d" % k])
        ts(T.P0[:], T.pb3[:, 0:C], -KEY, None, AL.mult, None, ["pb3"], ["P0"])
        ts(T.M48[:, 15::16], T.jp[:, 0:48:16], bc[:, 21:22], None, AL.add, None, ["jp", "b21", "M48"], ["M48"])
        if t == 0:
            quantc("EX")
        tt(T.G48[:], T.P0[:].indirect(T.L0[:, 32:35]), T.s48[:], AL.add, ["P0", "L0", "s48"], ["G48"])
        tt(T.K1[:], T.P0[:].indirect(T.L0[:, 0:21]), T.y1[:], AL.add, ["P0", "L0", "y1"], ["K1"])

        def own():
            scan(T.s48[:], T.G48[:], T.M48[:], 2.0 ** 23, AL.min, AL.add, ["G48", "M48"], ["s48"])

        def earlier(k):
            for pb in VB[(k + 1) % 2]:
                mm(pb, C, "EK", 0, "xk", 0, True, False, ["xk0"])
                if k > 4:
                    mm(pb, C, "EX", 0, "xx", 0, False, False, ["xx0"])

        own()
        if t == 0:
            quant("xe", 0, 208, T.XT[:, 0:832], ["XTz0"])
        for k in range(1, 8):
            w = SW * (k - 1)
            sk = "SM%d" % k
            va, vb = VB[k % 2]
            V, vk = (T.K1[:, 0:C], "K1") if k == 1 else (T[va][:, 0:C], va)
            if 1 < k < 7:
                earlier(k)
            if t == 0 and 1 < k < 6:
                unpack(k - 2, "pe")
            for s in (0, 2, 1)[:3 if k == 1 else 2]:
                c = w + CELL[s]
                act(pl("jk", s), V, AF.Sign, [vk, "s48"], [sk + ".%d" % s, "jk%d" % s], bias=T.s48[:, 16 * s + 15:16 * s + 16],
                    scale=-1.0, accum_out=T.SM[:, c:c + 1])
            if k == 1:
                ts(T.y1[:], V, bc[:, 14:15], bc[:, 23:24], AL.add, AL.subtract, ["K1", "pc", "pd"], ["y1"])
                ts(T.y2[:], V, bc[:, 13:14], bc[:, 22:23], AL.add, AL.subtract, ["K1", "pc", "pd"], ["y2"])
                ts(T.M48[:, 15::16], T.s48[:, 15::16], bc[:, 7:8], None, AL.add, None, ["s48", "b7"], ["M48"])
                scan(T.PT[:, 0::4], T.y1[:], T.y2[:], 0.0, AL.max, AL.subtract, ["y1", "y2"], ["XKh", "PT"])
            else:
                ts(T.CB[:], T[vb][:, 0:C], T.s48[:, 31:32], 2.0, AL.is_lt, AL.mult, [vb, "s48"], ["CBk"])
            if k < 7:
                ts(T.OF[:, 0:16], T.SM[:, w:w + 8].indirect(CWa), -0.5, 167.5, AL.mult, AL.add,
                   [sk + ".0", "SMc", "CW"], ["OFa"])
            else:
                quant_pt("lt", 0, 0, 160, "LT")
                mm("pb2", 160, "EL", 0, "lt", 0, True, True, ["lt0"])
            if k == 1:
                quant_pt("xk", 0, 0, C, "XK")
                earlier(k)
            else:
                scan(T.SM[:, w + 16:w + CELL[1] + 1], T.CB[:, 0:168], T.CB[:, 168:C], -335.0, AL.add, AL.add, ["CBk"],
                     [sk + ".1"])
            if k == 7:
                break
            o, tk = TW * (k - 1), ["TB%d" % (k if k > 1 else 0)]
            n, e = divmod(k - 1, 4)
            a, z = 4 * C * n, "XTz%d" % n
            win = T.TB[:, o:o + 352]
            act(T.XT[:, a + e + 832:a + 4 * C:4], win.indirect(T.OF[:, 0:8]), AF.Copy, ["OFa", z] + tk, ["XT0"])
            if k > 1:
                ts(T.M48[:, 15::16], T.s48[:, 15::16], bc[:, 7:8], None, AL.add, None, ["s48", "b7"], ["M48"])
            sr = [sk + ".%d" % s for s in range(3)] + ["SMc"]
            ts(T.OF[:, 16:48], T.SM[:, w:w + SW].indirect(CWb), -0.5, 167.5, AL.mult, AL.add, sr + ["CW"], ["OFb"])
            act(T.XT[:, a + e + 448:a + 832:4], win.indirect(T.OF[:, 24:30]), AF.Copy, ["OFb", z] + tk, ["XT2"])
            act(T.G48[:], T.TB[:, o + 352:o + TW].indirect(T.OF[:, 32:35]), AF.Identity, ["OFb", "TB%d" % k], ["G48"],
                bias=MID * KEY, scale=KEY)
            quant("xe", 208, C, T.XT[:, a + 832:a + 4 * C], ["XT0", z])
            for pb in VB[(k + 1) % 2]:
                mm(pb, C, "EX", 0, "xe", 0, False, False, ["xe0", "xe208"])
            cp(T.XT[:, a + e:a + 448:4], win.indirect(T.OF[:, 16:23]), ["OFb", z] + tk, ["XT1"])
            quant("xl", 0, 208, T.XT[:, a:a + 832], ["XT1", "XT2", z])
            for pb in VB[(k + 1) % 2]:
                mm(pb, 208, "EX", 0, "xl", 0, False, True, ["xl0"])
            own()
            if k == 4:
                ts(T.LS[:, 0:21], T.L0f[:, 0:21], -2.0, 335.0, AL.mult, AL.add, ["L0f"], ["LSa"])
                quant("xx", 0, C, T.XT[:, 0:4 * C], ["XT0", "XT1", "XT2", z])
            if t == 0 and k in (1, 2, 3):
                quantc("EU0") if k == 1 else consts_ve(k - 1)
            if t == 0 and 1 < k < 6:
                unpack(k - 2, "ac" if k < 4 else "ve")
            if t == 0 and k > 3 or t and k == 2:
                sort(k - 4 if t == 0 else 3)
            if k > 4:
                piece(k - 5, 0, 160, T.SM[:, 0:5 * SW].indirect(CB),
                      ["SM%d.%d" % (a, s) for a in range(1, 6) for s in range(3)] + ["CB"], "LT")
            if k == 6 and t == 0:
                quantc("EL")
        for j in range(2):
            piece(j, 160, 64, T.SM[:].indirect(CF), ["SM%d.%d" % (a, s) for a in (6, 7) for s in range(3)] + ["CB"],
                  "LF")
        act(T.LS[:, 32:192], T.pb2[:, 0:160], AF.Copy, ["pb2"], ["LSb"])
        if t == R - 1:
            act(T.Vs[:], T[VB[1][0]][:, 0:C], AF.Copy, [VB[1][0]], ["Vs"])
        if t == 0:
            sort(3)
        quant_pt("lf", 0, 160, 128, "LF")
        mm("pb3", 128, "EL", 0, "lf", 0, True, True, ["lf0"])
        cp(T.LS[:, 192:256], T.pb3[:, 0:64], ["pb3"], ["LSc"])
        ts(NL[:], T.LS[:].indirect(CP), -0.5, 167.5, AL.mult, AL.add, ["LS0", "LSa", "LSb", "LSc", "CP"], ["NL"])
        zk = ["NL"]

        def pick(h, b):
            (a, e), (x, y) = HV[h], LV[h]
            o, i = T.Z[:, 4 * a + b:4 * e:4], pl("G", b).indirect(NL[:, x:y])
            if b < 2 - h:
                cp(o, i, ["G%d" % b] + zk, ["Z%d.%d" % (h, b)])
            else:
                act(o, i, AF.Copy, ["G%d" % b] + zk, ["Z%d.%d" % (h, b)])

        def pack(h):
            a, e = HV[h]
            quant("z", a, e, T.Z[:, 4 * a:4 * e], ["Z%d.%d" % (h, b) for b in range(4)])

        def layer(h, b, j):
            a, e = HV[h]
            pb = "pb%d" % (2 * b + j)
            mm(pb, e - a, "wl", 128 * (b + 4 * j), "z", a, True, True, ["w0", "wsc", "z%d" % a])
            if j and (h, b) == (1, 0):
                cp(pl("yt", b, a, e), T[pb][:, 0:e - a], [pb], ["yt%d.%d" % (h, b)])
            elif j:
                act(pl("yt", b, a, e), T[pb][:, 0:e - a], AF.Copy, [pb], ["yt%d.%d" % (h, b)])

        def best(h, b):
            a, e = HV[h]
            tt(pl("Ym", b, a, e), T["pb%d" % (2 * b)][:, 0:e - a], pl("yt", b, a, e), AL.max,
               ["pb%d" % (2 * b), "yt%d.%d" % (h, b)], ["Y%d.%d" % (h, b)])

        for h, b in ((0, 0), (0, 2), (0, 1), (0, 3), (1, 0), (1, 2), (1, 3)):
            pick(h, b)
        pack(0)
        pick(1, 1)
        for b in range(4):
            for j in (1, 0):
                layer(0, b, j)
        cp(T.iW[:].indirect(NL[:, 0:21]), T.ji[:], ["ji"] + zk, ["iW"])
        pack(1)
        act(T.tm[:], T.iW[:].indirect(ll[:]), AF.Copy, ["iW", lr], ["tm"])
        for b in range(4):
            best(0, b)
        for b, j in ((0, 1), (1, 1), (0, 0), (2, 1), (1, 0), (3, 1), (2, 0), (3, 0)):
            layer(1, b, j)

        def back(h, b, e):
            (a, z), (x, y) = HV[h], LV[h]
            o, i = T.Yp[:, 4 * a + b:4 * z:4], pl("Ym", b).indirect(T.ML[:, x:y])
            rk = ["ML", "Y0.%d" % b, "Y1.%d" % b]
            if e == "ve":
                ts(o, i, 0.03125, None, AL.mult, None, rk, ["Yp%d.%d" % (h, b)])
            else:
                act(o, i, AF.Copy, rk, ["Yp%d.%d" % (h, b)], scale=0.03125)

        scan(T.sa[:], T.tm[:], T.MN[:], 4096.0, AL.min, AL.add, ["tm", "MN"], ["sa"])
        best(1, 0)
        ts(T.ML[:, 0:21], T.sa[:, 15::16], -512.0, None, AL.add, None, ["sa"], ["ML"])
        for b in range(1, 4):
            best(1, b)
        for h, b, e in ((0, 0, "ac"), (0, 1, "ac"), (0, 2, "ve"), (1, 0, "ac"), (0, 3, "ve"), (1, 1, "ac"),
                        (1, 2, "ve"), (1, 3, "ac")):
            back(h, b, e)
        for h in range(2):
            a, e = HV[h]
            quant("y%d" % t, a, e, T.Yp[:, 4 * a:4 * e], ["Yp%d.%d" % (h, b) for b in range(4)])
        for h in range(2):
            a, e = HV[h]
            k, sem = ["y%d%d" % (t, a)], ("ya%d", "yb%d")[h] % t
            send(pc, T["ry%dq" % t][:, a:e].bitcast(dt.uint8), T["y%dq" % t][:, a:e].bitcast(dt.uint8), sem, k)
            if h == 0:
                send(pc, T["ry%ds" % t][:], T["y%ds" % t][:], sem, k + ["y%d160" % t])
            arrives(["ry%d.%d" % (t, h)], sem, (2 - h) * ne(t))
        for h in range(2):
            a, e = HV[h]
            for b in range(4):
                mm("pb%d" % (4 * h + b), e - a, "EU%d" % b, 0, X, a, True, False, [X + "0", X + "160"])
        if t == R - 1:
            tt(T.tb[:], T.Vs[:], T.JR[:, 0:C], AL.subtract, ["Vs", "JR"], ["tb"])
            quant("v", 0, 128, T.vin[:], ["vin"])
            ts(T.tb[:], T.tb[:], 1.0 / KEY, M1, AL.mult, AL.add, ["tb"], ["tb"])
            ts(T.tb[:], T.tb[:], -M1, 335.0 + MID - 8 * UP, AL.add, AL.add, ["tb"], ["tb"])
            tt(T.Vs[:], T.TT[:, 352:TW].indirect(NL[:, 0:21]), T.tb[:], AL.add, ["tb", "TTf", "TTz", "NL"], ["Vs"])
            dmas("sy", [(T.tot[:], T.Vs[112:113, :])], "out", ["Vs"])
        N, xt = "x%d" % (t + 1), T["xt%d" % t]
        for h in range(2):
            a, e = HV[h]
            for b in range(4):
                pb = "pb%d" % (4 * h + b)
                mm(pb, e - a, "EU%d" % b, 0, "ry%d" % t, a, False, True, ["ry%d.%d" % (t, h)])
                o = xt[:, 4 * a + b:4 * e:4]
                if b % 2:
                    cp(o, T[pb][:, 0:e - a], [pb], ["xt%d.%d" % (h, b)])
                else:
                    act(o, T[pb][:, 0:e - a], AF.Copy, [pb], ["xt%d.%d" % (h, b)])
            quant(N, a, e, xt[:, 4 * a:4 * e], ["xt%d.%d" % (h, b) for b in range(4)])
            if t < R - 1:
                send(part(t + 1), T["r" + N + "q"][:, a:e].bitcast(dt.uint8), T[N + "q"][:, a:e].bitcast(dt.uint8),
                     "xa%d" % (t + 1), [N + str(a)])
        if t < R - 1:
            mm("pb1", HV[0][1], "uu", 0, N, 0, True, True, [N + "0"])
            for pb in ("pb0", "pb7"):
                mm(pb, C, "uu", 0, N, 0, True, True, [N + "0", N + "160"])
            send(part(t + 1), T["r" + N + "s"][:], T[N + "s"][:], "xa%d" % (t + 1), [N + "0", N + "160"])
            arrives(["r" + N], "xa%d" % (t + 1), 3 * ne(t + 1))
            held("pb1", "Hpb0", ((0, 80, "a"), (80, HV[0][1], "b")))
    for h in range(2):
        a, e = HV[h]
        pb, nk = "pb%d" % h, ["x2%d" % a]
        mm(pb, e - a, "v", 0, "x2", a, True, True, ["v0"] + nk)
        dmas("sy", [(T.oc[:, 4 * a:4 * e], T.x2q[:, a:e].bitcast(dt.uint8))], "out", nk)
        if h:
            cp(T.ysb[:, a:e], T[pb][:, 0:e - a], [pb], ["ysb%d" % h])
            dmas("ac", [(T.osc[4 * k:4 * k + 4, :], T.x2s[32 * k:32 * k + 4, :]) for k in range(4)], "out",
                 ["x20"] + nk)
        else:
            act(T.ysb[:, a:e], T[pb][:, 0:e - a], AF.Copy, [pb], ["ysb%d" % h])
        dmas("sy" if h else "ac", [(T.y[:, a:e], T.ysb[:, a:e])], "out", ["ysb%d" % h])
    for s in tick:
        g.wait_ge(T.sem[s], tick[s])
    for s in dcount:
        g.wait_ge(T.sem[s], dcount[s])
    for s in arr:
        g.wait_ge(T.sem[s], arr[s])
    g.wait_ge(T.sem.loc, sent[0])
